import numpy as np
import ml_dtypes


def mxq(x, axis, fmt="e4m3"):
    dtype, down = {"e4m3": (ml_dtypes.float8_e4m3fn, 7), "e5m2": (ml_dtypes.float8_e5m2, 14)}[fmt]
    v = np.moveaxis(np.asarray(x, np.float32).astype(ml_dtypes.bfloat16).astype(np.float64), axis, -1)
    blocks = v.reshape(v.shape[:-1] + (-1, 32))
    amax = np.abs(blocks).max(-1, keepdims=True)
    byte = np.maximum(np.where(amax > 0, np.frexp(amax)[1] - 1 + 127, 0) - down, 1)
    scale = np.exp2(byte - 127.0)
    codes = (blocks / scale).astype(np.float32).astype(dtype).astype(np.float64)
    return np.moveaxis((codes * scale).reshape(v.shape), -1, axis)


WIDE = False


def mx_kscale(k):
    if not WIDE:
        return np.ones(k)
    levels = np.array([10, -10, 5, -5, 0])
    if k % 512:
        return np.exp2(np.random.permutation(np.resize(levels, k // 32))).repeat(32)
    a = np.empty((k // 512, 16))
    for p in range(k // 512):
        a[p, :8] = np.random.permutation(np.resize(levels, 8))
        for g in range(8):
            far = levels[np.abs(levels - a[p, g]) >= 10]
            a[p, g + 8] = far[np.random.randint(len(far))]
    return np.exp2(a.ravel()).repeat(32)


def f64(x):
    return np.asarray(x).astype(np.float64)


def striped(idx):
    return np.tile(idx.reshape(-1, 16).T, (8, 1)).astype(np.uint16)


def unstriped(offs):
    return offs[:16].T.reshape(-1).astype(np.int64)


E2M1 = np.array([0.0, 0.5, 1.0, 1.5, 2.0, 3.0, 4.0, 6.0, -0.0, -0.5, -1.0, -1.5, -2.0, -3.0, -4.0, -6.0])


def pack_weight(w, fmt):
    k, n = w.shape
    w = f64(np.asarray(w, np.float32).astype(ml_dtypes.bfloat16)).reshape(k // 32, 32, n)
    amax = np.abs(w).max(1)
    if fmt == "e4m3":
        byte = np.frexp(amax)[1] - 1 + 127 - 7
    else:
        mant, ex = np.frexp(amax / 6.0)
        byte = np.where(mant > 0.5, ex, ex - 1) + 127
    byte = np.clip(np.where(amax > 0, byte, 1), 1, 254)
    scaled = (w * np.exp2(127.0 - byte)[:, None, :]).reshape(k, n).astype(np.float32)
    by_word = np.ascontiguousarray(scaled.reshape(k // 512, 128, 4, n).transpose(0, 1, 3, 2))
    if fmt == "e4m3":
        words = by_word.astype(ml_dtypes.float8_e4m3fn).view(np.uint8)
    else:
        c = by_word.astype(ml_dtypes.float4_e2m1fn).view(np.uint8) & 0xF
        words = (c[..., 0::2] | (c[..., 1::2] << 4)).reshape(k // 512, 128, 2 * n)
    return np.ascontiguousarray(words), np.ascontiguousarray(byte.astype(np.uint8).reshape(k // 512, 16, n))


def unpack_weight(words, scales, fmt):
    g, _, n = scales.shape
    words = np.ascontiguousarray(words).reshape(g, 128, n, -1)
    if fmt == "e4m3":
        vals = words.view(ml_dtypes.float8_e4m3fn).astype(np.float64)
    else:
        nib = np.empty((g, 128, n, 4), np.uint8)
        nib[..., 0::2] = words & 0xF
        nib[..., 1::2] = words >> 4
        vals = E2M1[nib]
    vals = vals * np.repeat(np.exp2(scales.astype(np.float64) - 127.0), 8, axis=1)[..., None]
    return vals.transpose(0, 1, 3, 2).reshape(g * 512, n)


def gelu(v):
    return 0.5 * v * (1.0 + np.tanh(np.sqrt(2.0 / np.pi) * (v + 0.044715 * v**3)))


K, T, S, H, N = 1024, 4096, 1024, 1024, 384

def setup_inputs():
    n = np.random.standard_normal
    s = mx_kscale(K)[:, None]
    u = mx_kscale(H)[:, None]
    tab_words, tab_scales = pack_weight(n((K, T)) * s, "e4m3")
    wq_words, wq_scales = pack_weight(n((K, H)) / np.sqrt(K) / s, "e2m1")
    return {
        "tab_words": tab_words, "tab_scales": tab_scales,
        "offs": striped(np.random.permutation(T)[:S]),
        "wi": (n((K, H)) / np.sqrt(K) / s).astype(np.float32),
        "wq_words": wq_words, "wq_scales": wq_scales,
        "gain": (np.exp(0.3 * n(H)) * u[:, 0]).astype(np.float32),
        "w2": (n((H, N)) / np.sqrt(H) / u).astype(np.float32),
    }

def reference(tab_words, tab_scales, offs, wi, wq_words, wq_scales, gain, w2):
    v = unpack_weight(tab_words, tab_scales, "e4m3")[:, unstriped(offs)]
    wiq = mxq(f64(wi), 0, "e4m3")
    wqq = unpack_weight(wq_words, wq_scales, "e2m1")
    a = wiq.T @ v
    b = wqq.T @ v
    h = f64(gain)[:, None] * np.log1p(a * a + b * b)
    hq = mxq(h, 0, "e4m3")
    w2q = mxq(f64(w2), 0, "e4m3")
    return w2q.T @ hq

@@ -1,0 +1,308 @@
+from contextlib import ExitStack
+
+import concourse.mybir as mybir
+
+K, T, S, H, N = 1024, 4096, 1024, 1024, 384
+FLOPS = 2 * (2 * K * H * S + H * N * S)
+
+F32 = mybir.dt.float32
+BF16 = mybir.dt.bfloat16
+I32 = mybir.dt.int32
+U32 = mybir.dt.uint32
+U16 = mybir.dt.uint16
+U8 = mybir.dt.uint8
+FP8X4 = mybir.dt.float8_e4m3fn_x4
+FP4X4 = mybir.dt.float4_e2m1fn_x4
+ACT = mybir.ActivationFunctionType
+ALU = mybir.AluOpType
+
+P = 128
+PACK = 4
+K_PASS = P * PACK
+PASSES = K // K_PASS
+GROUPS = H // K_PASS
+BANK = 512
+HALVES = S // BANK
+N_TILES = N // P
+RUN = 4
+UNIT_WIDTHS = (((256, 256), (256, 256)), ((256, 256), (256, 128, 128)))
+
+
+def tile_list_radar_log_power_kernel(tc, tab_words, tab_scales, offs, wi, wq_words, wq_scales, gain, w2, out):
+    nc = tc.nc
+    with ExitStack() as ctx:
+        keep = ctx.enter_context(tc.tile_pool(name="keep", bufs=1))
+        staging = ctx.enter_context(tc.tile_pool(name="staging", bufs=1))
+        ring = ctx.enter_context(tc.tile_pool(name="ring", bufs=3))
+        psum = ctx.enter_context(tc.psum_pool(name="psum", bufs=8))
+
+        offsets = keep.tile([P, S // 16], U16, name="offsets")
+        nc.sync.dma_start(offsets[:], offs)
+
+        piece = PACK * K_PASS
+        w2_at = GROUPS * PASSES * piece
+        gain_at = w2_at + GROUPS * PACK * N
+        raw_columns = gain_at + GROUPS * PACK
+        raw_end = -(-4 * raw_columns // 64) * 64
+        scale_window = staging.tile([P, T // 4], I32, name="scale_window", offset=raw_end - 64, align_bytes=64)
+        nc.vector.memset(scale_window[:], 0)
+        nc.scalar.dma_start(scale_window[0:P:4, :], tab_scales.rearrange("a q t -> (a q) t").bitcast(I32))
+        one = keep.tile([P, 1], F32, name="one")
+        nc.vector.memset(one[:], 1.0)
+        v_planes = keep.tile([P, PASSES * S // 4], I32, name="v_planes", align_bytes=64)
+        nc.vector.memset(v_planes[:], 0)
+        zero = keep.tile([P, 1], F32, name="zero")
+        nc.scalar.activation(zero[:], one[:], ACT.Ln)
+
+        wq_scales_raw = keep.tile([P, PASSES, H // 4], I32, name="wq_scales_raw", tag="wq_a", align_bytes=64)
+        nc.gpsimd.memset(wq_scales_raw[:], 0)
+        for quad in range(4):
+            nc.gpsimd.dma_start(
+                wq_scales_raw[32 * quad : 32 * quad + 4, :, :],
+                wq_scales[:, 4 * quad : 4 * quad + 4, :].rearrange("a r c -> r a c").bitcast(I32),
+            )
+        wq_raw = keep.tile([P, PASSES, H // 2], I32, name="wq_raw", tag="wq_b", align_bytes=64)
+        nc.sync.dma_start(wq_raw[:], wq_words.rearrange("a p c -> p a c").bitcast(I32))
+
+        table0 = keep.tile([P, T], I32, name="table0", align_bytes=64)
+        nc.sync.dma_start(table0[:], tab_words[0].rearrange("p t i -> p (t i)").bitcast(I32))
+
+        picked_scales = keep.tile([P, S // 4], I32, name="picked_scales", align_bytes=64)
+        nc.vector.tensor_copy(picked_scales[:].bitcast(U8), scale_window[:].bitcast(U8).indirect(offsets[:]))
+
+        def place_scales(a):
+            for quad in range(4):
+                first = 64 * a + 16 * quad
+                nc.sync.dma_start(
+                    v_planes[32 * quad : 32 * quad + 4, a * S // 4 : (a + 1) * S // 4],
+                    picked_scales[first : first + 16 : 4, :],
+                )
+
+        place_scales(0)
+        table1 = staging.tile([P, T], I32, name="table1", offset=raw_end + PASSES * H, align_bytes=64)
+        nc.sync.dma_start(table1[:], tab_words[1].rearrange("p t i -> p (t i)").bitcast(I32))
+        place_scales(1)
+        table = [table0, table1]
+        v_scales = v_planes[:].bitcast(U8)
+
+        raw = staging.tile([P, raw_columns], F32, name="raw", offset=0, align_bytes=64)
+        wi_raw = {}
+        for g in range(GROUPS):
+            for a in range(PASSES):
+                at = (g * PASSES + a) * piece
+                wi_raw[g, a] = raw[:, at : at + piece].rearrange("p (j c) -> p j c", j=PACK)
+                rows = wi[a * K_PASS : (a + 1) * K_PASS, g * K_PASS : (g + 1) * K_PASS]
+                nc.sync.dma_start(wi_raw[g, a], rows.rearrange("(p j) c -> p j c", j=PACK))
+        gains = raw[:, gain_at:].rearrange("p (g t) -> p g t", g=GROUPS)
+        nc.sync.dma_start(gains, gain.rearrange("(g p t) -> p g t", p=P, t=PACK))
+        w2_raw = []
+        for g in range(GROUPS):
+            at = w2_at + g * PACK * N
+            w2_raw.append(raw[:, at : at + PACK * N])
+            nc.sync.dma_start(w2_raw[g], w2[g * K_PASS : (g + 1) * K_PASS, :].rearrange("(p j) n -> p (j n)", j=PACK))
+
+        wq_planes = staging.tile([P, PASSES * H // 4], I32, name="wq_planes", offset=raw_end, align_bytes=64)
+        nc.vector.tensor_copy(
+            wq_planes[:].bitcast(U8).rearrange("p (b t m) -> p b m t", t=PACK, m=P),
+            wq_scales_raw[:].rearrange("p a c -> p (a c)").bitcast(U8).rearrange("p (b m t) -> p b m t", t=PACK, m=P),
+        )
+        wq_codes = keep.tile([P, PASSES * H // 2], I32, name="wq_codes", tag="wq_a", align_bytes=64)
+        nc.vector.tensor_copy(
+            wq_codes[:].bitcast(U16).rearrange("p (b t m) -> p b t m", t=PACK, m=P),
+            wq_raw[:].rearrange("p a c -> p (a c)").bitcast(U16).rearrange("p (b m t) -> p b t m", t=PACK, m=P),
+        )
+        wq_bytes = wq_codes[:].bitcast(U8)
+        wq_scale_bytes = wq_planes[:].bitcast(U8)
+
+        v_codes = [
+            keep.tile([P, S], U32, name="v_codes0", tag="wq_b", align_bytes=64),
+            keep.tile([P, S], U32, name="v_codes1", align_bytes=64),
+        ]
+        nc.vector.tensor_copy(v_codes[0][:], table[0][:].bitcast(U32).indirect(offsets[:]))
+        for half in range(HALVES):
+            nc.vector.tensor_copy(
+                v_codes[1][:, half * BANK : (half + 1) * BANK],
+                table[1][:].bitcast(U32).indirect(offsets[:, half * BANK // 16 : (half + 1) * BANK // 16]),
+            )
+
+        power = {}
+        units = {}
+        for g in range(GROUPS):
+            units[g] = []
+            for half in range(HALVES):
+                tile = keep.tile([P, PACK * BANK], F32, name=f"power{g}_{half}")
+                at = 0
+                for width in UNIT_WIDTHS[g][half]:
+                    units[g].append((half * BANK + at, width))
+                    power[g, half * BANK + at] = tile[:, PACK * at : PACK * (at + width)]
+                    at += width
+                power[g, "half", half] = tile
+
+        def quadrature_pass(bank, g, half, t, a):
+            col = (a * GROUPS + g) * K_PASS + t * P
+            nc.tensor.matmul_mx(
+                out=bank[:],
+                lhsT=wq_bytes[:, 2 * col : 2 * (col + P)].bitcast(FP4X4),
+                lhsT_scale=wq_scale_bytes[:, col : col + P],
+                rhs=v_codes[a][:, half * BANK : (half + 1) * BANK].bitcast(FP8X4),
+                rhs_scale=v_scales[:, a * S + half * BANK : a * S + (half + 1) * BANK],
+                start=(a == 0),
+                stop=(a == PASSES - 1),
+            )
+
+        def quadrature_square(bank, g, half, t):
+            tile = power[g, "half", half]
+            widths = UNIT_WIDTHS[g][half]
+            at = 0
+            for width in sorted(set(widths), reverse=True):
+                span = width * widths.count(width)
+                nc.scalar.activation(
+                    tile[:, PACK * at : PACK * (at + span)].rearrange("p (u t j) -> p u t j", t=PACK, j=width)[:, :, t, :],
+                    bank[:, at : at + span].rearrange("p (u j) -> p u j", j=width),
+                    ACT.Square,
+                    bias=zero[:],
+                )
+                at += span
+
+        def quadrature(g, first_pass_ahead):
+            slots = [(half, t) for half in range(HALVES) for t in range(PACK)]
+            banks = {}
+            if first_pass_ahead:
+                for half, t in slots:
+                    banks[half, t] = psum.tile([P, BANK], F32, name="bank")
+                    quadrature_pass(banks[half, t], g, half, t, 0)
+            for half, t in slots:
+                if not first_pass_ahead:
+                    banks[half, t] = psum.tile([P, BANK], F32, name="bank")
+                    quadrature_pass(banks[half, t], g, half, t, 0)
+                quadrature_pass(banks[half, t], g, half, t, 1)
+                quadrature_square(banks[half, t], g, half, t)
+
+        wi_codes = {}
+        wi_scales = {}
+
+        def prepare_wi(g, a):
+            grouped = ring.tile([P, piece], BF16, name="grouped", align_bytes=64)
+            nc.vector.tensor_copy(
+                grouped[:].rearrange("p (t m j) -> p m j t", t=PACK, j=PACK),
+                wi_raw[g, a].rearrange("p j (m t) -> p m j t", t=PACK),
+            )
+            wi_codes[g, a] = keep.tile([P, K_PASS], U32, name=f"wi_codes{g}_{a}", align_bytes=64)
+            wi_scales[g, a] = keep.tile([P, K_PASS], U8, name=f"wi_scales{g}_{a}", align_bytes=64)
+            nc.vector.quantize_mx(out=wi_codes[g, a][:].bitcast(FP8X4), scales=wi_scales[g, a][:], in_=grouped[:])
+
+        def log_power(g, start, width):
+            squares = ring.tile([P, PACK * width], F32, name="squares")
+            per_bank = BANK // width
+            for first in range(0, PACK, per_bank):
+                bank = psum.tile([P, BANK], F32, name="bank")
+                for t in range(first, first + per_bank):
+                    for a in range(PASSES):
+                        nc.tensor.matmul_mx(
+                            out=bank[:, (t - first) * width : (t - first + 1) * width],
+                            lhsT=wi_codes[g, a][:, t * P : (t + 1) * P].bitcast(FP8X4),
+                            lhsT_scale=wi_scales[g, a][:, t * P : (t + 1) * P],
+                            rhs=v_codes[a][:, start : start + width].bitcast(FP8X4),
+                            rhs_scale=v_scales[:, a * S + start : a * S + start + width],
+                            start=(a == 0),
+                            stop=(a == PASSES - 1),
+                        )
+                nc.scalar.activation(squares[:, first * width : first * width + BANK], bank[:], ACT.Square, bias=zero[:])
+            nc.vector.tensor_tensor(power[g, start], squares[:], power[g, start], ALU.add)
+            nc.scalar.activation(power[g, start], power[g, start], ACT.Ln, bias=one[:])
+
+        h_codes = [keep.tile([P, S], U32, name=f"h_codes{g}", align_bytes=64) for g in range(GROUPS)]
+        h_scales = [keep.tile([P, S], U8, name=f"h_scales{g}", align_bytes=64) for g in range(GROUPS)]
+        h_rounded = {}
+
+        def apply_gain(g, start, width):
+            h = ring.tile([P, PACK * width], BF16, name="h", align_bytes=64)
+            nc.vector.tensor_tensor(
+                h[:].rearrange("p (c i t) -> p c t i", i=RUN, t=PACK),
+                power[g, start].rearrange("p (t c i) -> p c t i", t=PACK, i=RUN),
+                gains[:, g, :].unsqueeze(1).unsqueeze(3).to_broadcast([P, width // RUN, PACK, RUN]),
+                ALU.mult,
+            )
+            h_rounded[g, start] = h
+
+        def quantize_h(g, start, width):
+            nc.vector.quantize_mx(
+                out=h_codes[g][:, start : start + width].bitcast(FP8X4),
+                scales=h_scales[g][:, start : start + width],
+                in_=h_rounded[g, start][:],
+            )
+
+        w2_grouped = keep.tile([P, GROUPS * PACK * N], BF16, name="w2_grouped", align_bytes=64)
+        w2_codes = keep.tile([P, GROUPS * N], U32, name="w2_codes", align_bytes=64)
+        w2_scales = keep.tile([P, GROUPS * N], U8, name="w2_scales", align_bytes=64)
+
+        def round_w2(g):
+            nc.vector.tensor_copy(
+                w2_grouped[:, g * PACK * N : (g + 1) * PACK * N].rearrange("p (c i j) -> p c j i", i=RUN, j=PACK),
+                w2_raw[g].rearrange("p (j c i) -> p c j i", j=PACK, i=RUN),
+            )
+
+        def quantize_w2(first, count):
+            nc.vector.quantize_mx(
+                out=w2_codes[:, first : first + count].bitcast(FP8X4),
+                scales=w2_scales[:, first : first + count],
+                in_=w2_grouped[:, PACK * first : PACK * (first + count)],
+            )
+
+        out_rows = out.rearrange("(c p) j -> p c j", p=P)
+
+        def features(start, width):
+            result = ring.tile([P, N_TILES, width], F32, name="result")
+            per_bank = BANK // width
+            for first in range(0, N_TILES, per_bank):
+                last = min(first + per_bank, N_TILES)
+                bank = psum.tile([P, BANK], F32, name="bank")
+                for c in range(first, last):
+                    for g in range(GROUPS):
+                        col = g * N + c * P
+                        nc.tensor.matmul_mx(
+                            out=bank[:, (c - first) * width : (c - first + 1) * width],
+                            lhsT=w2_codes[:, col : col + P].bitcast(FP8X4),
+                            lhsT_scale=w2_scales[:, col : col + P],
+                            rhs=h_codes[g][:, start : start + width].bitcast(FP8X4),
+                            rhs_scale=h_scales[g][:, start : start + width],
+                            start=(g == 0),
+                            stop=(g == GROUPS - 1),
+                        )
+                nc.scalar.copy(
+                    result[:, first:last, :].rearrange("p c j -> p (c j)"), bank[:, : (last - first) * width]
+                )
+            nc.sync.dma_start(out_rows[:, :, start : start + width], result[:])
+
+        quadrature(0, True)
+        prepare_wi(0, 0)
+        prepare_wi(0, 1)
+        log_power(0, *units[0][0])
+        log_power(0, *units[0][1])
+        prepare_wi(1, 0)
+        log_power(0, *units[0][2])
+        prepare_wi(1, 1)
+        log_power(0, *units[0][3])
+        quadrature(1, False)
+        log_power(1, *units[1][0])
+        apply_gain(0, *units[0][0])
+        round_w2(0)
+        quantize_h(0, *units[0][0])
+        round_w2(1)
+        apply_gain(0, *units[0][1])
+        quantize_w2(0, 512)
+        quantize_w2(512, 256)
+        quantize_h(0, *units[0][1])
+        later = list(units[0][2:])
+        count = len(units[1])
+        for u in range(count):
+            if u + 1 < count:
+                log_power(1, *units[1][u + 1])
+            apply_gain(1, *units[1][u])
+            extra = later.pop(0) if later else None
+            if extra:
+                apply_gain(0, *extra)
+            quantize_h(1, *units[1][u])
+            if extra:
+                quantize_h(0, *extra)
+            features(*units[1][u])

@@ -25,6 +25,8 @@ BANK = 512
 HALVES = S // BANK
 N_TILES = N // P
 RUN = 4
+SPAN = PACK * RUN
+SPANS = K_PASS // SPAN
 UNIT_WIDTHS = (((256, 256), (256, 256)), ((256, 256), (256, 128, 128)))
 
 
@@ -41,27 +43,32 @@ def tile_list_radar_log_power_kernel(tc, tab_words, tab_scales, offs, wi, wq_wor
 
         piece = PACK * K_PASS
         w2_at = GROUPS * PASSES * piece
-        gain_at = w2_at + GROUPS * PACK * N
-        raw_columns = gain_at + GROUPS * PACK
-        raw_end = -(-4 * raw_columns // 64) * 64
-        scale_window = staging.tile([P, T // 4], I32, name="scale_window", offset=raw_end - 64, align_bytes=64)
+        raw_columns = w2_at + GROUPS * PACK * N
+        raw_end = 4 * raw_columns
+        table1_at = raw_end + 4 * S
+        table1_end = table1_at + 4 * T
+
+        scale_window = staging.tile([P, T // 4], I32, name="scale_window", offset=table1_end - 64, align_bytes=64)
         nc.vector.memset(scale_window[:], 0)
         nc.scalar.dma_start(scale_window[0:P:4, :], tab_scales.rearrange("a q t -> (a q) t").bitcast(I32))
+        wq_scales_raw = keep.tile([P, PASSES, H // 4], I32, name="wq_scales_raw", align_bytes=64)
+        nc.vector.memset(wq_scales_raw[:], 0)
         one = keep.tile([P, 1], F32, name="one")
         nc.vector.memset(one[:], 1.0)
         v_planes = keep.tile([P, PASSES * S // 4], I32, name="v_planes", align_bytes=64)
         nc.vector.memset(v_planes[:], 0)
+        gain_rows = keep.tile([P, P], F32, name="gain_rows")
+        nc.vector.memset(gain_rows[:], 0.0)
         zero = keep.tile([P, 1], F32, name="zero")
         nc.scalar.activation(zero[:], one[:], ACT.Ln)
 
-        wq_scales_raw = keep.tile([P, PASSES, H // 4], I32, name="wq_scales_raw", tag="wq_a", align_bytes=64)
-        nc.gpsimd.memset(wq_scales_raw[:], 0)
         for quad in range(4):
             nc.gpsimd.dma_start(
                 wq_scales_raw[32 * quad : 32 * quad + 4, :, :],
                 wq_scales[:, 4 * quad : 4 * quad + 4, :].rearrange("a r c -> r a c").bitcast(I32),
             )
-        wq_raw = keep.tile([P, PASSES, H // 2], I32, name="wq_raw", tag="wq_b", align_bytes=64)
+        nc.gpsimd.dma_start(gain_rows[0:P:16, :], gain.rearrange("(g b c) -> b g c", g=GROUPS, c=P))
+        wq_raw = staging.tile([P, PASSES, H // 2], I32, name="wq_raw", offset=raw_end - 64, align_bytes=64)
         nc.sync.dma_start(wq_raw[:], wq_words.rearrange("a p c -> p a c").bitcast(I32))
 
         table0 = keep.tile([P, T], I32, name="table0", align_bytes=64)
@@ -79,11 +86,18 @@ def tile_list_radar_log_power_kernel(tc, tab_words, tab_scales, offs, wi, wq_wor
                 )
 
         place_scales(0)
-        table1 = staging.tile([P, T], I32, name="table1", offset=raw_end + PASSES * H, align_bytes=64)
+        table1 = staging.tile([P, T], I32, name="table1", offset=table1_at, align_bytes=64)
         nc.sync.dma_start(table1[:], tab_words[1].rearrange("p t i -> p (t i)").bitcast(I32))
         place_scales(1)
-        table = [table0, table1]
         v_scales = v_planes[:].bitcast(U8)
+
+        wq_codes = staging.tile(
+            [P, PASSES * H // 2], I32, name="wq_codes", offset=table1_end + PASSES * H, align_bytes=64
+        )
+        nc.vector.tensor_copy(
+            wq_codes[:].rearrange("p (b t s w) -> p b t s w", t=PACK, s=SPANS, w=2),
+            wq_raw[:].rearrange("p a (g s t w) -> p (a g) t s w", t=PACK, s=SPANS, w=2),
+        )
 
         raw = staging.tile([P, raw_columns], F32, name="raw", offset=0, align_bytes=64)
         wi_raw = {}
@@ -93,37 +107,40 @@ def tile_list_radar_log_power_kernel(tc, tab_words, tab_scales, offs, wi, wq_wor
                 wi_raw[g, a] = raw[:, at : at + piece].rearrange("p (j c) -> p j c", j=PACK)
                 rows = wi[a * K_PASS : (a + 1) * K_PASS, g * K_PASS : (g + 1) * K_PASS]
                 nc.sync.dma_start(wi_raw[g, a], rows.rearrange("(p j) c -> p j c", j=PACK))
-        gains = raw[:, gain_at:].rearrange("p (g t) -> p g t", g=GROUPS)
-        nc.sync.dma_start(gains, gain.rearrange("(g p t) -> p g t", p=P, t=PACK))
         w2_raw = []
         for g in range(GROUPS):
             at = w2_at + g * PACK * N
             w2_raw.append(raw[:, at : at + PACK * N])
-            nc.sync.dma_start(w2_raw[g], w2[g * K_PASS : (g + 1) * K_PASS, :].rearrange("(p j) n -> p (j n)", j=PACK))
-
-        wq_planes = staging.tile([P, PASSES * H // 4], I32, name="wq_planes", offset=raw_end, align_bytes=64)
-        nc.vector.tensor_copy(
-            wq_planes[:].bitcast(U8).rearrange("p (b t m) -> p b m t", t=PACK, m=P),
-            wq_scales_raw[:].rearrange("p a c -> p (a c)").bitcast(U8).rearrange("p (b m t) -> p b m t", t=PACK, m=P),
-        )
-        wq_codes = keep.tile([P, PASSES * H // 2], I32, name="wq_codes", tag="wq_a", align_bytes=64)
-        nc.vector.tensor_copy(
-            wq_codes[:].bitcast(U16).rearrange("p (b t m) -> p b t m", t=PACK, m=P),
-            wq_raw[:].rearrange("p a c -> p (a c)").bitcast(U16).rearrange("p (b m t) -> p b t m", t=PACK, m=P),
-        )
-        wq_bytes = wq_codes[:].bitcast(U8)
-        wq_scale_bytes = wq_planes[:].bitcast(U8)
+            rows = w2[g * K_PASS : (g + 1) * K_PASS, :].rearrange("(s t i) n -> t s i n", t=PACK, i=RUN)
+            for t in range(PACK):
+                nc.sync.dma_start(w2_raw[g][:, t * N : (t + 1) * N], rows[t])
 
         v_codes = [
-            keep.tile([P, S], U32, name="v_codes0", tag="wq_b", align_bytes=64),
+            staging.tile([P, S], U32, name="v_codes0", offset=raw_end, align_bytes=64),
             keep.tile([P, S], U32, name="v_codes1", align_bytes=64),
         ]
-        nc.vector.tensor_copy(v_codes[0][:], table[0][:].bitcast(U32).indirect(offsets[:]))
+        nc.vector.tensor_copy(v_codes[0][:], table0[:].bitcast(U32).indirect(offsets[:]))
+        wq_planes = staging.tile([P, PASSES * H // 4], I32, name="wq_planes", offset=table1_end, align_bytes=64)
+        nc.vector.tensor_copy(
+            wq_planes[:].rearrange("p (b t s) -> p b t s", t=PACK, s=SPANS),
+            wq_scales_raw[:].rearrange("p a (g s t) -> p (a g) t s", t=PACK, s=SPANS),
+        )
+        gain_sorted = keep.tile([P, P], F32, name="gain_sorted", align_bytes=64)
+        nc.vector.tensor_copy(
+            gain_sorted[:].rearrange("p (t s i) -> p t s i", t=PACK, i=RUN),
+            gain_rows[:].rearrange("p (s t i) -> p t s i", t=PACK, i=RUN),
+        )
+        gain_turned = keep.tile([P, P], F32, name="gain_turned", align_bytes=64)
+        nc.vector.transpose(gain_turned[:], gain_sorted[:])
+        gains = keep.tile([P, GROUPS, PACK], F32, name="gains")
+        nc.vector.tensor_copy(gains[:], gain_turned[:].rearrange("p (t g x) -> p g t x", t=PACK, g=GROUPS)[:, :, :, 0])
         for half in range(HALVES):
             nc.vector.tensor_copy(
                 v_codes[1][:, half * BANK : (half + 1) * BANK],
-                table[1][:].bitcast(U32).indirect(offsets[:, half * BANK // 16 : (half + 1) * BANK // 16]),
+                table1[:].bitcast(U32).indirect(offsets[:, half * BANK // 16 : (half + 1) * BANK // 16]),
             )
+        wq_bytes = wq_codes[:].bitcast(U8)
+        wq_scale_bytes = wq_planes[:].bitcast(U8)
 
         power = {}
         units = {}
@@ -184,8 +201,8 @@ def tile_list_radar_log_power_kernel(tc, tab_words, tab_scales, offs, wi, wq_wor
         def prepare_wi(g, a):
             grouped = ring.tile([P, piece], BF16, name="grouped", align_bytes=64)
             nc.vector.tensor_copy(
-                grouped[:].rearrange("p (t m j) -> p m j t", t=PACK, j=PACK),
-                wi_raw[g, a].rearrange("p j (m t) -> p m j t", t=PACK),
+                grouped[:].rearrange("p (t s i j) -> p t s j i", t=PACK, i=RUN, j=PACK),
+                wi_raw[g, a].rearrange("p j (s t i) -> p t s j i", t=PACK, i=RUN),
             )
             wi_codes[g, a] = keep.tile([P, K_PASS], U32, name=f"wi_codes{g}_{a}", align_bytes=64)
             wi_scales[g, a] = keep.tile([P, K_PASS], U8, name=f"wi_scales{g}_{a}", align_bytes=64)
@@ -236,8 +253,8 @@ def tile_list_radar_log_power_kernel(tc, tab_words, tab_scales, offs, wi, wq_wor
         w2_codes = keep.tile([P, GROUPS * N], U32, name="w2_codes", align_bytes=64)
         w2_scales = keep.tile([P, GROUPS * N], U8, name="w2_scales", align_bytes=64)
 
-        def round_w2(g):
-            nc.vector.tensor_copy(
+        def round_w2(g, copy):
+            copy(
                 w2_grouped[:, g * PACK * N : (g + 1) * PACK * N].rearrange("p (c i j) -> p c j i", i=RUN, j=PACK),
                 w2_raw[g].rearrange("p (j c i) -> p c j i", j=PACK, i=RUN),
             )
@@ -286,9 +303,9 @@ def tile_list_radar_log_power_kernel(tc, tab_words, tab_scales, offs, wi, wq_wor
         quadrature(1, False)
         log_power(1, *units[1][0])
         apply_gain(0, *units[0][0])
-        round_w2(0)
+        round_w2(0, nc.vector.tensor_copy)
         quantize_h(0, *units[0][0])
-        round_w2(1)
+        round_w2(1, nc.scalar.copy)
         apply_gain(0, *units[0][1])
         quantize_w2(0, 512)
         quantize_w2(512, 256)

@@ -1,6 +1,7 @@
 from contextlib import ExitStack
 
 import concourse.mybir as mybir
+from concourse.masks import make_identity
 
 K, T, S, H, N = 1024, 4096, 1024, 1024, 384
 FLOPS = 2 * (2 * K * H * S + H * N * S)
@@ -27,7 +28,7 @@ N_TILES = N // P
 RUN = 4
 SPAN = PACK * RUN
 SPANS = K_PASS // SPAN
-UNIT_WIDTHS = (((256, 256), (256, 256)), ((256, 256), (256, 128, 128)))
+UNIT_WIDTHS = (((256, 256), (256, 128, 128)), ((256, 256), (256, 128, 128)))
 
 
 def tile_list_radar_log_power_kernel(tc, tab_words, tab_scales, offs, wi, wq_words, wq_scales, gain, w2, out):
@@ -50,28 +51,31 @@ def tile_list_radar_log_power_kernel(tc, tab_words, tab_scales, offs, wi, wq_wor
 
         scale_window = staging.tile([P, T // 4], I32, name="scale_window", offset=table1_end - 64, align_bytes=64)
         nc.vector.memset(scale_window[:], 0)
-        nc.scalar.dma_start(scale_window[0:P:4, :], tab_scales.rearrange("a q t -> (a q) t").bitcast(I32))
+        nc.sync.dma_start(scale_window[0:P:4, :], tab_scales.rearrange("a q t -> (a q) t").bitcast(I32))
         wq_scales_raw = keep.tile([P, PASSES, H // 4], I32, name="wq_scales_raw", align_bytes=64)
         nc.vector.memset(wq_scales_raw[:], 0)
-        one = keep.tile([P, 1], F32, name="one")
+        gain_rows = keep.tile([P, P], F32, name="gain_rows")
+        nc.vector.memset(gain_rows[:], 0.0)
+        one = keep.tile([P, 1], F32, name="one", tag="table0", align_bytes=64)
         nc.vector.memset(one[:], 1.0)
         v_planes = keep.tile([P, PASSES * S // 4], I32, name="v_planes", align_bytes=64)
         nc.vector.memset(v_planes[:], 0)
-        gain_rows = keep.tile([P, P], F32, name="gain_rows")
-        nc.vector.memset(gain_rows[:], 0.0)
         zero = keep.tile([P, 1], F32, name="zero")
         nc.scalar.activation(zero[:], one[:], ACT.Ln)
 
+        identity = keep.tile([P, P], F32, name="identity")
+        make_identity(nc, identity[:])
+
         for quad in range(4):
-            nc.gpsimd.dma_start(
+            nc.sync.dma_start(
                 wq_scales_raw[32 * quad : 32 * quad + 4, :, :],
                 wq_scales[:, 4 * quad : 4 * quad + 4, :].rearrange("a r c -> r a c").bitcast(I32),
             )
-        nc.gpsimd.dma_start(gain_rows[0:P:16, :], gain.rearrange("(g b c) -> b g c", g=GROUPS, c=P))
+        nc.sync.dma_start(gain_rows[0:P:16, :], gain.rearrange("(g b c) -> b g c", g=GROUPS, c=P))
         wq_raw = staging.tile([P, PASSES, H // 2], I32, name="wq_raw", offset=raw_end - 64, align_bytes=64)
         nc.sync.dma_start(wq_raw[:], wq_words.rearrange("a p c -> p a c").bitcast(I32))
 
-        table0 = keep.tile([P, T], I32, name="table0", align_bytes=64)
+        table0 = keep.tile([P, T], I32, name="table0", tag="table0", align_bytes=64)
         nc.sync.dma_start(table0[:], tab_words[0].rearrange("p t i -> p (t i)").bitcast(I32))
 
         picked_scales = keep.tile([P, S // 4], I32, name="picked_scales", align_bytes=64)
@@ -91,6 +95,20 @@ def tile_list_radar_log_power_kernel(tc, tab_words, tab_scales, offs, wi, wq_wor
         place_scales(1)
         v_scales = v_planes[:].bitcast(U8)
 
+        wq_planes = staging.tile([P, PASSES * H // 4], I32, name="wq_planes", offset=table1_end, align_bytes=64)
+        nc.vector.tensor_copy(
+            wq_planes[:].rearrange("p (b t s) -> p b t s", t=PACK, s=SPANS),
+            wq_scales_raw[:].rearrange("p a (g s t) -> p (a g) t s", t=PACK, s=SPANS),
+        )
+        gain_sorted = keep.tile([P, P], F32, name="gain_sorted", align_bytes=64)
+        nc.vector.tensor_copy(
+            gain_sorted[:].rearrange("p (t s i) -> p t s i", t=PACK, i=RUN),
+            gain_rows[:].rearrange("p (s t i) -> p t s i", t=PACK, i=RUN),
+        )
+        gain_turned = keep.tile([P, P], F32, name="gain_turned", align_bytes=64)
+        nc.vector.transpose(gain_turned[:], gain_sorted[:])
+        gains = keep.tile([P, GROUPS, PACK], F32, name="gains")
+        nc.vector.tensor_copy(gains[:], gain_turned[:].rearrange("p (t g x) -> p g t x", t=PACK, g=GROUPS)[:, :, :, 0])
         wq_codes = staging.tile(
             [P, PASSES * H // 2], I32, name="wq_codes", offset=table1_end + PASSES * H, align_bytes=64
         )
@@ -119,26 +137,12 @@ def tile_list_radar_log_power_kernel(tc, tab_words, tab_scales, offs, wi, wq_wor
             staging.tile([P, S], U32, name="v_codes0", offset=raw_end, align_bytes=64),
             keep.tile([P, S], U32, name="v_codes1", align_bytes=64),
         ]
-        nc.vector.tensor_copy(v_codes[0][:], table0[:].bitcast(U32).indirect(offsets[:]))
-        wq_planes = staging.tile([P, PASSES * H // 4], I32, name="wq_planes", offset=table1_end, align_bytes=64)
-        nc.vector.tensor_copy(
-            wq_planes[:].rearrange("p (b t s) -> p b t s", t=PACK, s=SPANS),
-            wq_scales_raw[:].rearrange("p a (g s t) -> p (a g) t s", t=PACK, s=SPANS),
-        )
-        gain_sorted = keep.tile([P, P], F32, name="gain_sorted", align_bytes=64)
-        nc.vector.tensor_copy(
-            gain_sorted[:].rearrange("p (t s i) -> p t s i", t=PACK, i=RUN),
-            gain_rows[:].rearrange("p (s t i) -> p t s i", t=PACK, i=RUN),
-        )
-        gain_turned = keep.tile([P, P], F32, name="gain_turned", align_bytes=64)
-        nc.vector.transpose(gain_turned[:], gain_sorted[:])
-        gains = keep.tile([P, GROUPS, PACK], F32, name="gains")
-        nc.vector.tensor_copy(gains[:], gain_turned[:].rearrange("p (t g x) -> p g t x", t=PACK, g=GROUPS)[:, :, :, 0])
-        for half in range(HALVES):
-            nc.vector.tensor_copy(
-                v_codes[1][:, half * BANK : (half + 1) * BANK],
-                table1[:].bitcast(U32).indirect(offsets[:, half * BANK // 16 : (half + 1) * BANK // 16]),
-            )
+        for a, table in enumerate((table0, table1)):
+            for half in range(HALVES):
+                nc.vector.tensor_copy(
+                    v_codes[a][:, half * BANK : (half + 1) * BANK],
+                    table[:].bitcast(U32).indirect(offsets[:, half * BANK // 16 : (half + 1) * BANK // 16]),
+                )
         wq_bytes = wq_codes[:].bitcast(U8)
         wq_scale_bytes = wq_planes[:].bitcast(U8)
 
@@ -195,6 +199,25 @@ def tile_list_radar_log_power_kernel(tc, tab_words, tab_scales, offs, wi, wq_wor
                 quadrature_pass(banks[half, t], g, half, t, 1)
                 quadrature_square(banks[half, t], g, half, t)
 
+        def quadrature_turned(g):
+            col = g * K_PASS
+            for start in range(0, S, P):
+                bank = psum.tile([P, BANK], F32, name="bank")
+                for a in range(PASSES):
+                    at = a * H + col
+                    nc.tensor.matmul_mx(
+                        out=bank[:],
+                        lhsT=v_codes[a][:, start : start + P].bitcast(FP8X4),
+                        lhsT_scale=v_scales[:, a * S + start : a * S + start + P],
+                        rhs=wq_bytes[:, 2 * at : 2 * (at + K_PASS)].bitcast(FP4X4),
+                        rhs_scale=wq_scale_bytes[:, at : at + K_PASS],
+                        start=(a == 0),
+                        stop=(a == PASSES - 1),
+                    )
+                tile = power[g, "half", start // BANK]
+                at = PACK * (start % BANK)
+                nc.scalar.activation(tile[:, at : at + BANK], bank[:], ACT.Square, bias=zero[:])
+
         wi_codes = {}
         wi_scales = {}
 
@@ -226,7 +249,43 @@ def tile_list_radar_log_power_kernel(tc, tab_words, tab_scales, offs, wi, wq_wor
                         )
                 nc.scalar.activation(squares[:, first * width : first * width + BANK], bank[:], ACT.Square, bias=zero[:])
             nc.vector.tensor_tensor(power[g, start], squares[:], power[g, start], ALU.add)
-            nc.scalar.activation(power[g, start], power[g, start], ACT.Ln, bias=one[:])
+            nc.scalar.activation(power[g, start], power[g, start], ACT.Ln, bias=1.0)
+
+        def log_power_turned(g, start, width):
+            squares = ring.tile([P, PACK * width], F32, name="squares")
+            for f in range(width // P):
+                bank = psum.tile([P, BANK], F32, name="bank")
+                first = start + f * P
+                for a in range(PASSES):
+                    nc.tensor.matmul_mx(
+                        out=bank[:],
+                        lhsT=v_codes[a][:, first : first + P].bitcast(FP8X4),
+                        lhsT_scale=v_scales[:, a * S + first : a * S + first + P],
+                        rhs=wi_codes[g, a][:].bitcast(FP8X4),
+                        rhs_scale=wi_scales[g, a][:],
+                        start=(a == 0),
+                        stop=(a == PASSES - 1),
+                    )
+                nc.scalar.activation(squares[:, f * BANK : (f + 1) * BANK], bank[:], ACT.Square, bias=zero[:])
+            for f in range(width // P):
+                bank = psum.tile([P, BANK], F32, name="bank")
+                for t in range(PACK):
+                    cols = slice(f * BANK + t * P, f * BANK + (t + 1) * P)
+                    for n, term in enumerate((power[g, start], squares)):
+                        nc.tensor.matmul(
+                            bank[:, t * P : (t + 1) * P],
+                            term[:, cols],
+                            identity[:],
+                            start=(n == 0),
+                            stop=(n == 1),
+                            is_transpose=True,
+                        )
+                nc.scalar.activation(
+                    power[g, start][:, f * BANK : (f + 1) * BANK].rearrange("p (j t) -> p j t", t=PACK),
+                    bank[:].rearrange("p (t j) -> p j t", t=PACK),
+                    ACT.Ln,
+                    bias=1.0,
+                )
 
         h_codes = [keep.tile([P, S], U32, name=f"h_codes{g}", align_bytes=64) for g in range(GROUPS)]
         h_scales = [keep.tile([P, S], U8, name=f"h_scales{g}", align_bytes=64) for g in range(GROUPS)]
@@ -238,6 +297,16 @@ def tile_list_radar_log_power_kernel(tc, tab_words, tab_scales, offs, wi, wq_wor
                 h[:].rearrange("p (c i t) -> p c t i", i=RUN, t=PACK),
                 power[g, start].rearrange("p (t c i) -> p c t i", t=PACK, i=RUN),
                 gains[:, g, :].unsqueeze(1).unsqueeze(3).to_broadcast([P, width // RUN, PACK, RUN]),
+                ALU.mult,
+            )
+            h_rounded[g, start] = h
+
+        def apply_gain_turned(g, start, width):
+            h = ring.tile([P, PACK * width], BF16, name="h", align_bytes=64)
+            nc.vector.tensor_tensor(
+                h[:].rearrange("p (j t) -> p j t", t=PACK),
+                power[g, start].rearrange("p (j t) -> p j t", t=PACK),
+                gains[:, g, :].unsqueeze(1).to_broadcast([P, width, PACK]),
                 ALU.mult,
             )
             h_rounded[g, start] = h
@@ -268,7 +337,7 @@ def tile_list_radar_log_power_kernel(tc, tab_words, tab_scales, offs, wi, wq_wor
 
         out_rows = out.rearrange("(c p) j -> p c j", p=P)
 
-        def features(start, width):
+        def features(start, width, copy):
             result = ring.tile([P, N_TILES, width], F32, name="result")
             per_bank = BANK // width
             for first in range(0, N_TILES, per_bank):
@@ -286,7 +355,7 @@ def tile_list_radar_log_power_kernel(tc, tab_words, tab_scales, offs, wi, wq_wor
                             start=(g == 0),
                             stop=(g == GROUPS - 1),
                         )
-                nc.scalar.copy(
+                copy(
                     result[:, first:last, :].rearrange("p c j -> p (c j)"), bank[:, : (last - first) * width]
                 )
             nc.sync.dma_start(out_rows[:, :, start : start + width], result[:])
@@ -294,32 +363,28 @@ def tile_list_radar_log_power_kernel(tc, tab_words, tab_scales, offs, wi, wq_wor
         quadrature(0, True)
         prepare_wi(0, 0)
         prepare_wi(0, 1)
-        log_power(0, *units[0][0])
-        log_power(0, *units[0][1])
-        prepare_wi(1, 0)
-        log_power(0, *units[0][2])
-        prepare_wi(1, 1)
-        log_power(0, *units[0][3])
-        quadrature(1, False)
-        log_power(1, *units[1][0])
-        apply_gain(0, *units[0][0])
-        round_w2(0, nc.vector.tensor_copy)
-        quantize_h(0, *units[0][0])
-        round_w2(1, nc.scalar.copy)
-        apply_gain(0, *units[0][1])
-        quantize_w2(0, 512)
-        quantize_w2(512, 256)
-        quantize_h(0, *units[0][1])
-        later = list(units[0][2:])
-        count = len(units[1])
-        for u in range(count):
-            if u + 1 < count:
-                log_power(1, *units[1][u + 1])
-            apply_gain(1, *units[1][u])
-            extra = later.pop(0) if later else None
-            if extra:
-                apply_gain(0, *extra)
-            quantize_h(1, *units[1][u])
-            if extra:
-                quantize_h(0, *extra)
-            features(*units[1][u])
+        order = [(0, 0), (0, 1), (1, 0), (0, 2), (1, 1), (0, 3), (1, 2), (0, 4), (1, 3), (1, 4)]
+        lag = 2
+        for step in range(len(order) + lag + 1):
+            if step == 1:
+                prepare_wi(1, 0)
+            if step == 2:
+                prepare_wi(1, 1)
+                quadrature_turned(1)
+            if step == 3:
+                round_w2(0, nc.vector.tensor_copy)
+                round_w2(1, nc.vector.tensor_copy)
+            if step < len(order):
+                g, u = order[step]
+                (log_power, log_power_turned)[g](g, *units[g][u])
+            if step == 4:
+                quantize_w2(0, 512)
+                quantize_w2(512, 256)
+            if 0 <= step - lag < len(order):
+                g, u = order[step - lag]
+                (apply_gain, apply_gain_turned)[g](g, *units[g][u])
+            if 0 <= step - lag - 1:
+                g, u = order[step - lag - 1]
+                quantize_h(g, *units[g][u])
+                if g == 1:
+                    features(*units[g][u], nc.vector.tensor_copy if u < 2 else nc.scalar.copy)

@@ -26,6 +26,8 @@ BANK = 512
 HALVES = S // BANK
 N_TILES = N // P
 RUN = 4
+TURNED = ((1, 0), (1, 1))
+VECTOR_COPIES = 2
 SPAN = PACK * RUN
 SPANS = K_PASS // SPAN
 UNIT_WIDTHS = (((256, 256), (256, 128, 128)), ((256, 256), (256, 128, 128)))
@@ -117,6 +119,10 @@ def tile_list_radar_log_power_kernel(tc, tab_words, tab_scales, offs, wi, wq_wor
             wq_raw[:].rearrange("p a (g s t w) -> p (a g) t s w", t=PACK, s=SPANS, w=2),
         )
 
+        def pieces(g):
+            width = K_PASS // (2 if g == 0 else 1)
+            return [slice(first, first + width) for first in range(0, K_PASS, width)]
+
         raw = staging.tile([P, raw_columns], F32, name="raw", offset=0, align_bytes=64)
         wi_raw = {}
         for g in range(GROUPS):
@@ -124,7 +130,8 @@ def tile_list_radar_log_power_kernel(tc, tab_words, tab_scales, offs, wi, wq_wor
                 at = (g * PASSES + a) * piece
                 wi_raw[g, a] = raw[:, at : at + piece].rearrange("p (j c) -> p j c", j=PACK)
                 rows = wi[a * K_PASS : (a + 1) * K_PASS, g * K_PASS : (g + 1) * K_PASS]
-                nc.sync.dma_start(wi_raw[g, a], rows.rearrange("(p j) c -> p j c", j=PACK))
+                for cols in pieces(g):
+                    nc.sync.dma_start(wi_raw[g, a][:, :, cols], rows.rearrange("(p j) c -> p j c", j=PACK)[:, :, cols])
         w2_raw = []
         for g in range(GROUPS):
             at = w2_at + g * PACK * N
@@ -185,48 +192,51 @@ def tile_list_radar_log_power_kernel(tc, tab_words, tab_scales, offs, wi, wq_wor
                 )
                 at += span
 
+        def turned_pass(bank, g, half, k, a):
+            start = half * BANK + k * P
+            at = a * H + g * K_PASS
+            nc.tensor.matmul_mx(
+                out=bank[:],
+                lhsT=v_codes[a][:, start : start + P].bitcast(FP8X4),
+                lhsT_scale=v_scales[:, a * S + start : a * S + start + P],
+                rhs=wq_bytes[:, 2 * at : 2 * (at + K_PASS)].bitcast(FP4X4),
+                rhs_scale=wq_scale_bytes[:, at : at + K_PASS],
+                start=(a == 0),
+                stop=(a == PASSES - 1),
+            )
+
+        def turned_square(bank, g, half, k):
+            tile = power[g, "half", half]
+            nc.scalar.activation(tile[:, k * BANK : (k + 1) * BANK], bank[:], ACT.Square, bias=zero[:])
+
         def quadrature(g, first_pass_ahead):
             slots = [(half, t) for half in range(HALVES) for t in range(PACK)]
             banks = {}
+            one_pass = {half: turned_pass if (g, half) in TURNED else quadrature_pass for half in range(HALVES)}
+            square = {half: turned_square if (g, half) in TURNED else quadrature_square for half in range(HALVES)}
             if first_pass_ahead:
                 for half, t in slots:
                     banks[half, t] = psum.tile([P, BANK], F32, name="bank")
-                    quadrature_pass(banks[half, t], g, half, t, 0)
+                    one_pass[half](banks[half, t], g, half, t, 0)
             for half, t in slots:
                 if not first_pass_ahead:
                     banks[half, t] = psum.tile([P, BANK], F32, name="bank")
-                    quadrature_pass(banks[half, t], g, half, t, 0)
-                quadrature_pass(banks[half, t], g, half, t, 1)
-                quadrature_square(banks[half, t], g, half, t)
-
-        def quadrature_turned(g):
-            col = g * K_PASS
-            for start in range(0, S, P):
-                bank = psum.tile([P, BANK], F32, name="bank")
-                for a in range(PASSES):
-                    at = a * H + col
-                    nc.tensor.matmul_mx(
-                        out=bank[:],
-                        lhsT=v_codes[a][:, start : start + P].bitcast(FP8X4),
-                        lhsT_scale=v_scales[:, a * S + start : a * S + start + P],
-                        rhs=wq_bytes[:, 2 * at : 2 * (at + K_PASS)].bitcast(FP4X4),
-                        rhs_scale=wq_scale_bytes[:, at : at + K_PASS],
-                        start=(a == 0),
-                        stop=(a == PASSES - 1),
-                    )
-                tile = power[g, "half", start // BANK]
-                at = PACK * (start % BANK)
-                nc.scalar.activation(tile[:, at : at + BANK], bank[:], ACT.Square, bias=zero[:])
+                    one_pass[half](banks[half, t], g, half, t, 0)
+                one_pass[half](banks[half, t], g, half, t, 1)
+                square[half](banks[half, t], g, half, t)
 
         wi_codes = {}
         wi_scales = {}
 
         def prepare_wi(g, a):
             grouped = ring.tile([P, piece], BF16, name="grouped", align_bytes=64)
-            nc.vector.tensor_copy(
-                grouped[:].rearrange("p (t s i j) -> p t s j i", t=PACK, i=RUN, j=PACK),
-                wi_raw[g, a].rearrange("p j (s t i) -> p t s j i", t=PACK, i=RUN),
-            )
+            for cols in pieces(g):
+                nc.vector.tensor_copy(
+                    grouped[:].rearrange("p (t s i j) -> p t s j i", t=PACK, i=RUN, j=PACK)[
+                        :, :, cols.start // SPAN : cols.stop // SPAN
+                    ],
+                    wi_raw[g, a][:, :, cols].rearrange("p j (s t i) -> p t s j i", t=PACK, i=RUN),
+                )
             wi_codes[g, a] = keep.tile([P, K_PASS], U32, name=f"wi_codes{g}_{a}", align_bytes=64)
             wi_scales[g, a] = keep.tile([P, K_PASS], U8, name=f"wi_scales{g}_{a}", align_bytes=64)
             nc.vector.quantize_mx(out=wi_codes[g, a][:].bitcast(FP8X4), scales=wi_scales[g, a][:], in_=grouped[:])
@@ -370,21 +380,21 @@ def tile_list_radar_log_power_kernel(tc, tab_words, tab_scales, offs, wi, wq_wor
                 prepare_wi(1, 0)
             if step == 2:
                 prepare_wi(1, 1)
-                quadrature_turned(1)
+                quadrature(1, False)
             if step == 3:
                 round_w2(0, nc.vector.tensor_copy)
                 round_w2(1, nc.vector.tensor_copy)
             if step < len(order):
                 g, u = order[step]
-                (log_power, log_power_turned)[g](g, *units[g][u])
+                (log_power_turned if (g, units[g][u][0] // BANK) in TURNED else log_power)(g, *units[g][u])
             if step == 4:
                 quantize_w2(0, 512)
                 quantize_w2(512, 256)
             if 0 <= step - lag < len(order):
                 g, u = order[step - lag]
-                (apply_gain, apply_gain_turned)[g](g, *units[g][u])
+                (apply_gain_turned if (g, units[g][u][0] // BANK) in TURNED else apply_gain)(g, *units[g][u])
             if 0 <= step - lag - 1:
                 g, u = order[step - lag - 1]
                 quantize_h(g, *units[g][u])
                 if g == 1:
-                    features(*units[g][u], nc.vector.tensor_copy if u < 2 else nc.scalar.copy)
+                    features(*units[g][u], nc.vector.tensor_copy if u < VECTOR_COPIES else nc.scalar.copy)

@@ -26,11 +26,13 @@ BANK = 512
 HALVES = S // BANK
 N_TILES = N // P
 RUN = 4
-TURNED = ((1, 0), (1, 1))
-VECTOR_COPIES = 2
 SPAN = PACK * RUN
 SPANS = K_PASS // SPAN
-UNIT_WIDTHS = (((256, 256), (256, 128, 128)), ((256, 256), (256, 128, 128)))
+FIRST_UNITS = ((0, 256), (256, 256), (512, 256), (768, 128), (896, 128))
+SECOND_UNITS = ((0, 256), (256, 256), (512, 256), (768, 128), (896, 128))
+UPRIGHT = ((0, 0), (0, 1))
+UNITS = (FIRST_UNITS, SECOND_UNITS)
+VECTOR_COPIES = 2
 
 
 def tile_list_radar_log_power_kernel(tc, tab_words, tab_scales, offs, wi, wq_words, wq_scales, gain, w2, out):
@@ -47,83 +49,70 @@ def tile_list_radar_log_power_kernel(tc, tab_words, tab_scales, offs, wi, wq_wor
         piece = PACK * K_PASS
         w2_at = GROUPS * PASSES * piece
         raw_columns = w2_at + GROUPS * PACK * N
-        raw_end = 4 * raw_columns
-        table1_at = raw_end + 4 * S
+        table0_at = 0
+        raw_at = table0_at + 4 * T - 64
+        table1_at = raw_at + 4 * raw_columns
         table1_end = table1_at + 4 * T
 
+        wq_rows = wq_words.rearrange("a p c -> p a c").bitcast(I32)
+        wq_raw = [
+            keep.tile([P, PASSES, K_PASS // 2], I32, name="wq_raw0", align_bytes=64),
+            staging.tile([P, PASSES, K_PASS // 2], I32, name="wq_raw1", offset=table1_end, align_bytes=64),
+        ]
+
+        seed = staging.tile([P, 1], F32, name="seed", offset=table0_at, align_bytes=64)
+        nc.vector.memset(seed[:], 0.0)
+
         scale_window = staging.tile([P, T // 4], I32, name="scale_window", offset=table1_end - 64, align_bytes=64)
-        nc.vector.memset(scale_window[:], 0)
-        nc.sync.dma_start(scale_window[0:P:4, :], tab_scales.rearrange("a q t -> (a q) t").bitcast(I32))
+        nc.sync.dma_start(scale_window[0:32, :], tab_scales.rearrange("a q t -> (a q) t").bitcast(I32))
+        nc.sync.dma_start(wq_raw[0][:], wq_rows[:, :, : K_PASS // 2])
         wq_scales_raw = keep.tile([P, PASSES, H // 4], I32, name="wq_scales_raw", align_bytes=64)
         nc.vector.memset(wq_scales_raw[:], 0)
-        gain_rows = keep.tile([P, P], F32, name="gain_rows")
-        nc.vector.memset(gain_rows[:], 0.0)
-        one = keep.tile([P, 1], F32, name="one", tag="table0", align_bytes=64)
-        nc.vector.memset(one[:], 1.0)
-        v_planes = keep.tile([P, PASSES * S // 4], I32, name="v_planes", align_bytes=64)
-        nc.vector.memset(v_planes[:], 0)
-        zero = keep.tile([P, 1], F32, name="zero")
-        nc.scalar.activation(zero[:], one[:], ACT.Ln)
-
-        identity = keep.tile([P, P], F32, name="identity")
-        make_identity(nc, identity[:])
-
         for quad in range(4):
             nc.sync.dma_start(
                 wq_scales_raw[32 * quad : 32 * quad + 4, :, :],
                 wq_scales[:, 4 * quad : 4 * quad + 4, :].rearrange("a r c -> r a c").bitcast(I32),
             )
-        nc.sync.dma_start(gain_rows[0:P:16, :], gain.rearrange("(g b c) -> b g c", g=GROUPS, c=P))
-        wq_raw = staging.tile([P, PASSES, H // 2], I32, name="wq_raw", offset=raw_end - 64, align_bytes=64)
-        nc.sync.dma_start(wq_raw[:], wq_words.rearrange("a p c -> p a c").bitcast(I32))
-
-        table0 = keep.tile([P, T], I32, name="table0", tag="table0", align_bytes=64)
+        one = keep.tile([P, 1], F32, name="one")
+        nc.vector.tensor_scalar_add(one[:], seed[:], 1.0)
+        nc.vector.memset(scale_window[32:64, :], 0)
+        nc.vector.memset(scale_window[64:P, :], 0)
+        table0 = staging.tile([P, T], I32, name="table0", offset=table0_at, align_bytes=64)
         nc.sync.dma_start(table0[:], tab_words[0].rearrange("p t i -> p (t i)").bitcast(I32))
+
+        identity = keep.tile([P, P], F32, name="identity")
+        make_identity(nc, identity[:])
+        zero = keep.tile([P, 1], F32, name="zero")
+        nc.scalar.activation(zero[:], one[:], ACT.Ln)
+        gain_rows = keep.tile([P, P], F32, name="gain_rows")
+        nc.vector.memset(gain_rows[:], 0.0)
+        nc.sync.dma_start(gain_rows[0:P:16, :], gain.rearrange("(g b c) -> b g c", g=GROUPS, c=P))
+        v_planes = keep.tile([P, PASSES * S // 4], I32, name="v_planes", align_bytes=64)
+        nc.vector.memset(v_planes[:], 0)
 
         picked_scales = keep.tile([P, S // 4], I32, name="picked_scales", align_bytes=64)
         nc.vector.tensor_copy(picked_scales[:].bitcast(U8), scale_window[:].bitcast(U8).indirect(offsets[:]))
 
         def place_scales(a):
             for quad in range(4):
-                first = 64 * a + 16 * quad
+                first = 16 * a + 4 * quad
                 nc.sync.dma_start(
                     v_planes[32 * quad : 32 * quad + 4, a * S // 4 : (a + 1) * S // 4],
-                    picked_scales[first : first + 16 : 4, :],
+                    picked_scales[first : first + 4, :],
                 )
 
         place_scales(0)
         table1 = staging.tile([P, T], I32, name="table1", offset=table1_at, align_bytes=64)
         nc.sync.dma_start(table1[:], tab_words[1].rearrange("p t i -> p (t i)").bitcast(I32))
         place_scales(1)
+        nc.sync.dma_start(wq_raw[1][:], wq_rows[:, :, K_PASS // 2 :])
         v_scales = v_planes[:].bitcast(U8)
-
-        wq_planes = staging.tile([P, PASSES * H // 4], I32, name="wq_planes", offset=table1_end, align_bytes=64)
-        nc.vector.tensor_copy(
-            wq_planes[:].rearrange("p (b t s) -> p b t s", t=PACK, s=SPANS),
-            wq_scales_raw[:].rearrange("p a (g s t) -> p (a g) t s", t=PACK, s=SPANS),
-        )
-        gain_sorted = keep.tile([P, P], F32, name="gain_sorted", align_bytes=64)
-        nc.vector.tensor_copy(
-            gain_sorted[:].rearrange("p (t s i) -> p t s i", t=PACK, i=RUN),
-            gain_rows[:].rearrange("p (s t i) -> p t s i", t=PACK, i=RUN),
-        )
-        gain_turned = keep.tile([P, P], F32, name="gain_turned", align_bytes=64)
-        nc.vector.transpose(gain_turned[:], gain_sorted[:])
-        gains = keep.tile([P, GROUPS, PACK], F32, name="gains")
-        nc.vector.tensor_copy(gains[:], gain_turned[:].rearrange("p (t g x) -> p g t x", t=PACK, g=GROUPS)[:, :, :, 0])
-        wq_codes = staging.tile(
-            [P, PASSES * H // 2], I32, name="wq_codes", offset=table1_end + PASSES * H, align_bytes=64
-        )
-        nc.vector.tensor_copy(
-            wq_codes[:].rearrange("p (b t s w) -> p b t s w", t=PACK, s=SPANS, w=2),
-            wq_raw[:].rearrange("p a (g s t w) -> p (a g) t s w", t=PACK, s=SPANS, w=2),
-        )
 
         def pieces(g):
             width = K_PASS // (2 if g == 0 else 1)
             return [slice(first, first + width) for first in range(0, K_PASS, width)]
 
-        raw = staging.tile([P, raw_columns], F32, name="raw", offset=0, align_bytes=64)
+        raw = staging.tile([P, raw_columns], F32, name="raw", offset=raw_at, align_bytes=64)
         wi_raw = {}
         for g in range(GROUPS):
             for a in range(PASSES):
@@ -140,95 +129,134 @@ def tile_list_radar_log_power_kernel(tc, tab_words, tab_scales, offs, wi, wq_wor
             for t in range(PACK):
                 nc.sync.dma_start(w2_raw[g][:, t * N : (t + 1) * N], rows[t])
 
-        v_codes = [
-            staging.tile([P, S], U32, name="v_codes0", offset=raw_end, align_bytes=64),
-            keep.tile([P, S], U32, name="v_codes1", align_bytes=64),
-        ]
-        for a, table in enumerate((table0, table1)):
+        v_codes = [keep.tile([P, S], U32, name=f"v_codes{a}", align_bytes=64) for a in range(PASSES)]
+
+        def gather_words(a, table):
             for half in range(HALVES):
                 nc.vector.tensor_copy(
                     v_codes[a][:, half * BANK : (half + 1) * BANK],
                     table[:].bitcast(U32).indirect(offsets[:, half * BANK // 16 : (half + 1) * BANK // 16]),
                 )
-        wq_bytes = wq_codes[:].bitcast(U8)
-        wq_scale_bytes = wq_planes[:].bitcast(U8)
+
+        wq_codes = {}
+        wq_planes = {}
+
+        def is_sorted(g):
+            return any((g, half) in UPRIGHT for half in range(HALVES))
+
+        def sort_wq(g):
+            if not is_sorted(g):
+                wq_codes[g] = [wq_raw[g][:, a, :].bitcast(U8) for a in range(PASSES)]
+                wq_planes[g] = [wq_scales_raw[:, a, g * P : (g + 1) * P].bitcast(U8) for a in range(PASSES)]
+                return
+            planes = keep.tile([P, PASSES, K_PASS // 4], I32, name=f"wq_planes{g}", align_bytes=64)
+            nc.vector.tensor_copy(
+                planes[:].rearrange("p a (t s) -> p a t s", t=PACK),
+                wq_scales_raw[:, :, g * P : (g + 1) * P].rearrange("p a (s t) -> p a t s", t=PACK),
+            )
+            codes = keep.tile([P, PASSES, K_PASS // 2], I32, name=f"wq_codes{g}", align_bytes=64)
+            nc.vector.tensor_copy(
+                codes[:].rearrange("p a (t s w) -> p a t s w", t=PACK, w=2),
+                wq_raw[g][:].rearrange("p a (s t w) -> p a t s w", t=PACK, w=2),
+            )
+            wq_codes[g] = [codes[:, a, :].bitcast(U8) for a in range(PASSES)]
+            wq_planes[g] = [planes[:, a, :].bitcast(U8) for a in range(PASSES)]
+
+        sort_wq(0)
+        gather_words(0, table0)
+        gain_sorted = keep.tile([P, P], F32, name="gain_sorted", align_bytes=64)
+        nc.vector.tensor_copy(
+            gain_sorted[:].rearrange("p (t s i) -> p t s i", t=PACK, i=RUN),
+            gain_rows[:].rearrange("p (s t i) -> p t s i", t=PACK, i=RUN),
+        )
+        gain_turned = keep.tile([P, P], F32, name="gain_turned", align_bytes=64)
+        nc.vector.transpose(gain_turned[:], gain_sorted[:])
+        gains = keep.tile([P, GROUPS, PACK], F32, name="gains")
+        nc.vector.tensor_copy(gains[:], gain_turned[:].rearrange("p (t g x) -> p g t x", t=PACK, g=GROUPS)[:, :, :, 0])
+        gather_words(1, table1)
+        sort_wq(1)
 
         power = {}
-        units = {}
         for g in range(GROUPS):
-            units[g] = []
             for half in range(HALVES):
-                tile = keep.tile([P, PACK * BANK], F32, name=f"power{g}_{half}")
-                at = 0
-                for width in UNIT_WIDTHS[g][half]:
-                    units[g].append((half * BANK + at, width))
-                    power[g, half * BANK + at] = tile[:, PACK * at : PACK * (at + width)]
-                    at += width
-                power[g, "half", half] = tile
+                power[g, half] = keep.tile([P, PACK * BANK], F32, name=f"power{g}_{half}")
 
-        def quadrature_pass(bank, g, half, t, a):
-            col = (a * GROUPS + g) * K_PASS + t * P
+        def power_of(g, start, width):
+            at = PACK * (start % BANK)
+            return power[g, start // BANK][:, at : at + PACK * width]
+
+        def is_upright(g, start):
+            return (g, start // BANK) in UPRIGHT
+
+        def cells_pass(bank, first, a, codes, scales):
             nc.tensor.matmul_mx(
                 out=bank[:],
-                lhsT=wq_bytes[:, 2 * col : 2 * (col + P)].bitcast(FP4X4),
-                lhsT_scale=wq_scale_bytes[:, col : col + P],
-                rhs=v_codes[a][:, half * BANK : (half + 1) * BANK].bitcast(FP8X4),
-                rhs_scale=v_scales[:, a * S + half * BANK : a * S + (half + 1) * BANK],
+                lhsT=v_codes[a][:, first : first + P].bitcast(FP8X4),
+                lhsT_scale=v_scales[:, a * S + first : a * S + first + P],
+                rhs=codes,
+                rhs_scale=scales,
                 start=(a == 0),
                 stop=(a == PASSES - 1),
             )
 
-        def quadrature_square(bank, g, half, t):
-            tile = power[g, "half", half]
-            widths = UNIT_WIDTHS[g][half]
-            at = 0
-            for width in sorted(set(widths), reverse=True):
-                span = width * widths.count(width)
+        def quadrature_pass(bank, g, half, k, a):
+            if (g, half) in UPRIGHT:
+                nc.tensor.matmul_mx(
+                    out=bank[:],
+                    lhsT=wq_codes[g][a][:, 2 * k * P : 2 * (k + 1) * P].bitcast(FP4X4),
+                    lhsT_scale=wq_planes[g][a][:, k * P : (k + 1) * P],
+                    rhs=v_codes[a][:, half * BANK : (half + 1) * BANK].bitcast(FP8X4),
+                    rhs_scale=v_scales[:, a * S + half * BANK : a * S + (half + 1) * BANK],
+                    start=(a == 0),
+                    stop=(a == PASSES - 1),
+                )
+            else:
+                cells_pass(bank, half * BANK + k * P, a, wq_codes[g][a].bitcast(FP4X4), wq_planes[g][a])
+
+        def quadrature_square(bank, g, half, k):
+            if (g, half) in UPRIGHT:
+                widths = [width for start, width in sorted(UNITS[g]) if start // BANK == half]
+                at = 0
+                for width in sorted(set(widths), reverse=True):
+                    span = width * widths.count(width)
+                    nc.scalar.activation(
+                        power_of(g, half * BANK + at, span).rearrange("p (u t j) -> p u t j", t=PACK, j=width)[:, :, k, :],
+                        bank[:, at : at + span].rearrange("p (u j) -> p u j", j=width),
+                        ACT.Square,
+                        bias=zero[:],
+                    )
+                    at += span
+            elif is_sorted(g):
+                nc.scalar.activation(power_of(g, half * BANK + k * P, P), bank[:], ACT.Square, bias=zero[:])
+            else:
                 nc.scalar.activation(
-                    tile[:, PACK * at : PACK * (at + span)].rearrange("p (u t j) -> p u t j", t=PACK, j=width)[:, :, t, :],
-                    bank[:, at : at + span].rearrange("p (u j) -> p u j", j=width),
+                    power_of(g, half * BANK + k * P, P).rearrange("p (t s i) -> p t s i", t=PACK, i=RUN),
+                    bank[:].rearrange("p (s t i) -> p t s i", t=PACK, i=RUN),
                     ACT.Square,
                     bias=zero[:],
                 )
-                at += span
 
-        def turned_pass(bank, g, half, k, a):
-            start = half * BANK + k * P
-            at = a * H + g * K_PASS
-            nc.tensor.matmul_mx(
-                out=bank[:],
-                lhsT=v_codes[a][:, start : start + P].bitcast(FP8X4),
-                lhsT_scale=v_scales[:, a * S + start : a * S + start + P],
-                rhs=wq_bytes[:, 2 * at : 2 * (at + K_PASS)].bitcast(FP4X4),
-                rhs_scale=wq_scale_bytes[:, at : at + K_PASS],
-                start=(a == 0),
-                stop=(a == PASSES - 1),
-            )
+        def first_quadrature():
+            slots = [(half, k) for half in range(HALVES) for k in range(PACK)]
+            banks = [psum.tile([P, BANK], F32, name="bank") for slot in slots]
+            for a in range(PASSES):
+                for bank, (half, k) in zip(banks, slots):
+                    quadrature_pass(bank, 0, half, k, a)
+                    if a == PASSES - 1:
+                        quadrature_square(bank, 0, half, k)
 
-        def turned_square(bank, g, half, k):
-            tile = power[g, "half", half]
-            nc.scalar.activation(tile[:, k * BANK : (k + 1) * BANK], bank[:], ACT.Square, bias=zero[:])
+        def second_quadrature(half):
+            for k in range(PACK):
+                bank = psum.tile([P, BANK], F32, name="bank")
+                for a in range(PASSES):
+                    quadrature_pass(bank, 1, half, k, a)
+                quadrature_square(bank, 1, half, k)
 
-        def quadrature(g, first_pass_ahead):
-            slots = [(half, t) for half in range(HALVES) for t in range(PACK)]
-            banks = {}
-            one_pass = {half: turned_pass if (g, half) in TURNED else quadrature_pass for half in range(HALVES)}
-            square = {half: turned_square if (g, half) in TURNED else quadrature_square for half in range(HALVES)}
-            if first_pass_ahead:
-                for half, t in slots:
-                    banks[half, t] = psum.tile([P, BANK], F32, name="bank")
-                    one_pass[half](banks[half, t], g, half, t, 0)
-            for half, t in slots:
-                if not first_pass_ahead:
-                    banks[half, t] = psum.tile([P, BANK], F32, name="bank")
-                    one_pass[half](banks[half, t], g, half, t, 0)
-                one_pass[half](banks[half, t], g, half, t, 1)
-                square[half](banks[half, t], g, half, t)
-
+        wi_grouped = {}
         wi_codes = {}
         wi_scales = {}
 
-        def prepare_wi(g, a):
+        def round_wi(g, a):
             grouped = ring.tile([P, piece], BF16, name="grouped", align_bytes=64)
             for cols in pieces(g):
                 nc.vector.tensor_copy(
@@ -237,51 +265,57 @@ def tile_list_radar_log_power_kernel(tc, tab_words, tab_scales, offs, wi, wq_wor
                     ],
                     wi_raw[g, a][:, :, cols].rearrange("p j (s t i) -> p t s j i", t=PACK, i=RUN),
                 )
+            wi_grouped[g, a] = grouped
+
+        def quantize_wi(g, a):
             wi_codes[g, a] = keep.tile([P, K_PASS], U32, name=f"wi_codes{g}_{a}", align_bytes=64)
             wi_scales[g, a] = keep.tile([P, K_PASS], U8, name=f"wi_scales{g}_{a}", align_bytes=64)
-            nc.vector.quantize_mx(out=wi_codes[g, a][:].bitcast(FP8X4), scales=wi_scales[g, a][:], in_=grouped[:])
+            nc.vector.quantize_mx(
+                out=wi_codes[g, a][:].bitcast(FP8X4), scales=wi_scales[g, a][:], in_=wi_grouped[g, a][:]
+            )
+
+        squares = {}
+
+        def in_phase(g, start, width):
+            squares[g, start] = ring.tile([P, PACK * width], F32, name="squares")
+            if is_upright(g, start):
+                per_bank = BANK // width
+                for first in range(0, PACK, per_bank):
+                    bank = psum.tile([P, BANK], F32, name="bank")
+                    for t in range(first, first + per_bank):
+                        for a in range(PASSES):
+                            nc.tensor.matmul_mx(
+                                out=bank[:, (t - first) * width : (t - first + 1) * width],
+                                lhsT=wi_codes[g, a][:, t * P : (t + 1) * P].bitcast(FP8X4),
+                                lhsT_scale=wi_scales[g, a][:, t * P : (t + 1) * P],
+                                rhs=v_codes[a][:, start : start + width].bitcast(FP8X4),
+                                rhs_scale=v_scales[:, a * S + start : a * S + start + width],
+                                start=(a == 0),
+                                stop=(a == PASSES - 1),
+                            )
+                    nc.scalar.activation(
+                        squares[g, start][:, first * width : first * width + BANK], bank[:], ACT.Square, bias=zero[:]
+                    )
+            else:
+                for f in range(width // P):
+                    bank = psum.tile([P, BANK], F32, name="bank")
+                    for a in range(PASSES):
+                        cells_pass(bank, start + f * P, a, wi_codes[g, a][:].bitcast(FP8X4), wi_scales[g, a][:])
+                    nc.scalar.activation(
+                        squares[g, start][:, f * BANK : (f + 1) * BANK], bank[:], ACT.Square, bias=zero[:]
+                    )
 
         def log_power(g, start, width):
-            squares = ring.tile([P, PACK * width], F32, name="squares")
-            per_bank = BANK // width
-            for first in range(0, PACK, per_bank):
-                bank = psum.tile([P, BANK], F32, name="bank")
-                for t in range(first, first + per_bank):
-                    for a in range(PASSES):
-                        nc.tensor.matmul_mx(
-                            out=bank[:, (t - first) * width : (t - first + 1) * width],
-                            lhsT=wi_codes[g, a][:, t * P : (t + 1) * P].bitcast(FP8X4),
-                            lhsT_scale=wi_scales[g, a][:, t * P : (t + 1) * P],
-                            rhs=v_codes[a][:, start : start + width].bitcast(FP8X4),
-                            rhs_scale=v_scales[:, a * S + start : a * S + start + width],
-                            start=(a == 0),
-                            stop=(a == PASSES - 1),
-                        )
-                nc.scalar.activation(squares[:, first * width : first * width + BANK], bank[:], ACT.Square, bias=zero[:])
-            nc.vector.tensor_tensor(power[g, start], squares[:], power[g, start], ALU.add)
-            nc.scalar.activation(power[g, start], power[g, start], ACT.Ln, bias=1.0)
-
-        def log_power_turned(g, start, width):
-            squares = ring.tile([P, PACK * width], F32, name="squares")
-            for f in range(width // P):
-                bank = psum.tile([P, BANK], F32, name="bank")
-                first = start + f * P
-                for a in range(PASSES):
-                    nc.tensor.matmul_mx(
-                        out=bank[:],
-                        lhsT=v_codes[a][:, first : first + P].bitcast(FP8X4),
-                        lhsT_scale=v_scales[:, a * S + first : a * S + first + P],
-                        rhs=wi_codes[g, a][:].bitcast(FP8X4),
-                        rhs_scale=wi_scales[g, a][:],
-                        start=(a == 0),
-                        stop=(a == PASSES - 1),
-                    )
-                nc.scalar.activation(squares[:, f * BANK : (f + 1) * BANK], bank[:], ACT.Square, bias=zero[:])
+            total = power_of(g, start, width)
+            if is_upright(g, start):
+                nc.vector.tensor_tensor(total, squares[g, start][:], total, ALU.add)
+                nc.scalar.activation(total, total, ACT.Ln, bias=1.0)
+                return
             for f in range(width // P):
                 bank = psum.tile([P, BANK], F32, name="bank")
                 for t in range(PACK):
                     cols = slice(f * BANK + t * P, f * BANK + (t + 1) * P)
-                    for n, term in enumerate((power[g, start], squares)):
+                    for n, term in enumerate((total, squares[g, start])):
                         nc.tensor.matmul(
                             bank[:, t * P : (t + 1) * P],
                             term[:, cols],
@@ -291,7 +325,7 @@ def tile_list_radar_log_power_kernel(tc, tab_words, tab_scales, offs, wi, wq_wor
                             is_transpose=True,
                         )
                 nc.scalar.activation(
-                    power[g, start][:, f * BANK : (f + 1) * BANK].rearrange("p (j t) -> p j t", t=PACK),
+                    total[:, f * BANK : (f + 1) * BANK].rearrange("p (j t) -> p j t", t=PACK),
                     bank[:].rearrange("p (t j) -> p j t", t=PACK),
                     ACT.Ln,
                     bias=1.0,
@@ -303,22 +337,20 @@ def tile_list_radar_log_power_kernel(tc, tab_words, tab_scales, offs, wi, wq_wor
 
         def apply_gain(g, start, width):
             h = ring.tile([P, PACK * width], BF16, name="h", align_bytes=64)
-            nc.vector.tensor_tensor(
-                h[:].rearrange("p (c i t) -> p c t i", i=RUN, t=PACK),
-                power[g, start].rearrange("p (t c i) -> p c t i", t=PACK, i=RUN),
-                gains[:, g, :].unsqueeze(1).unsqueeze(3).to_broadcast([P, width // RUN, PACK, RUN]),
-                ALU.mult,
-            )
-            h_rounded[g, start] = h
-
-        def apply_gain_turned(g, start, width):
-            h = ring.tile([P, PACK * width], BF16, name="h", align_bytes=64)
-            nc.vector.tensor_tensor(
-                h[:].rearrange("p (j t) -> p j t", t=PACK),
-                power[g, start].rearrange("p (j t) -> p j t", t=PACK),
-                gains[:, g, :].unsqueeze(1).to_broadcast([P, width, PACK]),
-                ALU.mult,
-            )
+            if is_upright(g, start):
+                nc.vector.tensor_tensor(
+                    h[:].rearrange("p (c i t) -> p c t i", i=RUN, t=PACK),
+                    power_of(g, start, width).rearrange("p (t c i) -> p c t i", t=PACK, i=RUN),
+                    gains[:, g, :].unsqueeze(1).unsqueeze(3).to_broadcast([P, width // RUN, PACK, RUN]),
+                    ALU.mult,
+                )
+            else:
+                nc.vector.tensor_tensor(
+                    h[:].rearrange("p (j t) -> p j t", t=PACK),
+                    power_of(g, start, width).rearrange("p (j t) -> p j t", t=PACK),
+                    gains[:, g, :].unsqueeze(1).to_broadcast([P, width, PACK]),
+                    ALU.mult,
+                )
             h_rounded[g, start] = h
 
         def quantize_h(g, start, width):
@@ -332,8 +364,8 @@ def tile_list_radar_log_power_kernel(tc, tab_words, tab_scales, offs, wi, wq_wor
         w2_codes = keep.tile([P, GROUPS * N], U32, name="w2_codes", align_bytes=64)
         w2_scales = keep.tile([P, GROUPS * N], U8, name="w2_scales", align_bytes=64)
 
-        def round_w2(g, copy):
-            copy(
+        def round_w2(g):
+            nc.vector.tensor_copy(
                 w2_grouped[:, g * PACK * N : (g + 1) * PACK * N].rearrange("p (c i j) -> p c j i", i=RUN, j=PACK),
                 w2_raw[g].rearrange("p (j c i) -> p c j i", j=PACK, i=RUN),
             )
@@ -370,31 +402,36 @@ def tile_list_radar_log_power_kernel(tc, tab_words, tab_scales, offs, wi, wq_wor
                 )
             nc.sync.dma_start(out_rows[:, :, start : start + width], result[:])
 
-        quadrature(0, True)
-        prepare_wi(0, 0)
-        prepare_wi(0, 1)
-        order = [(0, 0), (0, 1), (1, 0), (0, 2), (1, 1), (0, 3), (1, 2), (0, 4), (1, 3), (1, 4)]
+        first_quadrature()
+        for a in range(PASSES):
+            round_wi(0, a)
+            quantize_wi(0, a)
+        first = [(0, *unit) for unit in FIRST_UNITS]
+        second = [(1, *unit) for unit in SECOND_UNITS]
+        units = first[:2] + [second[0], first[2], second[1], first[3], second[2], first[4]] + second[3:]
         lag = 2
-        for step in range(len(order) + lag + 1):
-            if step == 1:
-                prepare_wi(1, 0)
+        done = 0
+        for step in range(len(units) + lag + 1):
+            if step in (1, 2):
+                round_wi(1, step - 1)
+                quantize_wi(1, step - 1)
             if step == 2:
-                prepare_wi(1, 1)
-                quadrature(1, False)
+                second_quadrature(0)
+                second_quadrature(1)
             if step == 3:
-                round_w2(0, nc.vector.tensor_copy)
-                round_w2(1, nc.vector.tensor_copy)
-            if step < len(order):
-                g, u = order[step]
-                (log_power_turned if (g, units[g][u][0] // BANK) in TURNED else log_power)(g, *units[g][u])
+                round_w2(0)
+                round_w2(1)
+            if step < len(units):
+                in_phase(*units[step])
+                log_power(*units[step])
             if step == 4:
                 quantize_w2(0, 512)
                 quantize_w2(512, 256)
-            if 0 <= step - lag < len(order):
-                g, u = order[step - lag]
-                (apply_gain_turned if (g, units[g][u][0] // BANK) in TURNED else apply_gain)(g, *units[g][u])
+            if 0 <= step - lag < len(units):
+                apply_gain(*units[step - lag])
             if 0 <= step - lag - 1:
-                g, u = order[step - lag - 1]
-                quantize_h(g, *units[g][u])
+                g, start, width = units[step - lag - 1]
+                quantize_h(g, start, width)
                 if g == 1:
-                    features(*units[g][u], nc.vector.tensor_copy if u < VECTOR_COPIES else nc.scalar.copy)
+                    features(start, width, nc.vector.tensor_copy if done < VECTOR_COPIES else nc.scalar.copy)
+                    done += 1

@@ -50,23 +50,23 @@ def tile_list_radar_log_power_kernel(tc, tab_words, tab_scales, offs, wi, wq_wor
         w2_at = GROUPS * PASSES * piece
         raw_columns = w2_at + GROUPS * PACK * N
         table0_at = 0
-        raw_at = table0_at + 4 * T - 64
+        raw_at = table0_at + 4 * T - 256
         table1_at = raw_at + 4 * raw_columns
         table1_end = table1_at + 4 * T
 
         wq_rows = wq_words.rearrange("a p c -> p a c").bitcast(I32)
         wq_raw = [
-            keep.tile([P, PASSES, K_PASS // 2], I32, name="wq_raw0", align_bytes=64),
-            staging.tile([P, PASSES, K_PASS // 2], I32, name="wq_raw1", offset=table1_end, align_bytes=64),
+            keep.tile([P, PASSES, K_PASS // 2], I32, name="wq_raw0", align_bytes=256),
+            staging.tile([P, PASSES, K_PASS // 2], I32, name="wq_raw1", offset=table1_end, align_bytes=256),
         ]
 
-        seed = staging.tile([P, 1], F32, name="seed", offset=table0_at, align_bytes=64)
+        seed = staging.tile([P, 1], F32, name="seed", offset=table0_at, align_bytes=256)
         nc.vector.memset(seed[:], 0.0)
 
-        scale_window = staging.tile([P, T // 4], I32, name="scale_window", offset=table1_end - 64, align_bytes=64)
+        scale_window = staging.tile([P, T // 4], I32, name="scale_window", offset=table1_end - 256, align_bytes=256)
         nc.sync.dma_start(scale_window[0:32, :], tab_scales.rearrange("a q t -> (a q) t").bitcast(I32))
         nc.sync.dma_start(wq_raw[0][:], wq_rows[:, :, : K_PASS // 2])
-        wq_scales_raw = keep.tile([P, PASSES, H // 4], I32, name="wq_scales_raw", align_bytes=64)
+        wq_scales_raw = keep.tile([P, PASSES, H // 4], I32, name="wq_scales_raw", align_bytes=256)
         nc.vector.memset(wq_scales_raw[:], 0)
         for quad in range(4):
             nc.sync.dma_start(
@@ -77,20 +77,20 @@ def tile_list_radar_log_power_kernel(tc, tab_words, tab_scales, offs, wi, wq_wor
         nc.vector.tensor_scalar_add(one[:], seed[:], 1.0)
         nc.vector.memset(scale_window[32:64, :], 0)
         nc.vector.memset(scale_window[64:P, :], 0)
-        table0 = staging.tile([P, T], I32, name="table0", offset=table0_at, align_bytes=64)
+        table0 = staging.tile([P, T], I32, name="table0", offset=table0_at, align_bytes=256)
         nc.sync.dma_start(table0[:], tab_words[0].rearrange("p t i -> p (t i)").bitcast(I32))
 
         identity = keep.tile([P, P], F32, name="identity")
         make_identity(nc, identity[:])
         zero = keep.tile([P, 1], F32, name="zero")
         nc.scalar.activation(zero[:], one[:], ACT.Ln)
-        gain_rows = keep.tile([P, P], F32, name="gain_rows")
+        gain_rows = keep.tile([P, P], F32, name="gain_rows", align_bytes=256)
         nc.vector.memset(gain_rows[:], 0.0)
         nc.sync.dma_start(gain_rows[0:P:16, :], gain.rearrange("(g b c) -> b g c", g=GROUPS, c=P))
-        v_planes = keep.tile([P, PASSES * S // 4], I32, name="v_planes", align_bytes=64)
+        v_planes = keep.tile([P, PASSES * S // 4], I32, name="v_planes", align_bytes=256)
         nc.vector.memset(v_planes[:], 0)
 
-        picked_scales = keep.tile([P, S // 4], I32, name="picked_scales", align_bytes=64)
+        picked_scales = keep.tile([P, S // 4], I32, name="picked_scales", align_bytes=256)
         nc.vector.tensor_copy(picked_scales[:].bitcast(U8), scale_window[:].bitcast(U8).indirect(offsets[:]))
 
         def place_scales(a):
@@ -102,7 +102,7 @@ def tile_list_radar_log_power_kernel(tc, tab_words, tab_scales, offs, wi, wq_wor
                 )
 
         place_scales(0)
-        table1 = staging.tile([P, T], I32, name="table1", offset=table1_at, align_bytes=64)
+        table1 = staging.tile([P, T], I32, name="table1", offset=table1_at, align_bytes=256)
         nc.sync.dma_start(table1[:], tab_words[1].rearrange("p t i -> p (t i)").bitcast(I32))
         place_scales(1)
         nc.sync.dma_start(wq_raw[1][:], wq_rows[:, :, K_PASS // 2 :])
@@ -112,7 +112,7 @@ def tile_list_radar_log_power_kernel(tc, tab_words, tab_scales, offs, wi, wq_wor
             width = K_PASS // (2 if g == 0 else 1)
             return [slice(first, first + width) for first in range(0, K_PASS, width)]
 
-        raw = staging.tile([P, raw_columns], F32, name="raw", offset=raw_at, align_bytes=64)
+        raw = staging.tile([P, raw_columns], F32, name="raw", offset=raw_at, align_bytes=256)
         wi_raw = {}
         for g in range(GROUPS):
             for a in range(PASSES):
@@ -129,7 +129,7 @@ def tile_list_radar_log_power_kernel(tc, tab_words, tab_scales, offs, wi, wq_wor
             for t in range(PACK):
                 nc.sync.dma_start(w2_raw[g][:, t * N : (t + 1) * N], rows[t])
 
-        v_codes = [keep.tile([P, S], U32, name=f"v_codes{a}", align_bytes=64) for a in range(PASSES)]
+        v_codes = [keep.tile([P, S], U32, name=f"v_codes{a}", align_bytes=256) for a in range(PASSES)]
 
         def gather_words(a, table):
             for half in range(HALVES):
@@ -149,12 +149,12 @@ def tile_list_radar_log_power_kernel(tc, tab_words, tab_scales, offs, wi, wq_wor
                 wq_codes[g] = [wq_raw[g][:, a, :].bitcast(U8) for a in range(PASSES)]
                 wq_planes[g] = [wq_scales_raw[:, a, g * P : (g + 1) * P].bitcast(U8) for a in range(PASSES)]
                 return
-            planes = keep.tile([P, PASSES, K_PASS // 4], I32, name=f"wq_planes{g}", align_bytes=64)
+            planes = keep.tile([P, PASSES, K_PASS // 4], I32, name=f"wq_planes{g}", align_bytes=256)
             nc.vector.tensor_copy(
                 planes[:].rearrange("p a (t s) -> p a t s", t=PACK),
                 wq_scales_raw[:, :, g * P : (g + 1) * P].rearrange("p a (s t) -> p a t s", t=PACK),
             )
-            codes = keep.tile([P, PASSES, K_PASS // 2], I32, name=f"wq_codes{g}", align_bytes=64)
+            codes = keep.tile([P, PASSES, K_PASS // 2], I32, name=f"wq_codes{g}", align_bytes=256)
             nc.vector.tensor_copy(
                 codes[:].rearrange("p a (t s w) -> p a t s w", t=PACK, w=2),
                 wq_raw[g][:].rearrange("p a (s t w) -> p a t s w", t=PACK, w=2),
@@ -164,12 +164,12 @@ def tile_list_radar_log_power_kernel(tc, tab_words, tab_scales, offs, wi, wq_wor
 
         sort_wq(0)
         gather_words(0, table0)
-        gain_sorted = keep.tile([P, P], F32, name="gain_sorted", align_bytes=64)
+        gain_sorted = keep.tile([P, P], F32, name="gain_sorted", align_bytes=256)
         nc.vector.tensor_copy(
             gain_sorted[:].rearrange("p (t s i) -> p t s i", t=PACK, i=RUN),
             gain_rows[:].rearrange("p (s t i) -> p t s i", t=PACK, i=RUN),
         )
-        gain_turned = keep.tile([P, P], F32, name="gain_turned", align_bytes=64)
+        gain_turned = keep.tile([P, P], F32, name="gain_turned", align_bytes=256)
         nc.vector.transpose(gain_turned[:], gain_sorted[:])
         gains = keep.tile([P, GROUPS, PACK], F32, name="gains")
         nc.vector.tensor_copy(gains[:], gain_turned[:].rearrange("p (t g x) -> p g t x", t=PACK, g=GROUPS)[:, :, :, 0])
@@ -257,7 +257,7 @@ def tile_list_radar_log_power_kernel(tc, tab_words, tab_scales, offs, wi, wq_wor
         wi_scales = {}
 
         def round_wi(g, a):
-            grouped = ring.tile([P, piece], BF16, name="grouped", align_bytes=64)
+            grouped = ring.tile([P, piece], BF16, name="grouped", align_bytes=256)
             for cols in pieces(g):
                 nc.vector.tensor_copy(
                     grouped[:].rearrange("p (t s i j) -> p t s j i", t=PACK, i=RUN, j=PACK)[
@@ -268,8 +268,8 @@ def tile_list_radar_log_power_kernel(tc, tab_words, tab_scales, offs, wi, wq_wor
             wi_grouped[g, a] = grouped
 
         def quantize_wi(g, a):
-            wi_codes[g, a] = keep.tile([P, K_PASS], U32, name=f"wi_codes{g}_{a}", align_bytes=64)
-            wi_scales[g, a] = keep.tile([P, K_PASS], U8, name=f"wi_scales{g}_{a}", align_bytes=64)
+            wi_codes[g, a] = keep.tile([P, K_PASS], U32, name=f"wi_codes{g}_{a}", align_bytes=256)
+            wi_scales[g, a] = keep.tile([P, K_PASS], U8, name=f"wi_scales{g}_{a}", align_bytes=256)
             nc.vector.quantize_mx(
                 out=wi_codes[g, a][:].bitcast(FP8X4), scales=wi_scales[g, a][:], in_=wi_grouped[g, a][:]
             )
@@ -331,12 +331,12 @@ def tile_list_radar_log_power_kernel(tc, tab_words, tab_scales, offs, wi, wq_wor
                     bias=1.0,
                 )
 
-        h_codes = [keep.tile([P, S], U32, name=f"h_codes{g}", align_bytes=64) for g in range(GROUPS)]
-        h_scales = [keep.tile([P, S], U8, name=f"h_scales{g}", align_bytes=64) for g in range(GROUPS)]
+        h_codes = [keep.tile([P, S], U32, name=f"h_codes{g}", align_bytes=256) for g in range(GROUPS)]
+        h_scales = [keep.tile([P, S], U8, name=f"h_scales{g}", align_bytes=256) for g in range(GROUPS)]
         h_rounded = {}
 
         def apply_gain(g, start, width):
-            h = ring.tile([P, PACK * width], BF16, name="h", align_bytes=64)
+            h = ring.tile([P, PACK * width], BF16, name="h", align_bytes=256)
             if is_upright(g, start):
                 nc.vector.tensor_tensor(
                     h[:].rearrange("p (c i t) -> p c t i", i=RUN, t=PACK),
@@ -360,9 +360,9 @@ def tile_list_radar_log_power_kernel(tc, tab_words, tab_scales, offs, wi, wq_wor
                 in_=h_rounded[g, start][:],
             )
 
-        w2_grouped = keep.tile([P, GROUPS * PACK * N], BF16, name="w2_grouped", align_bytes=64)
-        w2_codes = keep.tile([P, GROUPS * N], U32, name="w2_codes", align_bytes=64)
-        w2_scales = keep.tile([P, GROUPS * N], U8, name="w2_scales", align_bytes=64)
+        w2_grouped = keep.tile([P, GROUPS * PACK * N], BF16, name="w2_grouped", align_bytes=256)
+        w2_codes = keep.tile([P, GROUPS * N], U32, name="w2_codes", align_bytes=256)
+        w2_scales = keep.tile([P, GROUPS * N], U8, name="w2_scales", align_bytes=256)
 
         def round_w2(g):
             nc.vector.tensor_copy(
@@ -380,7 +380,7 @@ def tile_list_radar_log_power_kernel(tc, tab_words, tab_scales, offs, wi, wq_wor
         out_rows = out.rearrange("(c p) j -> p c j", p=P)
 
         def features(start, width, copy):
-            result = ring.tile([P, N_TILES, width], F32, name="result")
+            result = ring.tile([P, N_TILES, width], F32, name="result", align_bytes=256)
             per_bank = BANK // width
             for first in range(0, N_TILES, per_bank):
                 last = min(first + per_bank, N_TILES)

@@ -32,7 +32,7 @@ FIRST_UNITS = ((0, 256), (256, 256), (512, 256), (768, 128), (896, 128))
 SECOND_UNITS = ((0, 256), (256, 256), (512, 256), (768, 128), (896, 128))
 UPRIGHT = ((0, 0), (0, 1))
 UNITS = (FIRST_UNITS, SECOND_UNITS)
-VECTOR_COPIES = 2
+VECTOR_COPIES = 1
 
 
 def tile_list_radar_log_power_kernel(tc, tab_words, tab_scales, offs, wi, wq_words, wq_scales, gain, w2, out):
@@ -57,14 +57,14 @@ def tile_list_radar_log_power_kernel(tc, tab_words, tab_scales, offs, wi, wq_wor
         wq_rows = wq_words.rearrange("a p c -> p a c").bitcast(I32)
         wq_raw = [
             keep.tile([P, PASSES, K_PASS // 2], I32, name="wq_raw0", align_bytes=256),
-            staging.tile([P, PASSES, K_PASS // 2], I32, name="wq_raw1", offset=table1_end, align_bytes=256),
+            staging.tile([P, PASSES, K_PASS // 2], I32, name="wq_raw1", offset=table0_at, align_bytes=256),
         ]
 
         seed = staging.tile([P, 1], F32, name="seed", offset=table0_at, align_bytes=256)
         nc.vector.memset(seed[:], 0.0)
 
         scale_window = staging.tile([P, T // 4], I32, name="scale_window", offset=table1_end - 256, align_bytes=256)
-        nc.sync.dma_start(scale_window[0:32, :], tab_scales.rearrange("a q t -> (a q) t").bitcast(I32))
+        nc.sync.dma_start(scale_window[96:P, :], tab_scales.rearrange("a q t -> (a q) t").bitcast(I32))
         nc.sync.dma_start(wq_raw[0][:], wq_rows[:, :, : K_PASS // 2])
         wq_scales_raw = keep.tile([P, PASSES, H // 4], I32, name="wq_scales_raw", align_bytes=256)
         nc.vector.memset(wq_scales_raw[:], 0)
@@ -75,8 +75,7 @@ def tile_list_radar_log_power_kernel(tc, tab_words, tab_scales, offs, wi, wq_wor
             )
         one = keep.tile([P, 1], F32, name="one")
         nc.vector.tensor_scalar_add(one[:], seed[:], 1.0)
-        nc.vector.memset(scale_window[32:64, :], 0)
-        nc.vector.memset(scale_window[64:P, :], 0)
+        nc.vector.memset(scale_window[0:96, :], 0)
         table0 = staging.tile([P, T], I32, name="table0", offset=table0_at, align_bytes=256)
         nc.sync.dma_start(table0[:], tab_words[0].rearrange("p t i -> p (t i)").bitcast(I32))
 
@@ -95,7 +94,7 @@ def tile_list_radar_log_power_kernel(tc, tab_words, tab_scales, offs, wi, wq_wor
 
         def place_scales(a):
             for quad in range(4):
-                first = 16 * a + 4 * quad
+                first = 96 + 16 * a + 4 * quad
                 nc.sync.dma_start(
                     v_planes[32 * quad : 32 * quad + 4, a * S // 4 : (a + 1) * S // 4],
                     picked_scales[first : first + 4, :],
@@ -105,16 +104,17 @@ def tile_list_radar_log_power_kernel(tc, tab_words, tab_scales, offs, wi, wq_wor
         table1 = staging.tile([P, T], I32, name="table1", offset=table1_at, align_bytes=256)
         nc.sync.dma_start(table1[:], tab_words[1].rearrange("p t i -> p (t i)").bitcast(I32))
         place_scales(1)
-        nc.sync.dma_start(wq_raw[1][:], wq_rows[:, :, K_PASS // 2 :])
         v_scales = v_planes[:].bitcast(U8)
 
         def pieces(g):
-            width = K_PASS // (2 if g == 0 else 1)
+            width = K_PASS
             return [slice(first, first + width) for first in range(0, K_PASS, width)]
 
         raw = staging.tile([P, raw_columns], F32, name="raw", offset=raw_at, align_bytes=256)
         wi_raw = {}
         for g in range(GROUPS):
+            if g == 1:
+                nc.sync.dma_start(wq_raw[1][:], wq_rows[:, :, K_PASS // 2 :])
             for a in range(PASSES):
                 at = (g * PASSES + a) * piece
                 wi_raw[g, a] = raw[:, at : at + piece].rearrange("p (j c) -> p j c", j=PACK)
@@ -381,9 +381,12 @@ def tile_list_radar_log_power_kernel(tc, tab_words, tab_scales, offs, wi, wq_wor
 
         def features(start, width, copy):
             result = ring.tile([P, N_TILES, width], F32, name="result", align_bytes=256)
-            per_bank = BANK // width
+            is_last = start + width == S
+            per_bank = 1 if is_last else BANK // width
             for first in range(0, N_TILES, per_bank):
                 last = min(first + per_bank, N_TILES)
+                if is_last:
+                    copy = nc.vector.tensor_copy if first == 1 else nc.scalar.copy
                 bank = psum.tile([P, BANK], F32, name="bank")
                 for c in range(first, last):
                     for g in range(GROUPS):

@@ -31,8 +31,89 @@ SPANS = K_PASS // SPAN
 FIRST_UNITS = ((0, 256), (256, 256), (512, 256), (768, 128), (896, 128))
 SECOND_UNITS = ((0, 256), (256, 256), (512, 256), (768, 128), (896, 128))
 UPRIGHT = ((0, 0), (0, 1))
-UNITS = (FIRST_UNITS, SECOND_UNITS)
-VECTOR_COPIES = 1
+UNITS = (((0, 256), (256, 256), (512, 256), (768, 256)), ((0, 256), (256, 256), (512, 256), (768, 128), (896, 128)))
+RING = 5
+PSUM_GAINS = False
+EARLY_BANKS = 8
+EARLY_VECTOR = ()
+LATE_FIRST = False
+PLAN = (
+    ('rw', 0, 0, 'V', 1),
+    ('qw', 0, 0),
+    ('rw', 0, 1, 'V', 1),
+    ('qw', 0, 1),
+    ('rw', 1, 0, 'V', 1),
+    ('qw', 1, 0),
+    ('rw', 1, 1, 'V', 1),
+    ('qw', 1, 1),
+    ('a', 0, 0, 256),
+    ('a', 0, 256, 256),
+    ('s', 0, 0, 256, 'V'),
+    ('l', 0, 0, 256),
+    ('b', 1, 0, 0, 'A'),
+    ('b', 1, 0, 1, 'A'),
+    ('b', 1, 0, 2, 'A'),
+    ('b', 1, 0, 3, 'A'),
+    ('a', 0, 512, 256),
+    ('s', 0, 256, 256, 'V'),
+    ('l', 0, 256, 256),
+    ('a', 1, 0, 256),
+    ('s', 0, 512, 256, 'V'),
+    ('l', 0, 512, 256),
+    ('g', 0, 0, 256),
+    ('r2', 0, 'V', 1),
+    ('r2', 1, 'V', 1),
+    ('a', 1, 256, 256),
+    ('s', 1, 0, 256, 'V'),
+    ('l', 1, 0, 256),
+    ('g', 0, 256, 256),
+    ('q', 0, 0, 256),
+    ('b', 1, 1, 0, 'A'),
+    ('b', 1, 1, 1, 'A'),
+    ('b', 1, 1, 2, 'A'),
+    ('b', 1, 1, 3, 'A'),
+    ('a', 0, 768, 256),
+    ('s', 1, 256, 256, 'V'),
+    ('l', 1, 256, 256),
+    ('q2', 0, 512),
+    ('q2', 512, 256),
+    ('g', 0, 512, 256),
+    ('q', 0, 256, 256),
+    ('a', 1, 512, 256),
+    ('s', 0, 768, 256, 'V'),
+    ('l', 0, 768, 256),
+    ('g', 1, 0, 256),
+    ('q', 0, 512, 256),
+    ('a', 1, 768, 128),
+    ('s', 1, 512, 256, 'V'),
+    ('l', 1, 512, 256),
+    ('g', 1, 256, 256),
+    ('q', 1, 0, 256),
+    ('f', 0, 256, 2),
+    ('a', 1, 896, 128),
+    ('s', 1, 768, 128, 'V'),
+    ('l', 1, 768, 128),
+    ('g', 0, 768, 256),
+    ('q', 1, 256, 256),
+    ('f', 256, 256, 2),
+    ('c', 0, 256, 'VVV'),
+    ('s', 1, 896, 128, 'V'),
+    ('l', 1, 896, 128),
+    ('g', 1, 512, 256),
+    ('q', 0, 768, 256),
+    ('c', 256, 256, 'AAA'),
+    ('g', 1, 768, 128),
+    ('q', 1, 512, 256),
+    ('f', 512, 256, 2),
+    ('g', 1, 896, 128),
+    ('q', 1, 768, 128),
+    ('f', 768, 128, 4),
+    ('c', 512, 256, 'AAA'),
+    ('q', 1, 896, 128),
+    ('f', 896, 128, 1),
+    ('c', 768, 128, 'AAA'),
+    ('c', 896, 128, 'AVA'),
+)
 
 
 def tile_list_radar_log_power_kernel(tc, tab_words, tab_scales, offs, wi, wq_words, wq_scales, gain, w2, out):
@@ -40,8 +121,9 @@ def tile_list_radar_log_power_kernel(tc, tab_words, tab_scales, offs, wi, wq_wor
     with ExitStack() as ctx:
         keep = ctx.enter_context(tc.tile_pool(name="keep", bufs=1))
         staging = ctx.enter_context(tc.tile_pool(name="staging", bufs=1))
-        ring = ctx.enter_context(tc.tile_pool(name="ring", bufs=3))
-        psum = ctx.enter_context(tc.psum_pool(name="psum", bufs=8))
+        ring = ctx.enter_context(tc.tile_pool(name="ring", bufs=RING))
+        psum = ctx.enter_context(tc.psum_pool(name="psum", bufs=7 if PSUM_GAINS else 8))
+        psum_keep = ctx.enter_context(tc.psum_pool(name="psum_keep", bufs=1))
 
         offsets = keep.tile([P, S // 16], U16, name="offsets")
         nc.sync.dma_start(offsets[:], offs)
@@ -83,9 +165,12 @@ def tile_list_radar_log_power_kernel(tc, tab_words, tab_scales, offs, wi, wq_wor
         make_identity(nc, identity[:])
         zero = keep.tile([P, 1], F32, name="zero")
         nc.scalar.activation(zero[:], one[:], ACT.Ln)
-        gain_rows = keep.tile([P, P], F32, name="gain_rows", align_bytes=256)
+        gain_rows = keep.tile([P, K_PASS if PSUM_GAINS else P], F32, name="gain_rows", align_bytes=256)
         nc.vector.memset(gain_rows[:], 0.0)
-        nc.sync.dma_start(gain_rows[0:P:16, :], gain.rearrange("(g b c) -> b g c", g=GROUPS, c=P))
+        if PSUM_GAINS:
+            nc.sync.dma_start(gain_rows[0:GROUPS, :], gain.rearrange("(g c) -> g c", g=GROUPS))
+        else:
+            nc.sync.dma_start(gain_rows[0:P:16, :], gain.rearrange("(g b c) -> b g c", g=GROUPS, c=P))
         v_planes = keep.tile([P, PASSES * S // 4], I32, name="v_planes", align_bytes=256)
         nc.vector.memset(v_planes[:], 0)
 
@@ -164,15 +249,24 @@ def tile_list_radar_log_power_kernel(tc, tab_words, tab_scales, offs, wi, wq_wor
 
         sort_wq(0)
         gather_words(0, table0)
-        gain_sorted = keep.tile([P, P], F32, name="gain_sorted", align_bytes=256)
+        gain_sorted = keep.tile([P, K_PASS if PSUM_GAINS else P], F32, name="gain_sorted", align_bytes=256)
         nc.vector.tensor_copy(
             gain_sorted[:].rearrange("p (t s i) -> p t s i", t=PACK, i=RUN),
             gain_rows[:].rearrange("p (s t i) -> p t s i", t=PACK, i=RUN),
         )
-        gain_turned = keep.tile([P, P], F32, name="gain_turned", align_bytes=256)
-        nc.vector.transpose(gain_turned[:], gain_sorted[:])
-        gains = keep.tile([P, GROUPS, PACK], F32, name="gains")
-        nc.vector.tensor_copy(gains[:], gain_turned[:].rearrange("p (t g x) -> p g t x", t=PACK, g=GROUPS)[:, :, :, 0])
+        if PSUM_GAINS:
+            gain_bank = psum_keep.tile([P, BANK], F32, name="gain_bank")
+            for t in range(PACK):
+                nc.tensor.transpose(gain_bank[:, t * P : (t + 1) * P], gain_sorted[:, t * P : (t + 1) * P], identity[:])
+            gains = gain_bank[:].rearrange("p (t r) -> p r t", t=PACK)
+        else:
+            gain_turned = keep.tile([P, P], F32, name="gain_turned", align_bytes=256)
+            nc.vector.transpose(gain_turned[:], gain_sorted[:])
+            gain_tile = keep.tile([P, GROUPS, PACK], F32, name="gains")
+            nc.vector.tensor_copy(
+                gain_tile[:], gain_turned[:].rearrange("p (t g x) -> p g t x", t=PACK, g=GROUPS)[:, :, :, 0]
+            )
+            gains = gain_tile[:]
         gather_words(1, table1)
         sort_wq(1)
 
@@ -213,57 +307,65 @@ def tile_list_radar_log_power_kernel(tc, tab_words, tab_scales, offs, wi, wq_wor
             else:
                 cells_pass(bank, half * BANK + k * P, a, wq_codes[g][a].bitcast(FP4X4), wq_planes[g][a])
 
-        def quadrature_square(bank, g, half, k):
+        def square(out_view, bank, view, engine):
+            if engine == "A":
+                nc.scalar.activation(out_view, view(bank[:]), ACT.Square, bias=zero[:])
+            else:
+                twin = ring.tile([P, BANK], F32, name="twin")
+                nc.vector.tensor_copy(twin[:], bank[:])
+                nc.vector.tensor_tensor(out_view, view(bank[:]), view(twin[:]), ALU.mult)
+
+        def quadrature_square(bank, g, half, k, engine):
             if (g, half) in UPRIGHT:
                 widths = [width for start, width in sorted(UNITS[g]) if start // BANK == half]
                 at = 0
                 for width in sorted(set(widths), reverse=True):
                     span = width * widths.count(width)
-                    nc.scalar.activation(
+                    square(
                         power_of(g, half * BANK + at, span).rearrange("p (u t j) -> p u t j", t=PACK, j=width)[:, :, k, :],
-                        bank[:, at : at + span].rearrange("p (u j) -> p u j", j=width),
-                        ACT.Square,
-                        bias=zero[:],
+                        bank,
+                        lambda x: x[:, at : at + span].rearrange("p (u j) -> p u j", j=width),
+                        engine,
                     )
                     at += span
             elif is_sorted(g):
-                nc.scalar.activation(power_of(g, half * BANK + k * P, P), bank[:], ACT.Square, bias=zero[:])
+                square(power_of(g, half * BANK + k * P, P), bank, lambda x: x, engine)
             else:
-                nc.scalar.activation(
+                square(
                     power_of(g, half * BANK + k * P, P).rearrange("p (t s i) -> p t s i", t=PACK, i=RUN),
-                    bank[:].rearrange("p (s t i) -> p t s i", t=PACK, i=RUN),
-                    ACT.Square,
-                    bias=zero[:],
+                    bank,
+                    lambda x: x.rearrange("p (s t i) -> p t s i", t=PACK, i=RUN),
+                    engine,
                 )
 
         def first_quadrature():
-            slots = [(half, k) for half in range(HALVES) for k in range(PACK)]
+            slots = [(half, k) for half in range(HALVES) for k in range(PACK)][:EARLY_BANKS]
             banks = [psum.tile([P, BANK], F32, name="bank") for slot in slots]
             for a in range(PASSES):
                 for bank, (half, k) in zip(banks, slots):
                     quadrature_pass(bank, 0, half, k, a)
                     if a == PASSES - 1:
-                        quadrature_square(bank, 0, half, k)
+                        quadrature_square(bank, 0, half, k, "V" if (half, k) in EARLY_VECTOR else "A")
 
-        def second_quadrature(half):
-            for k in range(PACK):
-                bank = psum.tile([P, BANK], F32, name="bank")
-                for a in range(PASSES):
-                    quadrature_pass(bank, 1, half, k, a)
-                quadrature_square(bank, 1, half, k)
+        def late_quadrature(g, half, k, engine):
+            bank = psum.tile([P, BANK], F32, name="bank")
+            for a in range(PASSES):
+                quadrature_pass(bank, g, half, k, a)
+            quadrature_square(bank, g, half, k, engine)
 
         wi_grouped = {}
         wi_codes = {}
         wi_scales = {}
 
-        def round_wi(g, a):
+        engines = {"V": nc.vector, "G": nc.gpsimd}
+
+        def round_wi(g, a, engine, parts):
             grouped = ring.tile([P, piece], BF16, name="grouped", align_bytes=256)
-            for cols in pieces(g):
-                nc.vector.tensor_copy(
-                    grouped[:].rearrange("p (t s i j) -> p t s j i", t=PACK, i=RUN, j=PACK)[
-                        :, :, cols.start // SPAN : cols.stop // SPAN
-                    ],
-                    wi_raw[g, a][:, :, cols].rearrange("p j (s t i) -> p t s j i", t=PACK, i=RUN),
+            for first in range(0, PACK, PACK // parts):
+                last = first + PACK // parts
+                engines[engine].tensor_copy(
+                    grouped[:].rearrange("p (t s i j) -> p t s j i", t=PACK, i=RUN, j=PACK)[:, first:last],
+                    wi_raw[g, a].rearrange("p j (s t i) -> p t s j i", t=PACK, i=RUN)[:, first:last],
                 )
             wi_grouped[g, a] = grouped
 
@@ -305,17 +407,19 @@ def tile_list_radar_log_power_kernel(tc, tab_words, tab_scales, offs, wi, wq_wor
                         squares[g, start][:, f * BANK : (f + 1) * BANK], bank[:], ACT.Square, bias=zero[:]
                     )
 
-        def log_power(g, start, width):
+        sums = {}
+
+        def add_squares(g, start, width, engine):
             total = power_of(g, start, width)
             if is_upright(g, start):
-                nc.vector.tensor_tensor(total, squares[g, start][:], total, ALU.add)
-                nc.scalar.activation(total, total, ACT.Ln, bias=1.0)
+                engines[engine].tensor_tensor(total, squares[g, start][:], total, ALU.add)
                 return
             for f in range(width // P):
                 bank = psum.tile([P, BANK], F32, name="bank")
+                sums[g, start + f * P] = bank
                 for t in range(PACK):
                     cols = slice(f * BANK + t * P, f * BANK + (t + 1) * P)
-                    for n, term in enumerate((total, squares[g, start])):
+                    for n, term in enumerate((squares[g, start], total) if LATE_FIRST else (total, squares[g, start])):
                         nc.tensor.matmul(
                             bank[:, t * P : (t + 1) * P],
                             term[:, cols],
@@ -324,9 +428,16 @@ def tile_list_radar_log_power_kernel(tc, tab_words, tab_scales, offs, wi, wq_wor
                             stop=(n == 1),
                             is_transpose=True,
                         )
+
+        def take_log(g, start, width):
+            total = power_of(g, start, width)
+            if is_upright(g, start):
+                nc.scalar.activation(total, total, ACT.Ln, bias=1.0)
+                return
+            for f in range(width // P):
                 nc.scalar.activation(
                     total[:, f * BANK : (f + 1) * BANK].rearrange("p (j t) -> p j t", t=PACK),
-                    bank[:].rearrange("p (t j) -> p j t", t=PACK),
+                    sums[g, start + f * P][:].rearrange("p (t j) -> p j t", t=PACK),
                     ACT.Ln,
                     bias=1.0,
                 )
@@ -364,11 +475,15 @@ def tile_list_radar_log_power_kernel(tc, tab_words, tab_scales, offs, wi, wq_wor
         w2_codes = keep.tile([P, GROUPS * N], U32, name="w2_codes", align_bytes=256)
         w2_scales = keep.tile([P, GROUPS * N], U8, name="w2_scales", align_bytes=256)
 
-        def round_w2(g):
-            nc.vector.tensor_copy(
-                w2_grouped[:, g * PACK * N : (g + 1) * PACK * N].rearrange("p (c i j) -> p c j i", i=RUN, j=PACK),
-                w2_raw[g].rearrange("p (j c i) -> p c j i", j=PACK, i=RUN),
-            )
+        def round_w2(g, engine, parts):
+            runs = N // RUN // parts
+            for first in range(0, N // RUN, runs):
+                engines[engine].tensor_copy(
+                    w2_grouped[:, g * PACK * N : (g + 1) * PACK * N].rearrange("p (c i j) -> p c j i", i=RUN, j=PACK)[
+                        :, first : first + runs
+                    ],
+                    w2_raw[g].rearrange("p (j c i) -> p c j i", j=PACK, i=RUN)[:, first : first + runs],
+                )
 
         def quantize_w2(first, count):
             nc.vector.quantize_mx(
@@ -379,17 +494,17 @@ def tile_list_radar_log_power_kernel(tc, tab_words, tab_scales, offs, wi, wq_wor
 
         out_rows = out.rearrange("(c p) j -> p c j", p=P)
 
-        def features(start, width, copy):
-            result = ring.tile([P, N_TILES, width], F32, name="result", align_bytes=256)
-            is_last = start + width == S
-            per_bank = 1 if is_last else BANK // width
+        feature_banks = {}
+
+        def features(start, width, per_bank):
+            feature_banks[start] = []
+            order = list(reversed(range(GROUPS))) if LATE_FIRST else list(range(GROUPS))
             for first in range(0, N_TILES, per_bank):
                 last = min(first + per_bank, N_TILES)
-                if is_last:
-                    copy = nc.vector.tensor_copy if first == 1 else nc.scalar.copy
                 bank = psum.tile([P, BANK], F32, name="bank")
+                feature_banks[start].append((first, last, bank))
                 for c in range(first, last):
-                    for g in range(GROUPS):
+                    for g in order:
                         col = g * N + c * P
                         nc.tensor.matmul_mx(
                             out=bank[:, (c - first) * width : (c - first + 1) * width],
@@ -397,44 +512,21 @@ def tile_list_radar_log_power_kernel(tc, tab_words, tab_scales, offs, wi, wq_wor
                             lhsT_scale=w2_scales[:, col : col + P],
                             rhs=h_codes[g][:, start : start + width].bitcast(FP8X4),
                             rhs_scale=h_scales[g][:, start : start + width],
-                            start=(g == 0),
-                            stop=(g == GROUPS - 1),
+                            start=(g == order[0]),
+                            stop=(g == order[-1]),
                         )
-                copy(
-                    result[:, first:last, :].rearrange("p c j -> p (c j)"), bank[:, : (last - first) * width]
-                )
+
+        def copy_features(start, width, who):
+            result = ring.tile([P, N_TILES, width], F32, name="result", align_bytes=256)
+            for (first, last, bank), engine in zip(feature_banks[start], who):
+                copy = nc.vector.tensor_copy if engine == "V" else nc.scalar.copy
+                copy(result[:, first:last, :].rearrange("p c j -> p (c j)"), bank[:, : (last - first) * width])
             nc.sync.dma_start(out_rows[:, :, start : start + width], result[:])
 
         first_quadrature()
-        for a in range(PASSES):
-            round_wi(0, a)
-            quantize_wi(0, a)
-        first = [(0, *unit) for unit in FIRST_UNITS]
-        second = [(1, *unit) for unit in SECOND_UNITS]
-        units = first[:2] + [second[0], first[2], second[1], first[3], second[2], first[4]] + second[3:]
-        lag = 2
-        done = 0
-        for step in range(len(units) + lag + 1):
-            if step in (1, 2):
-                round_wi(1, step - 1)
-                quantize_wi(1, step - 1)
-            if step == 2:
-                second_quadrature(0)
-                second_quadrature(1)
-            if step == 3:
-                round_w2(0)
-                round_w2(1)
-            if step < len(units):
-                in_phase(*units[step])
-                log_power(*units[step])
-            if step == 4:
-                quantize_w2(0, 512)
-                quantize_w2(512, 256)
-            if 0 <= step - lag < len(units):
-                apply_gain(*units[step - lag])
-            if 0 <= step - lag - 1:
-                g, start, width = units[step - lag - 1]
-                quantize_h(g, start, width)
-                if g == 1:
-                    features(start, width, nc.vector.tensor_copy if done < VECTOR_COPIES else nc.scalar.copy)
-                    done += 1
+        actions = {
+            "rw": round_wi, "qw": quantize_wi, "b": late_quadrature, "a": in_phase, "s": add_squares, "l": take_log,
+            "g": apply_gain, "q": quantize_h, "r2": round_w2, "q2": quantize_w2, "f": features, "c": copy_features,
+        }
+        for item in PLAN:
+            actions[item[0]](*item[1:])

@@ -307,9 +307,11 @@ def tile_list_radar_log_power_kernel(tc, tab_words, tab_scales, offs, wi, wq_wor
             else:
                 cells_pass(bank, half * BANK + k * P, a, wq_codes[g][a].bitcast(FP4X4), wq_planes[g][a])
 
+        pointer_bias = [zero[:]]
+
         def square(out_view, bank, view, engine):
             if engine == "A":
-                nc.scalar.activation(out_view, view(bank[:]), ACT.Square, bias=zero[:])
+                nc.scalar.activation(out_view, view(bank[:]), ACT.Square, bias=pointer_bias.pop() if pointer_bias else 0.0)
             else:
                 twin = ring.tile([P, BANK], F32, name="twin")
                 nc.vector.tensor_copy(twin[:], bank[:])
@@ -396,7 +398,7 @@ def tile_list_radar_log_power_kernel(tc, tab_words, tab_scales, offs, wi, wq_wor
                                 stop=(a == PASSES - 1),
                             )
                     nc.scalar.activation(
-                        squares[g, start][:, first * width : first * width + BANK], bank[:], ACT.Square, bias=zero[:]
+                        squares[g, start][:, first * width : first * width + BANK], bank[:], ACT.Square, bias=0.0
                     )
             else:
                 for f in range(width // P):
@@ -404,7 +406,7 @@ def tile_list_radar_log_power_kernel(tc, tab_words, tab_scales, offs, wi, wq_wor
                     for a in range(PASSES):
                         cells_pass(bank, start + f * P, a, wi_codes[g, a][:].bitcast(FP8X4), wi_scales[g, a][:])
                     nc.scalar.activation(
-                        squares[g, start][:, f * BANK : (f + 1) * BANK], bank[:], ACT.Square, bias=zero[:]
+                        squares[g, start][:, f * BANK : (f + 1) * BANK], bank[:], ACT.Square, bias=0.0
                     )
 
         sums = {}

@@ -32,10 +32,11 @@ FIRST_UNITS = ((0, 256), (256, 256), (512, 256), (768, 128), (896, 128))
 SECOND_UNITS = ((0, 256), (256, 256), (512, 256), (768, 128), (896, 128))
 UPRIGHT = ((0, 0), (0, 1))
 UNITS = (((0, 256), (256, 256), (512, 256), (768, 256)), ((0, 256), (256, 256), (512, 256), (768, 128), (896, 128)))
-RING = 5
+LOADS = (('wi', 0, 0), ('wq',), ('wi', 0, 1), ('wi', 1, 0), ('wi', 1, 1), ('w2', 0), ('w2', 1))
+RING = 4
 PSUM_GAINS = False
 EARLY_BANKS = 8
-EARLY_VECTOR = ()
+EARLY_VECTOR = ((1, 1),)
 LATE_FIRST = False
 PLAN = (
     ('rw', 0, 0, 'V', 1),
@@ -44,75 +45,75 @@ PLAN = (
     ('qw', 0, 1),
     ('rw', 1, 0, 'V', 1),
     ('qw', 1, 0),
-    ('rw', 1, 1, 'V', 1),
-    ('qw', 1, 1),
-    ('a', 0, 0, 256),
-    ('a', 0, 256, 256),
-    ('s', 0, 0, 256, 'V'),
-    ('l', 0, 0, 256),
     ('b', 1, 0, 0, 'A'),
     ('b', 1, 0, 1, 'A'),
     ('b', 1, 0, 2, 'A'),
-    ('b', 1, 0, 3, 'A'),
-    ('a', 0, 512, 256),
-    ('s', 0, 256, 256, 'V'),
-    ('l', 0, 256, 256),
-    ('a', 1, 0, 256),
-    ('s', 0, 512, 256, 'V'),
-    ('l', 0, 512, 256),
-    ('g', 0, 0, 256),
-    ('r2', 0, 'V', 1),
-    ('r2', 1, 'V', 1),
-    ('a', 1, 256, 256),
-    ('s', 1, 0, 256, 'V'),
-    ('l', 1, 0, 256),
-    ('g', 0, 256, 256),
-    ('q', 0, 0, 256),
+    ('b', 1, 0, 3, 'V'),
+    ('a', 0, 0, 256),
+    ('rw', 1, 1, 'V', 1),
+    ('qw', 1, 1),
     ('b', 1, 1, 0, 'A'),
     ('b', 1, 1, 1, 'A'),
     ('b', 1, 1, 2, 'A'),
     ('b', 1, 1, 3, 'A'),
-    ('a', 0, 768, 256),
-    ('s', 1, 256, 256, 'V'),
-    ('l', 1, 256, 256),
+    ('a', 0, 256, 256),
+    ('a', 0, 512, 256),
+    ('s', 0, 0, 256, 'V'),
+    ('l', 0, 0, 256),
+    ('a', 1, 0, 256),
+    ('s', 0, 256, 256, 'V'),
+    ('l', 0, 256, 256),
+    ('r2', 0, 'V', 1),
+    ('r2', 1, 'V', 1),
+    ('a', 1, 256, 256),
+    ('s', 0, 512, 256, 'V'),
+    ('l', 0, 512, 256),
+    ('g', 0, 0, 256),
+    ('a', 1, 512, 256),
+    ('s', 1, 0, 256, 'V'),
+    ('l', 1, 0, 256),
     ('q2', 0, 512),
     ('q2', 512, 256),
+    ('g', 0, 256, 256),
+    ('q', 0, 0, 256),
+    ('a', 1, 768, 128),
+    ('s', 1, 256, 256, 'V'),
+    ('l', 1, 256, 256),
     ('g', 0, 512, 256),
     ('q', 0, 256, 256),
-    ('a', 1, 512, 256),
-    ('s', 0, 768, 256, 'V'),
-    ('l', 0, 768, 256),
-    ('g', 1, 0, 256),
-    ('q', 0, 512, 256),
-    ('a', 1, 768, 128),
+    ('a', 0, 768, 256),
     ('s', 1, 512, 256, 'V'),
     ('l', 1, 512, 256),
-    ('g', 1, 256, 256),
-    ('q', 1, 0, 256),
-    ('f', 0, 256, 2),
+    ('g', 1, 0, 256),
+    ('q', 0, 512, 256),
     ('a', 1, 896, 128),
     ('s', 1, 768, 128, 'V'),
     ('l', 1, 768, 128),
-    ('g', 0, 768, 256),
+    ('g', 1, 256, 256),
+    ('q', 1, 0, 256),
+    ('f', 0, 256, 2),
+    ('s', 0, 768, 256, 'V'),
+    ('l', 0, 768, 256),
+    ('g', 1, 512, 256),
     ('q', 1, 256, 256),
     ('f', 256, 256, 2),
-    ('c', 0, 256, 'VVV'),
+    ('c', 0, 256, 'AAA'),
     ('s', 1, 896, 128, 'V'),
     ('l', 1, 896, 128),
-    ('g', 1, 512, 256),
-    ('q', 0, 768, 256),
-    ('c', 256, 256, 'AAA'),
     ('g', 1, 768, 128),
     ('q', 1, 512, 256),
     ('f', 512, 256, 2),
-    ('g', 1, 896, 128),
+    ('c', 256, 256, 'AAA'),
+    ('g', 0, 768, 256),
     ('q', 1, 768, 128),
-    ('f', 768, 128, 4),
     ('c', 512, 256, 'AAA'),
+    ('g', 1, 896, 128),
+    ('q', 0, 768, 256),
+    ('f', 768, 128, 4),
     ('q', 1, 896, 128),
     ('f', 896, 128, 1),
     ('c', 768, 128, 'AAA'),
-    ('c', 896, 128, 'AVA'),
+    ('cs', 896, 128, 'AVA'),
 )
 
 
@@ -191,28 +192,30 @@ def tile_list_radar_log_power_kernel(tc, tab_words, tab_scales, offs, wi, wq_wor
         place_scales(1)
         v_scales = v_planes[:].bitcast(U8)
 
-        def pieces(g):
-            width = K_PASS
-            return [slice(first, first + width) for first in range(0, K_PASS, width)]
-
         raw = staging.tile([P, raw_columns], F32, name="raw", offset=raw_at, align_bytes=256)
         wi_raw = {}
-        for g in range(GROUPS):
-            if g == 1:
-                nc.sync.dma_start(wq_raw[1][:], wq_rows[:, :, K_PASS // 2 :])
-            for a in range(PASSES):
-                at = (g * PASSES + a) * piece
-                wi_raw[g, a] = raw[:, at : at + piece].rearrange("p (j c) -> p j c", j=PACK)
-                rows = wi[a * K_PASS : (a + 1) * K_PASS, g * K_PASS : (g + 1) * K_PASS]
-                for cols in pieces(g):
-                    nc.sync.dma_start(wi_raw[g, a][:, :, cols], rows.rearrange("(p j) c -> p j c", j=PACK)[:, :, cols])
-        w2_raw = []
-        for g in range(GROUPS):
+        w2_raw = {}
+
+        def load_wi(g, a):
+            at = (g * PASSES + a) * piece
+            wi_raw[g, a] = raw[:, at : at + piece].rearrange("p (j c) -> p j c", j=PACK)
+            rows = wi[a * K_PASS : (a + 1) * K_PASS, g * K_PASS : (g + 1) * K_PASS]
+            nc.sync.dma_start(wi_raw[g, a], rows.rearrange("(p j) c -> p j c", j=PACK))
+
+        def load_w2(g):
             at = w2_at + g * PACK * N
-            w2_raw.append(raw[:, at : at + PACK * N])
+            w2_raw[g] = raw[:, at : at + PACK * N]
             rows = w2[g * K_PASS : (g + 1) * K_PASS, :].rearrange("(s t i) n -> t s i n", t=PACK, i=RUN)
             for t in range(PACK):
                 nc.sync.dma_start(w2_raw[g][:, t * N : (t + 1) * N], rows[t])
+
+        for item in LOADS:
+            if item[0] == "wi":
+                load_wi(item[1], item[2])
+            elif item[0] == "w2":
+                load_w2(item[1])
+            else:
+                nc.sync.dma_start(wq_raw[1][:], wq_rows[:, :, K_PASS // 2 :])
 
         v_codes = [keep.tile([P, S], U32, name=f"v_codes{a}", align_bytes=256) for a in range(PASSES)]
 
@@ -444,6 +447,15 @@ def tile_list_radar_log_power_kernel(tc, tab_words, tab_scales, offs, wi, wq_wor
                     bias=1.0,
                 )
 
+        def take_log_part(g, start, width):
+            at = start % P
+            nc.scalar.activation(
+                power_of(g, start, width).rearrange("p (j t) -> p j t", t=PACK),
+                sums[g, start - at][:].rearrange("p (t j) -> p j t", t=PACK)[:, at : at + width],
+                ACT.Ln,
+                bias=1.0,
+            )
+
         h_codes = [keep.tile([P, S], U32, name=f"h_codes{g}", align_bytes=256) for g in range(GROUPS)]
         h_scales = [keep.tile([P, S], U8, name=f"h_scales{g}", align_bytes=256) for g in range(GROUPS)]
         h_rounded = {}
@@ -525,10 +537,18 @@ def tile_list_radar_log_power_kernel(tc, tab_words, tab_scales, offs, wi, wq_wor
                 copy(result[:, first:last, :].rearrange("p c j -> p (c j)"), bank[:, : (last - first) * width])
             nc.sync.dma_start(out_rows[:, :, start : start + width], result[:])
 
+        def copy_and_store(start, width, who):
+            for (first, last, bank), engine in zip(feature_banks[start], who):
+                result = ring.tile([P, last - first, width], F32, name="piece", align_bytes=256)
+                copy = nc.vector.tensor_copy if engine == "V" else nc.scalar.copy
+                copy(result[:].rearrange("p c j -> p (c j)"), bank[:, : (last - first) * width])
+                nc.sync.dma_start(out_rows[:, first:last, start : start + width], result[:])
+
         first_quadrature()
         actions = {
             "rw": round_wi, "qw": quantize_wi, "b": late_quadrature, "a": in_phase, "s": add_squares, "l": take_log,
             "g": apply_gain, "q": quantize_h, "r2": round_w2, "q2": quantize_w2, "f": features, "c": copy_features,
+            "lp": take_log_part, "cs": copy_and_store,
         }
         for item in PLAN:
             actions[item[0]](*item[1:])

@@ -36,22 +36,22 @@ LOADS = (('wi', 0, 0), ('wq',), ('wi', 0, 1), ('wi', 1, 0), ('wi', 1, 1), ('w2',
 RING = 4
 PSUM_GAINS = False
 EARLY_BANKS = 8
-EARLY_VECTOR = ((1, 1),)
+EARLY_VECTOR = ((1, 2),)
 LATE_FIRST = False
 PLAN = (
     ('rw', 0, 0, 'V', 1),
     ('qw', 0, 0),
     ('rw', 0, 1, 'V', 1),
     ('qw', 0, 1),
+    ('a', 0, 0, 256),
     ('rw', 1, 0, 'V', 1),
     ('qw', 1, 0),
+    ('rw', 1, 1, 'V', 1),
+    ('qw', 1, 1),
     ('b', 1, 0, 0, 'A'),
     ('b', 1, 0, 1, 'A'),
     ('b', 1, 0, 2, 'A'),
     ('b', 1, 0, 3, 'V'),
-    ('a', 0, 0, 256),
-    ('rw', 1, 1, 'V', 1),
-    ('qw', 1, 1),
     ('b', 1, 1, 0, 'A'),
     ('b', 1, 1, 1, 'A'),
     ('b', 1, 1, 2, 'A'),
@@ -68,12 +68,12 @@ PLAN = (
     ('a', 1, 256, 256),
     ('s', 0, 512, 256, 'V'),
     ('l', 0, 512, 256),
+    ('q2', 0, 512),
+    ('q2', 512, 256),
     ('g', 0, 0, 256),
     ('a', 1, 512, 256),
     ('s', 1, 0, 256, 'V'),
     ('l', 1, 0, 256),
-    ('q2', 0, 512),
-    ('q2', 512, 256),
     ('g', 0, 256, 256),
     ('q', 0, 0, 256),
     ('a', 1, 768, 128),
@@ -97,19 +97,19 @@ PLAN = (
     ('g', 1, 512, 256),
     ('q', 1, 256, 256),
     ('f', 256, 256, 2),
-    ('c', 0, 256, 'AAA'),
     ('s', 1, 896, 128, 'V'),
     ('l', 1, 896, 128),
     ('g', 1, 768, 128),
     ('q', 1, 512, 256),
     ('f', 512, 256, 2),
-    ('c', 256, 256, 'AAA'),
+    ('c', 0, 256, 'AAA'),
     ('g', 0, 768, 256),
     ('q', 1, 768, 128),
-    ('c', 512, 256, 'AAA'),
+    ('c', 256, 256, 'AAA'),
     ('g', 1, 896, 128),
     ('q', 0, 768, 256),
     ('f', 768, 128, 4),
+    ('c', 512, 256, 'AAA'),
     ('q', 1, 896, 128),
     ('f', 896, 128, 1),
     ('c', 768, 128, 'AAA'),

@@ -122,9 +122,28 @@ def tile_list_radar_log_power_kernel(tc, tab_words, tab_scales, offs, wi, wq_wor
     with ExitStack() as ctx:
         keep = ctx.enter_context(tc.tile_pool(name="keep", bufs=1))
         staging = ctx.enter_context(tc.tile_pool(name="staging", bufs=1))
-        ring = ctx.enter_context(tc.tile_pool(name="ring", bufs=RING))
-        psum = ctx.enter_context(tc.psum_pool(name="psum", bufs=7 if PSUM_GAINS else 8))
+        ring = ctx.enter_context(tc.tile_pool(name="ring", bufs=1))
+        psum = ctx.enter_context(tc.psum_pool(name="psum", bufs=1))
         psum_keep = ctx.enter_context(tc.psum_pool(name="psum_keep", bufs=1))
+
+        made = {"bank": 0}
+        room = {"grouped": 4096, "squares": 4096, "h": 2048, "result": 3072, "twin": 2048, "piece": 512}
+        depth = {"grouped": RING, "squares": RING, "h": RING, "result": RING, "twin": 2, "piece": 3}
+        starts = {}
+        for kind in room:
+            starts[kind] = sum(room[other] * depth[other] for other in starts)
+            made[kind] = 0
+
+        def next_bank():
+            n = made["bank"]
+            made["bank"] = n + 1
+            return psum.tile([P, BANK], F32, name=f"bank{n}", offset=4 * BANK * (n % (7 if PSUM_GAINS else 8)))
+
+        def stream(kind, shape, dtype):
+            n = made[kind]
+            made[kind] = n + 1
+            at = starts[kind] + room[kind] * (n % depth[kind])
+            return ring.tile(shape, dtype, name=f"{kind}{n}", offset=at, align_bytes=256)
 
         offsets = keep.tile([P, S // 16], U16, name="offsets")
         nc.sync.dma_start(offsets[:], offs)
@@ -316,7 +335,7 @@ def tile_list_radar_log_power_kernel(tc, tab_words, tab_scales, offs, wi, wq_wor
             if engine == "A":
                 nc.scalar.activation(out_view, view(bank[:]), ACT.Square, bias=pointer_bias.pop() if pointer_bias else 0.0)
             else:
-                twin = ring.tile([P, BANK], F32, name="twin")
+                twin = stream("twin", [P, BANK], F32)
                 nc.vector.tensor_copy(twin[:], bank[:])
                 nc.vector.tensor_tensor(out_view, view(bank[:]), view(twin[:]), ALU.mult)
 
@@ -345,7 +364,7 @@ def tile_list_radar_log_power_kernel(tc, tab_words, tab_scales, offs, wi, wq_wor
 
         def first_quadrature():
             slots = [(half, k) for half in range(HALVES) for k in range(PACK)][:EARLY_BANKS]
-            banks = [psum.tile([P, BANK], F32, name="bank") for slot in slots]
+            banks = [next_bank() for slot in slots]
             for a in range(PASSES):
                 for bank, (half, k) in zip(banks, slots):
                     quadrature_pass(bank, 0, half, k, a)
@@ -353,7 +372,7 @@ def tile_list_radar_log_power_kernel(tc, tab_words, tab_scales, offs, wi, wq_wor
                         quadrature_square(bank, 0, half, k, "V" if (half, k) in EARLY_VECTOR else "A")
 
         def late_quadrature(g, half, k, engine):
-            bank = psum.tile([P, BANK], F32, name="bank")
+            bank = next_bank()
             for a in range(PASSES):
                 quadrature_pass(bank, g, half, k, a)
             quadrature_square(bank, g, half, k, engine)
@@ -365,7 +384,7 @@ def tile_list_radar_log_power_kernel(tc, tab_words, tab_scales, offs, wi, wq_wor
         engines = {"V": nc.vector, "G": nc.gpsimd}
 
         def round_wi(g, a, engine, parts):
-            grouped = ring.tile([P, piece], BF16, name="grouped", align_bytes=256)
+            grouped = stream("grouped", [P, piece], BF16)
             for first in range(0, PACK, PACK // parts):
                 last = first + PACK // parts
                 engines[engine].tensor_copy(
@@ -384,11 +403,11 @@ def tile_list_radar_log_power_kernel(tc, tab_words, tab_scales, offs, wi, wq_wor
         squares = {}
 
         def in_phase(g, start, width):
-            squares[g, start] = ring.tile([P, PACK * width], F32, name="squares")
+            squares[g, start] = stream("squares", [P, PACK * width], F32)
             if is_upright(g, start):
                 per_bank = BANK // width
                 for first in range(0, PACK, per_bank):
-                    bank = psum.tile([P, BANK], F32, name="bank")
+                    bank = next_bank()
                     for t in range(first, first + per_bank):
                         for a in range(PASSES):
                             nc.tensor.matmul_mx(
@@ -405,7 +424,7 @@ def tile_list_radar_log_power_kernel(tc, tab_words, tab_scales, offs, wi, wq_wor
                     )
             else:
                 for f in range(width // P):
-                    bank = psum.tile([P, BANK], F32, name="bank")
+                    bank = next_bank()
                     for a in range(PASSES):
                         cells_pass(bank, start + f * P, a, wi_codes[g, a][:].bitcast(FP8X4), wi_scales[g, a][:])
                     nc.scalar.activation(
@@ -420,7 +439,7 @@ def tile_list_radar_log_power_kernel(tc, tab_words, tab_scales, offs, wi, wq_wor
                 engines[engine].tensor_tensor(total, squares[g, start][:], total, ALU.add)
                 return
             for f in range(width // P):
-                bank = psum.tile([P, BANK], F32, name="bank")
+                bank = next_bank()
                 sums[g, start + f * P] = bank
                 for t in range(PACK):
                     cols = slice(f * BANK + t * P, f * BANK + (t + 1) * P)
@@ -461,7 +480,7 @@ def tile_list_radar_log_power_kernel(tc, tab_words, tab_scales, offs, wi, wq_wor
         h_rounded = {}
 
         def apply_gain(g, start, width):
-            h = ring.tile([P, PACK * width], BF16, name="h", align_bytes=256)
+            h = stream("h", [P, PACK * width], BF16)
             if is_upright(g, start):
                 nc.vector.tensor_tensor(
                     h[:].rearrange("p (c i t) -> p c t i", i=RUN, t=PACK),
@@ -515,7 +534,7 @@ def tile_list_radar_log_power_kernel(tc, tab_words, tab_scales, offs, wi, wq_wor
             order = list(reversed(range(GROUPS))) if LATE_FIRST else list(range(GROUPS))
             for first in range(0, N_TILES, per_bank):
                 last = min(first + per_bank, N_TILES)
-                bank = psum.tile([P, BANK], F32, name="bank")
+                bank = next_bank()
                 feature_banks[start].append((first, last, bank))
                 for c in range(first, last):
                     for g in order:
@@ -531,7 +550,7 @@ def tile_list_radar_log_power_kernel(tc, tab_words, tab_scales, offs, wi, wq_wor
                         )
 
         def copy_features(start, width, who):
-            result = ring.tile([P, N_TILES, width], F32, name="result", align_bytes=256)
+            result = stream("result", [P, N_TILES, width], F32)
             for (first, last, bank), engine in zip(feature_banks[start], who):
                 copy = nc.vector.tensor_copy if engine == "V" else nc.scalar.copy
                 copy(result[:, first:last, :].rearrange("p c j -> p (c j)"), bank[:, : (last - first) * width])
@@ -539,7 +558,7 @@ def tile_list_radar_log_power_kernel(tc, tab_words, tab_scales, offs, wi, wq_wor
 
         def copy_and_store(start, width, who):
             for (first, last, bank), engine in zip(feature_banks[start], who):
-                result = ring.tile([P, last - first, width], F32, name="piece", align_bytes=256)
+                result = stream("piece", [P, last - first, width], F32)
                 copy = nc.vector.tensor_copy if engine == "V" else nc.scalar.copy
                 copy(result[:].rearrange("p c j -> p (c j)"), bank[:, : (last - first) * width])
                 nc.sync.dma_start(out_rows[:, first:last, start : start + width], result[:])

@@ -28,93 +28,24 @@ N_TILES = N // P
 RUN = 4
 SPAN = PACK * RUN
 SPANS = K_PASS // SPAN
-FIRST_UNITS = ((0, 256), (256, 256), (512, 256), (768, 128), (896, 128))
-SECOND_UNITS = ((0, 256), (256, 256), (512, 256), (768, 128), (896, 128))
 UPRIGHT = ((0, 0), (0, 1))
 UNITS = (((0, 256), (256, 256), (512, 256), (768, 256)), ((0, 256), (256, 256), (512, 256), (768, 128), (896, 128)))
+ORDER = ((0, 0), (0, 1), (1, 0), (1, 1), (0, 2), (1, 2), (0, 3), (1, 3), (1, 4))
+ADDERS = {}
+COPIERS = ("AA", "AA", "AA", "A", "AVA")
 LOADS = (('wi', 0, 0), ('wq',), ('wi', 0, 1), ('wi', 1, 0), ('wi', 1, 1), ('w2', 0), ('w2', 1))
 RING = 4
 PSUM_GAINS = False
 EARLY_BANKS = 8
-EARLY_VECTOR = ((1, 2),)
+VECTOR_BANKS = ((0, 1, 2), (1, 0, 3))
 LATE_FIRST = False
-PLAN = (
-    ('rw', 0, 0, 'V', 1),
-    ('qw', 0, 0),
-    ('rw', 0, 1, 'V', 1),
-    ('qw', 0, 1),
-    ('a', 0, 0, 256),
-    ('rw', 1, 0, 'V', 1),
-    ('qw', 1, 0),
-    ('rw', 1, 1, 'V', 1),
-    ('qw', 1, 1),
-    ('b', 1, 0, 0, 'A'),
-    ('b', 1, 0, 1, 'A'),
-    ('b', 1, 0, 2, 'A'),
-    ('b', 1, 0, 3, 'V'),
-    ('b', 1, 1, 0, 'A'),
-    ('b', 1, 1, 1, 'A'),
-    ('b', 1, 1, 2, 'A'),
-    ('b', 1, 1, 3, 'A'),
-    ('a', 0, 256, 256),
-    ('a', 0, 512, 256),
-    ('s', 0, 0, 256, 'V'),
-    ('l', 0, 0, 256),
-    ('a', 1, 0, 256),
-    ('s', 0, 256, 256, 'V'),
-    ('l', 0, 256, 256),
-    ('r2', 0, 'V', 1),
-    ('r2', 1, 'V', 1),
-    ('a', 1, 256, 256),
-    ('s', 0, 512, 256, 'V'),
-    ('l', 0, 512, 256),
-    ('q2', 0, 512),
-    ('q2', 512, 256),
-    ('g', 0, 0, 256),
-    ('a', 1, 512, 256),
-    ('s', 1, 0, 256, 'V'),
-    ('l', 1, 0, 256),
-    ('g', 0, 256, 256),
-    ('q', 0, 0, 256),
-    ('a', 1, 768, 128),
-    ('s', 1, 256, 256, 'V'),
-    ('l', 1, 256, 256),
-    ('g', 0, 512, 256),
-    ('q', 0, 256, 256),
-    ('a', 0, 768, 256),
-    ('s', 1, 512, 256, 'V'),
-    ('l', 1, 512, 256),
-    ('g', 1, 0, 256),
-    ('q', 0, 512, 256),
-    ('a', 1, 896, 128),
-    ('s', 1, 768, 128, 'V'),
-    ('l', 1, 768, 128),
-    ('g', 1, 256, 256),
-    ('q', 1, 0, 256),
-    ('f', 0, 256, 2),
-    ('s', 0, 768, 256, 'V'),
-    ('l', 0, 768, 256),
-    ('g', 1, 512, 256),
-    ('q', 1, 256, 256),
-    ('f', 256, 256, 2),
-    ('s', 1, 896, 128, 'V'),
-    ('l', 1, 896, 128),
-    ('g', 1, 768, 128),
-    ('q', 1, 512, 256),
-    ('f', 512, 256, 2),
-    ('c', 0, 256, 'AAA'),
-    ('g', 0, 768, 256),
-    ('q', 1, 768, 128),
-    ('c', 256, 256, 'AAA'),
-    ('g', 1, 896, 128),
-    ('q', 0, 768, 256),
-    ('f', 768, 128, 4),
-    ('c', 512, 256, 'AAA'),
-    ('q', 1, 896, 128),
-    ('f', 896, 128, 1),
-    ('c', 768, 128, 'AAA'),
-    ('cs', 896, 128, 'AVA'),
-)
+LAG = 2
+GAIN_LAG = 4
+QUANT_LAG = 5
+COPY_LAG = 1
+W2_STEP = 4
+LATE_STEP = 1
+WI_STEP = 0
 
 
 def tile_list_radar_log_power_kernel(tc, tab_words, tab_scales, offs, wi, wq_words, wq_scales, gain, w2, out):
@@ -279,8 +210,8 @@ def tile_list_radar_log_power_kernel(tc, tab_words, tab_scales, offs, wi, wq_wor
         if PSUM_GAINS:
             gain_bank = psum_keep.tile([P, BANK], F32, name="gain_bank")
             for t in range(PACK):
-                nc.tensor.transpose(gain_bank[:, t * P : (t + 1) * P], gain_sorted[:, t * P : (t + 1) * P], identity[:])
-            gains = gain_bank[:].rearrange("p (t r) -> p r t", t=PACK)
+                nc.tensor.transpose(gain_bank[:, t::PACK], gain_sorted[:, t * P : (t + 1) * P], identity[:])
+            gains = gain_bank[:].rearrange("p (r t) -> p r t", t=PACK)
         else:
             gain_turned = keep.tile([P, P], F32, name="gain_turned", align_bytes=256)
             nc.vector.transpose(gain_turned[:], gain_sorted[:])
@@ -290,7 +221,6 @@ def tile_list_radar_log_power_kernel(tc, tab_words, tab_scales, offs, wi, wq_wor
             )
             gains = gain_tile[:]
         gather_words(1, table1)
-        sort_wq(1)
 
         power = {}
         for g in range(GROUPS):
@@ -369,7 +299,7 @@ def tile_list_radar_log_power_kernel(tc, tab_words, tab_scales, offs, wi, wq_wor
                 for bank, (half, k) in zip(banks, slots):
                     quadrature_pass(bank, 0, half, k, a)
                     if a == PASSES - 1:
-                        quadrature_square(bank, 0, half, k, "V" if (half, k) in EARLY_VECTOR else "A")
+                        quadrature_square(bank, 0, half, k, "V" if (0, half, k) in VECTOR_BANKS else "A")
 
         def late_quadrature(g, half, k, engine):
             bank = next_bank()
@@ -564,10 +494,51 @@ def tile_list_radar_log_power_kernel(tc, tab_words, tab_scales, offs, wi, wq_wor
                 nc.sync.dma_start(out_rows[:, first:last, start : start + width], result[:])
 
         first_quadrature()
-        actions = {
-            "rw": round_wi, "qw": quantize_wi, "b": late_quadrature, "a": in_phase, "s": add_squares, "l": take_log,
-            "g": apply_gain, "q": quantize_h, "r2": round_w2, "q2": quantize_w2, "f": features, "c": copy_features,
-            "lp": take_log_part, "cs": copy_and_store,
-        }
-        for item in PLAN:
-            actions[item[0]](*item[1:])
+        for a in range(PASSES):
+            round_wi(0, a, "V", 1)
+            quantize_wi(0, a)
+            if a == 0:
+                sort_wq(1)
+
+        order = [(g,) + UNITS[g][u] for g, u in ORDER]
+        done = set()
+        ready = []
+        last = len(order) - 1
+        for step in range(len(order) + QUANT_LAG + COPY_LAG + 1):
+            if step == LATE_STEP:
+                slots = [(g, half, k) for g in range(GROUPS) for half in range(HALVES) for k in range(PACK)]
+                for slot in slots[EARLY_BANKS:]:
+                    late_quadrature(*slot, "V" if slot in VECTOR_BANKS else "A")
+            if step <= last:
+                in_phase(*order[step])
+            if step == WI_STEP:
+                for a in range(PASSES):
+                    round_wi(1, a, "V", 1)
+                    quantize_wi(1, a)
+            if 0 <= step - LAG <= last:
+                add_squares(*order[step - LAG], ADDERS.get(ORDER[step - LAG], "V"))
+                take_log(*order[step - LAG])
+            if step == W2_STEP:
+                for g in range(GROUPS):
+                    round_w2(g, "V", 1)
+                quantize_w2(0, BANK)
+                quantize_w2(BANK, GROUPS * N - BANK)
+            if 0 <= step - GAIN_LAG <= last:
+                apply_gain(*order[step - GAIN_LAG])
+            for start, width, at in ready:
+                if at + COPY_LAG == step:
+                    who = COPIERS[[s for s, w in UNITS[1]].index(start)]
+                    if start + width == S:
+                        copy_and_store(start, width, who)
+                    else:
+                        copy_features(start, width, who)
+            if 0 <= step - QUANT_LAG <= last:
+                g, start, width = order[step - QUANT_LAG]
+                quantize_h(g, start, width)
+                for cell in range(start, start + width, P):
+                    done.add((g, cell))
+                for start, width in UNITS[1]:
+                    complete = all((g, cell) in done for g in range(GROUPS) for cell in range(start, start + width, P))
+                    if complete and start not in feature_banks:
+                        features(start, width, 1 if start + width == S else BANK // width)
+                        ready.append((start, width, step))

@@ -97,7 +97,7 @@ def tile_list_radar_log_power_kernel(tc, tab_words, tab_scales, offs, wi, wq_wor
         nc.vector.memset(seed[:], 0.0)
 
         scale_window = staging.tile([P, T // 4], I32, name="scale_window", offset=table1_end - 256, align_bytes=256)
-        nc.sync.dma_start(scale_window[96:P, :], tab_scales.rearrange("a q t -> (a q) t").bitcast(I32))
+        nc.sync.dma_start(scale_window[96:P, :], tab_scales.rearrange("a q t -> q a t").bitcast(I32))
         nc.sync.dma_start(wq_raw[0][:], wq_rows[:, :, : K_PASS // 2])
         wq_scales_raw = keep.tile([P, PASSES, H // 4], I32, name="wq_scales_raw", align_bytes=256)
         nc.vector.memset(wq_scales_raw[:], 0)
@@ -128,18 +128,10 @@ def tile_list_radar_log_power_kernel(tc, tab_words, tab_scales, offs, wi, wq_wor
         picked_scales = keep.tile([P, S // 4], I32, name="picked_scales", align_bytes=256)
         nc.vector.tensor_copy(picked_scales[:].bitcast(U8), scale_window[:].bitcast(U8).indirect(offsets[:]))
 
-        def place_scales(a):
-            for quad in range(4):
-                first = 96 + 16 * a + 4 * quad
-                nc.sync.dma_start(
-                    v_planes[32 * quad : 32 * quad + 4, a * S // 4 : (a + 1) * S // 4],
-                    picked_scales[first : first + 4, :],
-                )
-
-        place_scales(0)
+        for quad in range(4):
+            nc.sync.dma_start(v_planes[32 * quad : 32 * quad + 4, :], picked_scales[96 + 8 * quad : 104 + 8 * quad, :])
         table1 = staging.tile([P, T], I32, name="table1", offset=table1_at, align_bytes=256)
         nc.sync.dma_start(table1[:], tab_words[1].rearrange("p t i -> p (t i)").bitcast(I32))
-        place_scales(1)
         v_scales = v_planes[:].bitcast(U8)
 
         raw = staging.tile([P, raw_columns], F32, name="raw", offset=raw_at, align_bytes=256)
@@ -525,13 +517,6 @@ def tile_list_radar_log_power_kernel(tc, tab_words, tab_scales, offs, wi, wq_wor
                 quantize_w2(BANK, GROUPS * N - BANK)
             if 0 <= step - GAIN_LAG <= last:
                 apply_gain(*order[step - GAIN_LAG])
-            for start, width, at in ready:
-                if at + COPY_LAG == step:
-                    who = COPIERS[[s for s, w in UNITS[1]].index(start)]
-                    if start + width == S:
-                        copy_and_store(start, width, who)
-                    else:
-                        copy_features(start, width, who)
             if 0 <= step - QUANT_LAG <= last:
                 g, start, width = order[step - QUANT_LAG]
                 quantize_h(g, start, width)
@@ -542,3 +527,10 @@ def tile_list_radar_log_power_kernel(tc, tab_words, tab_scales, offs, wi, wq_wor
                     if complete and start not in feature_banks:
                         features(start, width, 1 if start + width == S else BANK // width)
                         ready.append((start, width, step))
+            for start, width, at in ready:
+                if at + COPY_LAG == step:
+                    who = COPIERS[[s for s, w in UNITS[1]].index(start)]
+                    if start + width == S:
+                        copy_and_store(start, width, who)
+                    else:
+                        copy_features(start, width, who)

@@ -32,16 +32,17 @@ UPRIGHT = ((0, 0), (0, 1))
 UNITS = (((0, 256), (256, 256), (512, 256), (768, 256)), ((0, 256), (256, 256), (512, 256), (768, 128), (896, 128)))
 ORDER = ((0, 0), (0, 1), (1, 0), (1, 1), (0, 2), (1, 2), (0, 3), (1, 3), (1, 4))
 ADDERS = {}
+FEATURES = ((0, 256), (256, 256), (512, 256), (768, 128), (896, 128))
 COPIERS = ("AA", "AA", "AA", "A", "AVA")
 LOADS = (('wi', 0, 0), ('wq',), ('wi', 0, 1), ('wi', 1, 0), ('wi', 1, 1), ('w2', 0), ('w2', 1))
 RING = 4
 PSUM_GAINS = False
 EARLY_BANKS = 8
-VECTOR_BANKS = ((0, 1, 2), (1, 0, 3))
+VECTOR_BANKS = ((0, 1, 2),)
 LATE_FIRST = False
-LAG = 2
-GAIN_LAG = 4
-QUANT_LAG = 5
+LAG = 3
+GAIN_LAG = 5
+QUANT_LAG = 6
 COPY_LAG = 1
 W2_STEP = 4
 LATE_STEP = 1
@@ -93,21 +94,18 @@ def tile_list_radar_log_power_kernel(tc, tab_words, tab_scales, offs, wi, wq_wor
             staging.tile([P, PASSES, K_PASS // 2], I32, name="wq_raw1", offset=table0_at, align_bytes=256),
         ]
 
-        seed = staging.tile([P, 1], F32, name="seed", offset=table0_at, align_bytes=256)
-        nc.vector.memset(seed[:], 0.0)
-
         scale_window = staging.tile([P, T // 4], I32, name="scale_window", offset=table1_end - 256, align_bytes=256)
         nc.sync.dma_start(scale_window[96:P, :], tab_scales.rearrange("a q t -> q a t").bitcast(I32))
         nc.sync.dma_start(wq_raw[0][:], wq_rows[:, :, : K_PASS // 2])
         wq_scales_raw = keep.tile([P, PASSES, H // 4], I32, name="wq_scales_raw", align_bytes=256)
-        nc.vector.memset(wq_scales_raw[:], 0)
+        nc.gpsimd.memset(wq_scales_raw[:], 0)
         for quad in range(4):
             nc.sync.dma_start(
                 wq_scales_raw[32 * quad : 32 * quad + 4, :, :],
                 wq_scales[:, 4 * quad : 4 * quad + 4, :].rearrange("a r c -> r a c").bitcast(I32),
             )
         one = keep.tile([P, 1], F32, name="one")
-        nc.vector.tensor_scalar_add(one[:], seed[:], 1.0)
+        nc.vector.memset(one[:], 1.0)
         nc.vector.memset(scale_window[0:96, :], 0)
         table0 = staging.tile([P, T], I32, name="table0", offset=table0_at, align_bytes=256)
         nc.sync.dma_start(table0[:], tab_words[0].rearrange("p t i -> p (t i)").bitcast(I32))
@@ -522,14 +520,14 @@ def tile_list_radar_log_power_kernel(tc, tab_words, tab_scales, offs, wi, wq_wor
                 quantize_h(g, start, width)
                 for cell in range(start, start + width, P):
                     done.add((g, cell))
-                for start, width in UNITS[1]:
+                for start, width in FEATURES:
                     complete = all((g, cell) in done for g in range(GROUPS) for cell in range(start, start + width, P))
                     if complete and start not in feature_banks:
                         features(start, width, 1 if start + width == S else BANK // width)
                         ready.append((start, width, step))
             for start, width, at in ready:
                 if at + COPY_LAG == step:
-                    who = COPIERS[[s for s, w in UNITS[1]].index(start)]
+                    who = COPIERS[[s for s, w in FEATURES].index(start)]
                     if start + width == S:
                         copy_and_store(start, width, who)
                     else:

@@ -402,9 +402,11 @@ def tile_list_radar_log_power_kernel(tc, tab_words, tab_scales, offs, wi, wq_wor
         def apply_gain(g, start, width):
             h = stream("h", [P, PACK * width], BF16)
             if is_upright(g, start):
+                whole = [unit for unit in UNITS[g] if unit[0] <= start < unit[0] + unit[1]][0]
+                first = (start - whole[0]) // RUN
                 nc.vector.tensor_tensor(
                     h[:].rearrange("p (c i t) -> p c t i", i=RUN, t=PACK),
-                    power_of(g, start, width).rearrange("p (t c i) -> p c t i", t=PACK, i=RUN),
+                    power_of(g, *whole).rearrange("p (t c i) -> p c t i", t=PACK, i=RUN)[:, first : first + width // RUN],
                     gains[:, g, :].unsqueeze(1).unsqueeze(3).to_broadcast([P, width // RUN, PACK, RUN]),
                     ALU.mult,
                 )
@@ -491,10 +493,11 @@ def tile_list_radar_log_power_kernel(tc, tab_words, tab_scales, offs, wi, wq_wor
                 sort_wq(1)
 
         order = [(g,) + UNITS[g][u] for g, u in ORDER]
+        closing = order[:-3] + [(g, start, P) for start in (S - 2 * P, S - P) for g in range(GROUPS)]
         done = set()
         ready = []
         last = len(order) - 1
-        for step in range(len(order) + QUANT_LAG + COPY_LAG + 1):
+        for step in range(len(closing) + QUANT_LAG + COPY_LAG + 1):
             if step == LATE_STEP:
                 slots = [(g, half, k) for g in range(GROUPS) for half in range(HALVES) for k in range(PACK)]
                 for slot in slots[EARLY_BANKS:]:
@@ -513,10 +516,10 @@ def tile_list_radar_log_power_kernel(tc, tab_words, tab_scales, offs, wi, wq_wor
                     round_w2(g, "V", 1)
                 quantize_w2(0, BANK)
                 quantize_w2(BANK, GROUPS * N - BANK)
-            if 0 <= step - GAIN_LAG <= last:
-                apply_gain(*order[step - GAIN_LAG])
-            if 0 <= step - QUANT_LAG <= last:
-                g, start, width = order[step - QUANT_LAG]
+            if 0 <= step - GAIN_LAG < len(closing):
+                apply_gain(*closing[step - GAIN_LAG])
+            if 0 <= step - QUANT_LAG < len(closing):
+                g, start, width = closing[step - QUANT_LAG]
                 quantize_h(g, start, width)
                 for cell in range(start, start + width, P):
                     done.add((g, cell))

@@ -38,7 +38,7 @@ LOADS = (('wi', 0, 0), ('wq',), ('wi', 0, 1), ('wi', 1, 0), ('wi', 1, 1), ('w2',
 RING = 4
 PSUM_GAINS = False
 EARLY_BANKS = 8
-VECTOR_BANKS = ((0, 1, 2),)
+VECTOR_BANKS = ((0, 1, 2), (1, 0, 3))
 LATE_FIRST = False
 LAG = 3
 GAIN_LAG = 5

@@ -43,7 +43,8 @@ LATE_FIRST = False
 LAG = 3
 GAIN_LAG = 5
 QUANT_LAG = 6
-COPY_LAG = 1
+COPY_LAG = 0
+FEATURE_LAG = {256: 1}
 W2_STEP = 4
 LATE_STEP = 1
 WI_STEP = 0
@@ -453,13 +454,11 @@ def tile_list_radar_log_power_kernel(tc, tab_words, tab_scales, offs, wi, wq_wor
 
         def features(start, width, per_bank):
             feature_banks[start] = []
-            order = list(reversed(range(GROUPS))) if LATE_FIRST else list(range(GROUPS))
             for first in range(0, N_TILES, per_bank):
-                last = min(first + per_bank, N_TILES)
-                bank = next_bank()
-                feature_banks[start].append((first, last, bank))
-                for c in range(first, last):
-                    for g in order:
+                feature_banks[start].append((first, min(first + per_bank, N_TILES), next_bank()))
+            for g in range(GROUPS):
+                for first, last, bank in feature_banks[start]:
+                    for c in range(first, last):
                         col = g * N + c * P
                         nc.tensor.matmul_mx(
                             out=bank[:, (c - first) * width : (c - first + 1) * width],
@@ -467,8 +466,8 @@ def tile_list_radar_log_power_kernel(tc, tab_words, tab_scales, offs, wi, wq_wor
                             lhsT_scale=w2_scales[:, col : col + P],
                             rhs=h_codes[g][:, start : start + width].bitcast(FP8X4),
                             rhs_scale=h_scales[g][:, start : start + width],
-                            start=(g == order[0]),
-                            stop=(g == order[-1]),
+                            start=(g == 0 and c == first),
+                            stop=(g == GROUPS - 1 and c == last - 1),
                         )
 
         def copy_features(start, width, who):
@@ -496,6 +495,7 @@ def tile_list_radar_log_power_kernel(tc, tab_words, tab_scales, offs, wi, wq_wor
         closing = order[:-3] + [(g, start, P) for start in (S - 2 * P, S - P) for g in range(GROUPS)]
         done = set()
         ready = []
+        closed = []
         last = len(order) - 1
         for step in range(len(closing) + QUANT_LAG + COPY_LAG + 1):
             if step == LATE_STEP:
@@ -525,9 +525,12 @@ def tile_list_radar_log_power_kernel(tc, tab_words, tab_scales, offs, wi, wq_wor
                     done.add((g, cell))
                 for start, width in FEATURES:
                     complete = all((g, cell) in done for g in range(GROUPS) for cell in range(start, start + width, P))
-                    if complete and start not in feature_banks:
-                        features(start, width, 1 if start + width == S else BANK // width)
-                        ready.append((start, width, step))
+                    if complete and start not in [s for s, w, at in closed]:
+                        closed.append((start, width, step))
+            for start, width, at in closed:
+                if at + FEATURE_LAG.get(start, 0) == step:
+                    features(start, width, 1 if start + width == S else BANK // width)
+                    ready.append((start, width, step))
             for start, width, at in ready:
                 if at + COPY_LAG == step:
                     who = COPIERS[[s for s, w in FEATURES].index(start)]

@@ -23,31 +23,22 @@ K_PASS = P * PACK
 PASSES = K // K_PASS
 GROUPS = H // K_PASS
 BANK = 512
+BANKS = 8
 HALVES = S // BANK
 N_TILES = N // P
 RUN = 4
-SPAN = PACK * RUN
-SPANS = K_PASS // SPAN
-UPRIGHT = ((0, 0), (0, 1))
-UNITS = (((0, 256), (256, 256), (512, 256), (768, 256)), ((0, 256), (256, 256), (512, 256), (768, 128), (896, 128)))
-ORDER = ((0, 0), (0, 1), (1, 0), (1, 1), (0, 2), (1, 2), (0, 3), (1, 3), (1, 4))
-ADDERS = {}
-FEATURES = ((0, 256), (256, 256), (512, 256), (768, 128), (896, 128))
-COPIERS = ("AA", "AA", "AA", "A", "AVA")
-LOADS = (('wi', 0, 0), ('wq',), ('wi', 0, 1), ('wi', 1, 0), ('wi', 1, 1), ('w2', 0), ('w2', 1))
+WIDE = 256
+UPRIGHT, TURNED = 0, 1
+
+UNITS = (
+    (UPRIGHT, 0, WIDE), (UPRIGHT, WIDE, WIDE), (TURNED, 0, WIDE), (TURNED, WIDE, WIDE), (UPRIGHT, 2 * WIDE, WIDE),
+    (TURNED, 2 * WIDE, WIDE), (UPRIGHT, 3 * WIDE, WIDE), (TURNED, 3 * WIDE, P), (TURNED, 3 * WIDE + P, P),
+)
+ON_VECTOR = ((UPRIGHT, 6), (TURNED, 3))
 RING = 4
-PSUM_GAINS = False
-EARLY_BANKS = 8
-VECTOR_BANKS = ((0, 1, 2), (1, 0, 3))
-LATE_FIRST = False
-LAG = 3
+SUM_LAG = 3
 GAIN_LAG = 5
-QUANT_LAG = 6
-COPY_LAG = 0
-FEATURE_LAG = {256: 1}
 W2_STEP = 4
-LATE_STEP = 1
-WI_STEP = 0
 
 
 def tile_list_radar_log_power_kernel(tc, tab_words, tab_scales, offs, wi, wq_words, wq_scales, gain, w2, out):
@@ -57,11 +48,10 @@ def tile_list_radar_log_power_kernel(tc, tab_words, tab_scales, offs, wi, wq_wor
         staging = ctx.enter_context(tc.tile_pool(name="staging", bufs=1))
         ring = ctx.enter_context(tc.tile_pool(name="ring", bufs=1))
         psum = ctx.enter_context(tc.psum_pool(name="psum", bufs=1))
-        psum_keep = ctx.enter_context(tc.psum_pool(name="psum_keep", bufs=1))
 
         made = {"bank": 0}
         room = {"grouped": 4096, "squares": 4096, "h": 2048, "result": 3072, "twin": 2048, "piece": 512}
-        depth = {"grouped": RING, "squares": RING, "h": RING, "result": RING, "twin": 2, "piece": 3}
+        depth = {"grouped": RING, "squares": RING, "h": RING, "result": RING, "twin": len(ON_VECTOR), "piece": N_TILES}
         starts = {}
         for kind in room:
             starts[kind] = sum(room[other] * depth[other] for other in starts)
@@ -70,7 +60,7 @@ def tile_list_radar_log_power_kernel(tc, tab_words, tab_scales, offs, wi, wq_wor
         def next_bank():
             n = made["bank"]
             made["bank"] = n + 1
-            return psum.tile([P, BANK], F32, name=f"bank{n}", offset=4 * BANK * (n % (7 if PSUM_GAINS else 8)))
+            return psum.tile([P, BANK], F32, name=f"bank{n}", offset=4 * BANK * (n % BANKS))
 
         def stream(kind, shape, dtype):
             n = made[kind]
@@ -90,19 +80,17 @@ def tile_list_radar_log_power_kernel(tc, tab_words, tab_scales, offs, wi, wq_wor
         table1_end = table1_at + 4 * T
 
         wq_rows = wq_words.rearrange("a p c -> p a c").bitcast(I32)
-        wq_raw = [
-            keep.tile([P, PASSES, K_PASS // 2], I32, name="wq_raw0", align_bytes=256),
-            staging.tile([P, PASSES, K_PASS // 2], I32, name="wq_raw1", offset=table0_at, align_bytes=256),
-        ]
+        wq_upright = keep.tile([P, PASSES, K_PASS // 2], I32, name="wq_upright", align_bytes=256)
+        wq_turned = staging.tile([P, PASSES, K_PASS // 2], I32, name="wq_turned", offset=table0_at, align_bytes=256)
 
         scale_window = staging.tile([P, T // 4], I32, name="scale_window", offset=table1_end - 256, align_bytes=256)
         nc.sync.dma_start(scale_window[96:P, :], tab_scales.rearrange("a q t -> q a t").bitcast(I32))
-        nc.sync.dma_start(wq_raw[0][:], wq_rows[:, :, : K_PASS // 2])
-        wq_scales_raw = keep.tile([P, PASSES, H // 4], I32, name="wq_scales_raw", align_bytes=256)
-        nc.gpsimd.memset(wq_scales_raw[:], 0)
+        nc.sync.dma_start(wq_upright[:], wq_rows[:, :, : K_PASS // 2])
+        wq_scale_rows = keep.tile([P, PASSES, H // 4], I32, name="wq_scale_rows", align_bytes=256)
+        nc.gpsimd.memset(wq_scale_rows[:], 0)
         for quad in range(4):
             nc.sync.dma_start(
-                wq_scales_raw[32 * quad : 32 * quad + 4, :, :],
+                wq_scale_rows[32 * quad : 32 * quad + 4, :, :],
                 wq_scales[:, 4 * quad : 4 * quad + 4, :].rearrange("a r c -> r a c").bitcast(I32),
             )
         one = keep.tile([P, 1], F32, name="one")
@@ -115,18 +103,14 @@ def tile_list_radar_log_power_kernel(tc, tab_words, tab_scales, offs, wi, wq_wor
         make_identity(nc, identity[:])
         zero = keep.tile([P, 1], F32, name="zero")
         nc.scalar.activation(zero[:], one[:], ACT.Ln)
-        gain_rows = keep.tile([P, K_PASS if PSUM_GAINS else P], F32, name="gain_rows", align_bytes=256)
+        gain_rows = keep.tile([P, P], F32, name="gain_rows", align_bytes=256)
         nc.vector.memset(gain_rows[:], 0.0)
-        if PSUM_GAINS:
-            nc.sync.dma_start(gain_rows[0:GROUPS, :], gain.rearrange("(g c) -> g c", g=GROUPS))
-        else:
-            nc.sync.dma_start(gain_rows[0:P:16, :], gain.rearrange("(g b c) -> b g c", g=GROUPS, c=P))
+        nc.sync.dma_start(gain_rows[0:P:16, :], gain.rearrange("(g b c) -> b g c", g=GROUPS, c=P))
         v_planes = keep.tile([P, PASSES * S // 4], I32, name="v_planes", align_bytes=256)
         nc.vector.memset(v_planes[:], 0)
 
         picked_scales = keep.tile([P, S // 4], I32, name="picked_scales", align_bytes=256)
         nc.vector.tensor_copy(picked_scales[:].bitcast(U8), scale_window[:].bitcast(U8).indirect(offsets[:]))
-
         for quad in range(4):
             nc.sync.dma_start(v_planes[32 * quad : 32 * quad + 4, :], picked_scales[96 + 8 * quad : 104 + 8 * quad, :])
         table1 = staging.tile([P, T], I32, name="table1", offset=table1_at, align_bytes=256)
@@ -135,28 +119,19 @@ def tile_list_radar_log_power_kernel(tc, tab_words, tab_scales, offs, wi, wq_wor
 
         raw = staging.tile([P, raw_columns], F32, name="raw", offset=raw_at, align_bytes=256)
         wi_raw = {}
-        w2_raw = {}
-
-        def load_wi(g, a):
-            at = (g * PASSES + a) * piece
-            wi_raw[g, a] = raw[:, at : at + piece].rearrange("p (j c) -> p j c", j=PACK)
-            rows = wi[a * K_PASS : (a + 1) * K_PASS, g * K_PASS : (g + 1) * K_PASS]
-            nc.sync.dma_start(wi_raw[g, a], rows.rearrange("(p j) c -> p j c", j=PACK))
-
-        def load_w2(g):
-            at = w2_at + g * PACK * N
-            w2_raw[g] = raw[:, at : at + PACK * N]
+        for g in range(GROUPS):
+            for a in range(PASSES):
+                at = (g * PASSES + a) * piece
+                wi_raw[g, a] = raw[:, at : at + piece].rearrange("p (j c) -> p j c", j=PACK)
+                rows = wi[a * K_PASS : (a + 1) * K_PASS, g * K_PASS : (g + 1) * K_PASS]
+                nc.sync.dma_start(wi_raw[g, a], rows.rearrange("(p j) c -> p j c", j=PACK))
+                if (g, a) == (0, 0):
+                    nc.sync.dma_start(wq_turned[:], wq_rows[:, :, K_PASS // 2 :])
+        w2_raw = [raw[:, w2_at + g * PACK * N : w2_at + (g + 1) * PACK * N] for g in range(GROUPS)]
+        for g in range(GROUPS):
             rows = w2[g * K_PASS : (g + 1) * K_PASS, :].rearrange("(s t i) n -> t s i n", t=PACK, i=RUN)
             for t in range(PACK):
                 nc.sync.dma_start(w2_raw[g][:, t * N : (t + 1) * N], rows[t])
-
-        for item in LOADS:
-            if item[0] == "wi":
-                load_wi(item[1], item[2])
-            elif item[0] == "w2":
-                load_w2(item[1])
-            else:
-                nc.sync.dma_start(wq_raw[1][:], wq_rows[:, :, K_PASS // 2 :])
 
         v_codes = [keep.tile([P, S], U32, name=f"v_codes{a}", align_bytes=256) for a in range(PASSES)]
 
@@ -167,50 +142,26 @@ def tile_list_radar_log_power_kernel(tc, tab_words, tab_scales, offs, wi, wq_wor
                     table[:].bitcast(U32).indirect(offsets[:, half * BANK // 16 : (half + 1) * BANK // 16]),
                 )
 
-        wq_codes = {}
-        wq_planes = {}
-
-        def is_sorted(g):
-            return any((g, half) in UPRIGHT for half in range(HALVES))
-
-        def sort_wq(g):
-            if not is_sorted(g):
-                wq_codes[g] = [wq_raw[g][:, a, :].bitcast(U8) for a in range(PASSES)]
-                wq_planes[g] = [wq_scales_raw[:, a, g * P : (g + 1) * P].bitcast(U8) for a in range(PASSES)]
-                return
-            planes = keep.tile([P, PASSES, K_PASS // 4], I32, name=f"wq_planes{g}", align_bytes=256)
-            nc.vector.tensor_copy(
-                planes[:].rearrange("p a (t s) -> p a t s", t=PACK),
-                wq_scales_raw[:, :, g * P : (g + 1) * P].rearrange("p a (s t) -> p a t s", t=PACK),
-            )
-            codes = keep.tile([P, PASSES, K_PASS // 2], I32, name=f"wq_codes{g}", align_bytes=256)
-            nc.vector.tensor_copy(
-                codes[:].rearrange("p a (t s w) -> p a t s w", t=PACK, w=2),
-                wq_raw[g][:].rearrange("p a (s t w) -> p a t s w", t=PACK, w=2),
-            )
-            wq_codes[g] = [codes[:, a, :].bitcast(U8) for a in range(PASSES)]
-            wq_planes[g] = [planes[:, a, :].bitcast(U8) for a in range(PASSES)]
-
-        sort_wq(0)
+        wq_planes = keep.tile([P, PASSES, K_PASS // 4], I32, name="wq_planes", align_bytes=256)
+        nc.vector.tensor_copy(
+            wq_planes[:].rearrange("p a (t s) -> p a t s", t=PACK),
+            wq_scale_rows[:, :, :P].rearrange("p a (s t) -> p a t s", t=PACK),
+        )
+        wq_sorted = keep.tile([P, PASSES, K_PASS // 2], I32, name="wq_sorted", align_bytes=256)
+        nc.vector.tensor_copy(
+            wq_sorted[:].rearrange("p a (t s w) -> p a t s w", t=PACK, w=2),
+            wq_upright[:].rearrange("p a (s t w) -> p a t s w", t=PACK, w=2),
+        )
         gather_words(0, table0)
-        gain_sorted = keep.tile([P, K_PASS if PSUM_GAINS else P], F32, name="gain_sorted", align_bytes=256)
+        gain_sorted = keep.tile([P, P], F32, name="gain_sorted", align_bytes=256)
         nc.vector.tensor_copy(
             gain_sorted[:].rearrange("p (t s i) -> p t s i", t=PACK, i=RUN),
             gain_rows[:].rearrange("p (s t i) -> p t s i", t=PACK, i=RUN),
         )
-        if PSUM_GAINS:
-            gain_bank = psum_keep.tile([P, BANK], F32, name="gain_bank")
-            for t in range(PACK):
-                nc.tensor.transpose(gain_bank[:, t::PACK], gain_sorted[:, t * P : (t + 1) * P], identity[:])
-            gains = gain_bank[:].rearrange("p (r t) -> p r t", t=PACK)
-        else:
-            gain_turned = keep.tile([P, P], F32, name="gain_turned", align_bytes=256)
-            nc.vector.transpose(gain_turned[:], gain_sorted[:])
-            gain_tile = keep.tile([P, GROUPS, PACK], F32, name="gains")
-            nc.vector.tensor_copy(
-                gain_tile[:], gain_turned[:].rearrange("p (t g x) -> p g t x", t=PACK, g=GROUPS)[:, :, :, 0]
-            )
-            gains = gain_tile[:]
+        gain_turned = keep.tile([P, P], F32, name="gain_turned", align_bytes=256)
+        nc.vector.transpose(gain_turned[:], gain_sorted[:])
+        gains = keep.tile([P, GROUPS, PACK], F32, name="gains")
+        nc.vector.tensor_copy(gains[:], gain_turned[:].rearrange("p (t g x) -> p g t x", t=PACK, g=GROUPS)[:, :, :, 0])
         gather_words(1, table1)
 
         power = {}
@@ -222,149 +173,105 @@ def tile_list_radar_log_power_kernel(tc, tab_words, tab_scales, offs, wi, wq_wor
             at = PACK * (start % BANK)
             return power[g, start // BANK][:, at : at + PACK * width]
 
-        def is_upright(g, start):
-            return (g, start // BANK) in UPRIGHT
+        def plane_pass(out_view, a, codes, scales, start, width):
+            nc.tensor.matmul_mx(
+                out=out_view,
+                lhsT=codes,
+                lhsT_scale=scales,
+                rhs=v_codes[a][:, start : start + width].bitcast(FP8X4),
+                rhs_scale=v_scales[:, a * S + start : a * S + start + width],
+                start=(a == 0),
+                stop=(a == PASSES - 1),
+            )
 
-        def cells_pass(bank, first, a, codes, scales):
+        def cells_pass(bank, a, codes, scales, start):
             nc.tensor.matmul_mx(
                 out=bank[:],
-                lhsT=v_codes[a][:, first : first + P].bitcast(FP8X4),
-                lhsT_scale=v_scales[:, a * S + first : a * S + first + P],
+                lhsT=v_codes[a][:, start : start + P].bitcast(FP8X4),
+                lhsT_scale=v_scales[:, a * S + start : a * S + start + P],
                 rhs=codes,
                 rhs_scale=scales,
                 start=(a == 0),
                 stop=(a == PASSES - 1),
             )
 
-        def quadrature_pass(bank, g, half, k, a):
-            if (g, half) in UPRIGHT:
-                nc.tensor.matmul_mx(
-                    out=bank[:],
-                    lhsT=wq_codes[g][a][:, 2 * k * P : 2 * (k + 1) * P].bitcast(FP4X4),
-                    lhsT_scale=wq_planes[g][a][:, k * P : (k + 1) * P],
-                    rhs=v_codes[a][:, half * BANK : (half + 1) * BANK].bitcast(FP8X4),
-                    rhs_scale=v_scales[:, a * S + half * BANK : a * S + (half + 1) * BANK],
-                    start=(a == 0),
-                    stop=(a == PASSES - 1),
-                )
+        def square_quadrature(g, n, bank):
+            if g == UPRIGHT:
+                half, t = divmod(n, PACK)
+                squared = power[g, half][:].rearrange("p (u t j) -> p u t j", t=PACK, j=WIDE)[:, :, t, :]
+                pattern, sizes = "p (u j) -> p u j", {"j": WIDE}
             else:
-                cells_pass(bank, half * BANK + k * P, a, wq_codes[g][a].bitcast(FP4X4), wq_planes[g][a])
-
-        pointer_bias = [zero[:]]
-
-        def square(out_view, bank, view, engine):
-            if engine == "A":
-                nc.scalar.activation(out_view, view(bank[:]), ACT.Square, bias=pointer_bias.pop() if pointer_bias else 0.0)
-            else:
+                squared = power_of(g, n * P, P).rearrange("p (t s i) -> p t s i", t=PACK, i=RUN)
+                pattern, sizes = "p (s t i) -> p t s i", {"t": PACK, "i": RUN}
+            values = bank[:].rearrange(pattern, **sizes)
+            if (g, n) in ON_VECTOR:
                 twin = stream("twin", [P, BANK], F32)
                 nc.vector.tensor_copy(twin[:], bank[:])
-                nc.vector.tensor_tensor(out_view, view(bank[:]), view(twin[:]), ALU.mult)
-
-        def quadrature_square(bank, g, half, k, engine):
-            if (g, half) in UPRIGHT:
-                widths = [width for start, width in sorted(UNITS[g]) if start // BANK == half]
-                at = 0
-                for width in sorted(set(widths), reverse=True):
-                    span = width * widths.count(width)
-                    square(
-                        power_of(g, half * BANK + at, span).rearrange("p (u t j) -> p u t j", t=PACK, j=width)[:, :, k, :],
-                        bank,
-                        lambda x: x[:, at : at + span].rearrange("p (u j) -> p u j", j=width),
-                        engine,
-                    )
-                    at += span
-            elif is_sorted(g):
-                square(power_of(g, half * BANK + k * P, P), bank, lambda x: x, engine)
+                nc.vector.tensor_tensor(squared, values, twin[:].rearrange(pattern, **sizes), ALU.mult)
             else:
-                square(
-                    power_of(g, half * BANK + k * P, P).rearrange("p (t s i) -> p t s i", t=PACK, i=RUN),
-                    bank,
-                    lambda x: x.rearrange("p (s t i) -> p t s i", t=PACK, i=RUN),
-                    engine,
-                )
+                nc.scalar.activation(squared, values, ACT.Square, bias=zero[:] if (g, n) == (UPRIGHT, 0) else 0.0)
 
-        def first_quadrature():
-            slots = [(half, k) for half in range(HALVES) for k in range(PACK)][:EARLY_BANKS]
-            banks = [next_bank() for slot in slots]
+        def upright_quadrature():
+            banks = [next_bank() for n in range(BANKS)]
             for a in range(PASSES):
-                for bank, (half, k) in zip(banks, slots):
-                    quadrature_pass(bank, 0, half, k, a)
+                for n, bank in enumerate(banks):
+                    half, t = divmod(n, PACK)
+                    codes = wq_sorted[:, a, :].bitcast(U8)[:, 2 * t * P : 2 * (t + 1) * P].bitcast(FP4X4)
+                    scales = wq_planes[:, a, :].bitcast(U8)[:, t * P : (t + 1) * P]
+                    plane_pass(bank[:], a, codes, scales, half * BANK, BANK)
                     if a == PASSES - 1:
-                        quadrature_square(bank, 0, half, k, "V" if (0, half, k) in VECTOR_BANKS else "A")
+                        square_quadrature(UPRIGHT, n, bank)
 
-        def late_quadrature(g, half, k, engine):
-            bank = next_bank()
-            for a in range(PASSES):
-                quadrature_pass(bank, g, half, k, a)
-            quadrature_square(bank, g, half, k, engine)
+        def turned_quadrature():
+            for n in range(S // P):
+                bank = next_bank()
+                for a in range(PASSES):
+                    codes = wq_turned[:, a, :].bitcast(U8).bitcast(FP4X4)
+                    cells_pass(bank, a, codes, wq_scale_rows[:, a, P:].bitcast(U8), n * P)
+                square_quadrature(TURNED, n, bank)
 
-        wi_grouped = {}
         wi_codes = {}
         wi_scales = {}
 
-        engines = {"V": nc.vector, "G": nc.gpsimd}
-
-        def round_wi(g, a, engine, parts):
-            grouped = stream("grouped", [P, piece], BF16)
-            for first in range(0, PACK, PACK // parts):
-                last = first + PACK // parts
-                engines[engine].tensor_copy(
-                    grouped[:].rearrange("p (t s i j) -> p t s j i", t=PACK, i=RUN, j=PACK)[:, first:last],
-                    wi_raw[g, a].rearrange("p j (s t i) -> p t s j i", t=PACK, i=RUN)[:, first:last],
+        def prepare_wi(g):
+            for a in range(PASSES):
+                grouped = stream("grouped", [P, piece], BF16)
+                nc.vector.tensor_copy(
+                    grouped[:].rearrange("p (t s i j) -> p t s j i", t=PACK, i=RUN, j=PACK),
+                    wi_raw[g, a].rearrange("p j (s t i) -> p t s j i", t=PACK, i=RUN),
                 )
-            wi_grouped[g, a] = grouped
-
-        def quantize_wi(g, a):
-            wi_codes[g, a] = keep.tile([P, K_PASS], U32, name=f"wi_codes{g}_{a}", align_bytes=256)
-            wi_scales[g, a] = keep.tile([P, K_PASS], U8, name=f"wi_scales{g}_{a}", align_bytes=256)
-            nc.vector.quantize_mx(
-                out=wi_codes[g, a][:].bitcast(FP8X4), scales=wi_scales[g, a][:], in_=wi_grouped[g, a][:]
-            )
+                wi_codes[g, a] = keep.tile([P, K_PASS], U32, name=f"wi_codes{g}_{a}", align_bytes=256)
+                wi_scales[g, a] = keep.tile([P, K_PASS], U8, name=f"wi_scales{g}_{a}", align_bytes=256)
+                nc.vector.quantize_mx(out=wi_codes[g, a][:].bitcast(FP8X4), scales=wi_scales[g, a][:], in_=grouped[:])
 
         squares = {}
 
         def in_phase(g, start, width):
             squares[g, start] = stream("squares", [P, PACK * width], F32)
-            if is_upright(g, start):
-                per_bank = BANK // width
-                for first in range(0, PACK, per_bank):
-                    bank = next_bank()
-                    for t in range(first, first + per_bank):
-                        for a in range(PASSES):
-                            nc.tensor.matmul_mx(
-                                out=bank[:, (t - first) * width : (t - first + 1) * width],
-                                lhsT=wi_codes[g, a][:, t * P : (t + 1) * P].bitcast(FP8X4),
-                                lhsT_scale=wi_scales[g, a][:, t * P : (t + 1) * P],
-                                rhs=v_codes[a][:, start : start + width].bitcast(FP8X4),
-                                rhs_scale=v_scales[:, a * S + start : a * S + start + width],
-                                start=(a == 0),
-                                stop=(a == PASSES - 1),
-                            )
-                    nc.scalar.activation(
-                        squares[g, start][:, first * width : first * width + BANK], bank[:], ACT.Square, bias=0.0
-                    )
-            else:
-                for f in range(width // P):
-                    bank = next_bank()
-                    for a in range(PASSES):
-                        cells_pass(bank, start + f * P, a, wi_codes[g, a][:].bitcast(FP8X4), wi_scales[g, a][:])
-                    nc.scalar.activation(
-                        squares[g, start][:, f * BANK : (f + 1) * BANK], bank[:], ACT.Square, bias=0.0
-                    )
-
-        sums = {}
-
-        def add_squares(g, start, width, engine):
-            total = power_of(g, start, width)
-            if is_upright(g, start):
-                engines[engine].tensor_tensor(total, squares[g, start][:], total, ALU.add)
-                return
             for f in range(width // P):
                 bank = next_bank()
-                sums[g, start + f * P] = bank
+                if g == UPRIGHT:
+                    for n, t in enumerate(range(2 * f, 2 * f + 2)):
+                        for a in range(PASSES):
+                            codes = wi_codes[g, a][:, t * P : (t + 1) * P].bitcast(FP8X4)
+                            scales = wi_scales[g, a][:, t * P : (t + 1) * P]
+                            plane_pass(bank[:, n * width : (n + 1) * width], a, codes, scales, start, width)
+                else:
+                    for a in range(PASSES):
+                        cells_pass(bank, a, wi_codes[g, a][:].bitcast(FP8X4), wi_scales[g, a][:], start + f * P)
+                nc.scalar.activation(squares[g, start][:, f * BANK : (f + 1) * BANK], bank[:], ACT.Square, bias=0.0)
+
+        def log_power(g, start, width):
+            total = power_of(g, start, width)
+            if g == UPRIGHT:
+                nc.vector.tensor_tensor(total, squares[g, start][:], total, ALU.add)
+                nc.scalar.activation(total, total, ACT.Ln, bias=1.0)
+                return
+            banks = [next_bank() for f in range(width // P)]
+            for f, bank in enumerate(banks):
                 for t in range(PACK):
                     cols = slice(f * BANK + t * P, f * BANK + (t + 1) * P)
-                    for n, term in enumerate((squares[g, start], total) if LATE_FIRST else (total, squares[g, start])):
+                    for n, term in enumerate((total, squares[g, start])):
                         nc.tensor.matmul(
                             bank[:, t * P : (t + 1) * P],
                             term[:, cols],
@@ -373,28 +280,13 @@ def tile_list_radar_log_power_kernel(tc, tab_words, tab_scales, offs, wi, wq_wor
                             stop=(n == 1),
                             is_transpose=True,
                         )
-
-        def take_log(g, start, width):
-            total = power_of(g, start, width)
-            if is_upright(g, start):
-                nc.scalar.activation(total, total, ACT.Ln, bias=1.0)
-                return
-            for f in range(width // P):
+            for f, bank in enumerate(banks):
                 nc.scalar.activation(
                     total[:, f * BANK : (f + 1) * BANK].rearrange("p (j t) -> p j t", t=PACK),
-                    sums[g, start + f * P][:].rearrange("p (t j) -> p j t", t=PACK),
+                    bank[:].rearrange("p (t j) -> p j t", t=PACK),
                     ACT.Ln,
                     bias=1.0,
                 )
-
-        def take_log_part(g, start, width):
-            at = start % P
-            nc.scalar.activation(
-                power_of(g, start, width).rearrange("p (j t) -> p j t", t=PACK),
-                sums[g, start - at][:].rearrange("p (t j) -> p j t", t=PACK)[:, at : at + width],
-                ACT.Ln,
-                bias=1.0,
-            )
 
         h_codes = [keep.tile([P, S], U32, name=f"h_codes{g}", align_bytes=256) for g in range(GROUPS)]
         h_scales = [keep.tile([P, S], U8, name=f"h_scales{g}", align_bytes=256) for g in range(GROUPS)]
@@ -402,12 +294,12 @@ def tile_list_radar_log_power_kernel(tc, tab_words, tab_scales, offs, wi, wq_wor
 
         def apply_gain(g, start, width):
             h = stream("h", [P, PACK * width], BF16)
-            if is_upright(g, start):
-                whole = [unit for unit in UNITS[g] if unit[0] <= start < unit[0] + unit[1]][0]
-                first = (start - whole[0]) // RUN
+            if g == UPRIGHT:
+                first = start % WIDE // RUN
+                unit = power_of(g, start - start % WIDE, WIDE).rearrange("p (t c i) -> p c t i", t=PACK, i=RUN)
                 nc.vector.tensor_tensor(
                     h[:].rearrange("p (c i t) -> p c t i", i=RUN, t=PACK),
-                    power_of(g, *whole).rearrange("p (t c i) -> p c t i", t=PACK, i=RUN)[:, first : first + width // RUN],
+                    unit[:, first : first + width // RUN],
                     gains[:, g, :].unsqueeze(1).unsqueeze(3).to_broadcast([P, width // RUN, PACK, RUN]),
                     ALU.mult,
                 )
@@ -431,33 +323,26 @@ def tile_list_radar_log_power_kernel(tc, tab_words, tab_scales, offs, wi, wq_wor
         w2_codes = keep.tile([P, GROUPS * N], U32, name="w2_codes", align_bytes=256)
         w2_scales = keep.tile([P, GROUPS * N], U8, name="w2_scales", align_bytes=256)
 
-        def round_w2(g, engine, parts):
-            runs = N // RUN // parts
-            for first in range(0, N // RUN, runs):
-                engines[engine].tensor_copy(
-                    w2_grouped[:, g * PACK * N : (g + 1) * PACK * N].rearrange("p (c i j) -> p c j i", i=RUN, j=PACK)[
-                        :, first : first + runs
-                    ],
-                    w2_raw[g].rearrange("p (j c i) -> p c j i", j=PACK, i=RUN)[:, first : first + runs],
+        def prepare_w2():
+            for g in range(GROUPS):
+                nc.vector.tensor_copy(
+                    w2_grouped[:, g * PACK * N : (g + 1) * PACK * N].rearrange("p (c i j) -> p c j i", i=RUN, j=PACK),
+                    w2_raw[g].rearrange("p (j c i) -> p c j i", j=PACK, i=RUN),
                 )
-
-        def quantize_w2(first, count):
-            nc.vector.quantize_mx(
-                out=w2_codes[:, first : first + count].bitcast(FP8X4),
-                scales=w2_scales[:, first : first + count],
-                in_=w2_grouped[:, PACK * first : PACK * (first + count)],
-            )
+            for first, last in ((0, BANK), (BANK, GROUPS * N)):
+                nc.vector.quantize_mx(
+                    out=w2_codes[:, first:last].bitcast(FP8X4),
+                    scales=w2_scales[:, first:last],
+                    in_=w2_grouped[:, PACK * first : PACK * last],
+                )
 
         out_rows = out.rearrange("(c p) j -> p c j", p=P)
 
-        feature_banks = {}
-
-        def features(start, width, per_bank):
-            feature_banks[start] = []
-            for first in range(0, N_TILES, per_bank):
-                feature_banks[start].append((first, min(first + per_bank, N_TILES), next_bank()))
+        def features(start, width):
+            per_bank = 1 if start + width == S else BANK // width
+            banks = [(first, min(first + per_bank, N_TILES), next_bank()) for first in range(0, N_TILES, per_bank)]
             for g in range(GROUPS):
-                for first, last, bank in feature_banks[start]:
+                for first, last, bank in banks:
                     for c in range(first, last):
                         col = g * N + c * P
                         nc.tensor.matmul_mx(
@@ -469,72 +354,46 @@ def tile_list_radar_log_power_kernel(tc, tab_words, tab_scales, offs, wi, wq_wor
                             start=(g == 0 and c == first),
                             stop=(g == GROUPS - 1 and c == last - 1),
                         )
-
-        def copy_features(start, width, who):
+            rows = out_rows[:, :, start : start + width]
+            if start + width == S:
+                for (first, last, bank), copy in zip(banks, (nc.scalar.copy, nc.vector.tensor_copy, nc.scalar.copy)):
+                    result = stream("piece", [P, width], F32)
+                    copy(result[:], bank[:, :width])
+                    nc.sync.dma_start(rows[:, first, :], result[:])
+                return
+            by_bank = start + width == S - WIDE
             result = stream("result", [P, N_TILES, width], F32)
-            for (first, last, bank), engine in zip(feature_banks[start], who):
-                copy = nc.vector.tensor_copy if engine == "V" else nc.scalar.copy
-                copy(result[:, first:last, :].rearrange("p c j -> p (c j)"), bank[:, : (last - first) * width])
-            nc.sync.dma_start(out_rows[:, :, start : start + width], result[:])
+            for first, last, bank in banks:
+                nc.scalar.copy(result[:, first:last, :].rearrange("p c j -> p (c j)"), bank[:, : (last - first) * width])
+                if by_bank:
+                    nc.sync.dma_start(rows[:, first:last, :], result[:, first:last, :])
+            if not by_bank:
+                nc.sync.dma_start(rows, result[:])
 
-        def copy_and_store(start, width, who):
-            for (first, last, bank), engine in zip(feature_banks[start], who):
-                result = stream("piece", [P, last - first, width], F32)
-                copy = nc.vector.tensor_copy if engine == "V" else nc.scalar.copy
-                copy(result[:].rearrange("p c j -> p (c j)"), bank[:, : (last - first) * width])
-                nc.sync.dma_start(out_rows[:, first:last, start : start + width], result[:])
-
-        first_quadrature()
-        for a in range(PASSES):
-            round_wi(0, a, "V", 1)
-            quantize_wi(0, a)
-            if a == 0:
-                sort_wq(1)
-
-        order = [(g,) + UNITS[g][u] for g, u in ORDER]
-        closing = order[:-3] + [(g, start, P) for start in (S - 2 * P, S - P) for g in range(GROUPS)]
-        done = set()
-        ready = []
-        closed = []
-        last = len(order) - 1
-        for step in range(len(closing) + QUANT_LAG + COPY_LAG + 1):
-            if step == LATE_STEP:
-                slots = [(g, half, k) for g in range(GROUPS) for half in range(HALVES) for k in range(PACK)]
-                for slot in slots[EARLY_BANKS:]:
-                    late_quadrature(*slot, "V" if slot in VECTOR_BANKS else "A")
-            if step <= last:
-                in_phase(*order[step])
-            if step == WI_STEP:
-                for a in range(PASSES):
-                    round_wi(1, a, "V", 1)
-                    quantize_wi(1, a)
-            if 0 <= step - LAG <= last:
-                add_squares(*order[step - LAG], ADDERS.get(ORDER[step - LAG], "V"))
-                take_log(*order[step - LAG])
+        upright_quadrature()
+        prepare_wi(UPRIGHT)
+        closing = list(UNITS[:-3]) + [(g, start, P) for start in (S - 2 * P, S - P) for g in range(GROUPS)]
+        waiting = None
+        for step in range(len(closing) + GAIN_LAG + 1):
+            if step == 1:
+                turned_quadrature()
+            if step < len(UNITS):
+                in_phase(*UNITS[step])
+            if step == 0:
+                prepare_wi(TURNED)
+            if 0 <= step - SUM_LAG < len(UNITS):
+                log_power(*UNITS[step - SUM_LAG])
             if step == W2_STEP:
-                for g in range(GROUPS):
-                    round_w2(g, "V", 1)
-                quantize_w2(0, BANK)
-                quantize_w2(BANK, GROUPS * N - BANK)
+                prepare_w2()
             if 0 <= step - GAIN_LAG < len(closing):
                 apply_gain(*closing[step - GAIN_LAG])
-            if 0 <= step - QUANT_LAG < len(closing):
-                g, start, width = closing[step - QUANT_LAG]
+            if 0 <= step - GAIN_LAG - 1 < len(closing):
+                g, start, width = closing[step - GAIN_LAG - 1]
                 quantize_h(g, start, width)
-                for cell in range(start, start + width, P):
-                    done.add((g, cell))
-                for start, width in FEATURES:
-                    complete = all((g, cell) in done for g in range(GROUPS) for cell in range(start, start + width, P))
-                    if complete and start not in [s for s, w, at in closed]:
-                        closed.append((start, width, step))
-            for start, width, at in closed:
-                if at + FEATURE_LAG.get(start, 0) == step:
-                    features(start, width, 1 if start + width == S else BANK // width)
-                    ready.append((start, width, step))
-            for start, width, at in ready:
-                if at + COPY_LAG == step:
-                    who = COPIERS[[s for s, w in FEATURES].index(start)]
-                    if start + width == S:
-                        copy_and_store(start, width, who)
-                    else:
-                        copy_features(start, width, who)
+                if waiting is not None:
+                    features(*waiting)
+                    waiting = None
+                if g == TURNED and start == WIDE:
+                    waiting = (start, width)
+                elif g == TURNED:
+                    features(start, width)

@@ -28,17 +28,11 @@ HALVES = S // BANK
 N_TILES = N // P
 RUN = 4
 WIDE = 256
-UPRIGHT, TURNED = 0, 1
-
-UNITS = (
-    (UPRIGHT, 0, WIDE), (UPRIGHT, WIDE, WIDE), (TURNED, 0, WIDE), (TURNED, WIDE, WIDE), (UPRIGHT, 2 * WIDE, WIDE),
-    (TURNED, 2 * WIDE, WIDE), (UPRIGHT, 3 * WIDE, WIDE), (TURNED, 3 * WIDE, P), (TURNED, 3 * WIDE + P, P),
-)
-ON_VECTOR = ((UPRIGHT, 6), (TURNED, 3))
+LATE, EARLY = 0, 1
+UPRIGHT_CELLS = 768
+RISING, FALLING = (0, 1), (1, 0)
 RING = 4
-SUM_LAG = 3
-GAIN_LAG = 5
-W2_STEP = 4
+LAST_GATHERS = (256, 256, 512)
 
 
 def tile_list_radar_log_power_kernel(tc, tab_words, tab_scales, offs, wi, wq_words, wq_scales, gain, w2, out):
@@ -50,8 +44,8 @@ def tile_list_radar_log_power_kernel(tc, tab_words, tab_scales, offs, wi, wq_wor
         psum = ctx.enter_context(tc.psum_pool(name="psum", bufs=1))
 
         made = {"bank": 0}
-        room = {"grouped": 4096, "squares": 4096, "h": 2048, "result": 3072, "twin": 2048, "piece": 512}
-        depth = {"grouped": RING, "squares": RING, "h": RING, "result": RING, "twin": len(ON_VECTOR), "piece": N_TILES}
+        room = {"grouped": 4096, "squares": 4096, "h": 2048, "result": 3072, "piece": 512, "twin": 2048}
+        depth = {"grouped": RING, "squares": RING + GROUPS, "h": RING, "result": RING, "piece": N_TILES, "twin": 2}
         starts = {}
         for kind in room:
             starts[kind] = sum(room[other] * depth[other] for other in starts)
@@ -79,13 +73,17 @@ def tile_list_radar_log_power_kernel(tc, tab_words, tab_scales, offs, wi, wq_wor
         table1_at = raw_at + 4 * raw_columns
         table1_end = table1_at + 4 * T
 
+        row = K_PASS // 2
         wq_rows = wq_words.rearrange("a p c -> p a c").bitcast(I32)
-        wq_upright = keep.tile([P, PASSES, K_PASS // 2], I32, name="wq_upright", align_bytes=256)
-        wq_turned = staging.tile([P, PASSES, K_PASS // 2], I32, name="wq_turned", offset=table0_at, align_bytes=256)
+        wq_late = [
+            keep.tile([P, row], I32, name="wq_late0", align_bytes=256),
+            staging.tile([P, row], I32, name="wq_late1", offset=table0_at, align_bytes=256),
+        ]
+        wq_early = staging.tile([P, PASSES, row], I32, name="wq_early", offset=table0_at + 4 * row, align_bytes=256)
 
         scale_window = staging.tile([P, T // 4], I32, name="scale_window", offset=table1_end - 256, align_bytes=256)
         nc.sync.dma_start(scale_window[96:P, :], tab_scales.rearrange("a q t -> q a t").bitcast(I32))
-        nc.sync.dma_start(wq_upright[:], wq_rows[:, :, : K_PASS // 2])
+        nc.sync.dma_start(wq_late[0][:], wq_rows[:, 0, :row])
         wq_scale_rows = keep.tile([P, PASSES, H // 4], I32, name="wq_scale_rows", align_bytes=256)
         nc.gpsimd.memset(wq_scale_rows[:], 0)
         for quad in range(4):
@@ -116,17 +114,17 @@ def tile_list_radar_log_power_kernel(tc, tab_words, tab_scales, offs, wi, wq_wor
         table1 = staging.tile([P, T], I32, name="table1", offset=table1_at, align_bytes=256)
         nc.sync.dma_start(table1[:], tab_words[1].rearrange("p t i -> p (t i)").bitcast(I32))
         v_scales = v_planes[:].bitcast(U8)
+        nc.sync.dma_start(wq_late[1][:], wq_rows[:, 1, :row])
+        nc.sync.dma_start(wq_early[:], wq_rows[:, :, row:])
 
         raw = staging.tile([P, raw_columns], F32, name="raw", offset=raw_at, align_bytes=256)
         wi_raw = {}
-        for g in range(GROUPS):
+        for n, g in enumerate((EARLY, LATE)):
             for a in range(PASSES):
-                at = (g * PASSES + a) * piece
+                at = (n * PASSES + a) * piece
                 wi_raw[g, a] = raw[:, at : at + piece].rearrange("p (j c) -> p j c", j=PACK)
                 rows = wi[a * K_PASS : (a + 1) * K_PASS, g * K_PASS : (g + 1) * K_PASS]
                 nc.sync.dma_start(wi_raw[g, a], rows.rearrange("(p j) c -> p j c", j=PACK))
-                if (g, a) == (0, 0):
-                    nc.sync.dma_start(wq_turned[:], wq_rows[:, :, K_PASS // 2 :])
         w2_raw = [raw[:, w2_at + g * PACK * N : w2_at + (g + 1) * PACK * N] for g in range(GROUPS)]
         for g in range(GROUPS):
             rows = w2[g * K_PASS : (g + 1) * K_PASS, :].rearrange("(s t i) n -> t s i n", t=PACK, i=RUN)
@@ -135,24 +133,21 @@ def tile_list_radar_log_power_kernel(tc, tab_words, tab_scales, offs, wi, wq_wor
 
         v_codes = [keep.tile([P, S], U32, name=f"v_codes{a}", align_bytes=256) for a in range(PASSES)]
 
-        def gather_words(a, table):
-            for half in range(HALVES):
+        def gather_words(a, table, counts):
+            first = 0
+            for count in counts:
                 nc.vector.tensor_copy(
-                    v_codes[a][:, half * BANK : (half + 1) * BANK],
-                    table[:].bitcast(U32).indirect(offsets[:, half * BANK // 16 : (half + 1) * BANK // 16]),
+                    v_codes[a][:, first : first + count],
+                    table[:].bitcast(U32).indirect(offsets[:, first // 16 : (first + count) // 16]),
                 )
+                first = first + count
 
         wq_planes = keep.tile([P, PASSES, K_PASS // 4], I32, name="wq_planes", align_bytes=256)
         nc.vector.tensor_copy(
             wq_planes[:].rearrange("p a (t s) -> p a t s", t=PACK),
-            wq_scale_rows[:, :, :P].rearrange("p a (s t) -> p a t s", t=PACK),
+            wq_scale_rows[:, :, P:].rearrange("p a (s t) -> p a t s", t=PACK),
         )
-        wq_sorted = keep.tile([P, PASSES, K_PASS // 2], I32, name="wq_sorted", align_bytes=256)
-        nc.vector.tensor_copy(
-            wq_sorted[:].rearrange("p a (t s w) -> p a t s w", t=PACK, w=2),
-            wq_upright[:].rearrange("p a (s t w) -> p a t s w", t=PACK, w=2),
-        )
-        gather_words(0, table0)
+        gather_words(0, table0, (BANK, BANK))
         gain_sorted = keep.tile([P, P], F32, name="gain_sorted", align_bytes=256)
         nc.vector.tensor_copy(
             gain_sorted[:].rearrange("p (t s i) -> p t s i", t=PACK, i=RUN),
@@ -162,7 +157,12 @@ def tile_list_radar_log_power_kernel(tc, tab_words, tab_scales, offs, wi, wq_wor
         nc.vector.transpose(gain_turned[:], gain_sorted[:])
         gains = keep.tile([P, GROUPS, PACK], F32, name="gains")
         nc.vector.tensor_copy(gains[:], gain_turned[:].rearrange("p (t g x) -> p g t x", t=PACK, g=GROUPS)[:, :, :, 0])
-        gather_words(1, table1)
+        gather_words(1, table1, LAST_GATHERS)
+        wq_sorted = keep.tile([P, PASSES, row], I32, name="wq_sorted", align_bytes=256)
+        nc.vector.tensor_copy(
+            wq_sorted[:].rearrange("p a (t s w) -> p a t s w", t=PACK, w=2),
+            wq_early[:].rearrange("p a (s t w) -> p a t s w", t=PACK, w=2),
+        )
 
         power = {}
         for g in range(GROUPS):
@@ -173,105 +173,137 @@ def tile_list_radar_log_power_kernel(tc, tab_words, tab_scales, offs, wi, wq_wor
             at = PACK * (start % BANK)
             return power[g, start // BANK][:, at : at + PACK * width]
 
-        def plane_pass(out_view, a, codes, scales, start, width):
+        def planes_of(start, width):
+            first = start % WIDE
+            unit = sums[start - first][:].rearrange("p (t j) -> p t j", t=PACK)
+            return unit[:, :, first : first + width]
+
+        def plane_pass(out_view, a, codes, scales, start, width, order):
             nc.tensor.matmul_mx(
                 out=out_view,
                 lhsT=codes,
                 lhsT_scale=scales,
                 rhs=v_codes[a][:, start : start + width].bitcast(FP8X4),
                 rhs_scale=v_scales[:, a * S + start : a * S + start + width],
-                start=(a == 0),
-                stop=(a == PASSES - 1),
+                start=(a == order[0]),
+                stop=(a == order[-1]),
             )
 
-        def cells_pass(bank, a, codes, scales, start):
+        def cells_pass(bank, a, codes, scales, start, order):
             nc.tensor.matmul_mx(
                 out=bank[:],
                 lhsT=v_codes[a][:, start : start + P].bitcast(FP8X4),
                 lhsT_scale=v_scales[:, a * S + start : a * S + start + P],
                 rhs=codes,
                 rhs_scale=scales,
-                start=(a == 0),
-                stop=(a == PASSES - 1),
+                start=(a == order[0]),
+                stop=(a == order[-1]),
             )
 
-        def square_quadrature(g, n, bank):
-            if g == UPRIGHT:
-                half, t = divmod(n, PACK)
-                squared = power[g, half][:].rearrange("p (u t j) -> p u t j", t=PACK, j=WIDE)[:, :, t, :]
-                pattern, sizes = "p (u j) -> p u j", {"j": WIDE}
-            else:
-                squared = power_of(g, n * P, P).rearrange("p (t s i) -> p t s i", t=PACK, i=RUN)
-                pattern, sizes = "p (s t i) -> p t s i", {"t": PACK, "i": RUN}
+        def square(squared, bank, pattern, sizes, on_vector=False, bias=0.0):
             values = bank[:].rearrange(pattern, **sizes)
-            if (g, n) in ON_VECTOR:
+            if on_vector:
                 twin = stream("twin", [P, BANK], F32)
                 nc.vector.tensor_copy(twin[:], bank[:])
                 nc.vector.tensor_tensor(squared, values, twin[:].rearrange(pattern, **sizes), ALU.mult)
             else:
-                nc.scalar.activation(squared, values, ACT.Square, bias=zero[:] if (g, n) == (UPRIGHT, 0) else 0.0)
+                nc.scalar.activation(squared, values, ACT.Square, bias=bias)
 
-        def upright_quadrature():
-            banks = [next_bank() for n in range(BANKS)]
+        def upright(g, start):
+            return g == EARLY and start < UPRIGHT_CELLS
+
+        def square_turned(g, n, bank, on_vector, bias=0.0):
+            squared = power_of(g, n * P, P).rearrange("p (t s i) -> p t s i", t=PACK, i=RUN)
+            square(squared, bank, "p (s t i) -> p t s i", {"t": PACK, "i": RUN}, on_vector, bias)
+
+        def late_quadrature(on_vector):
+            banks = [next_bank() for n in range(S // P)]
             for a in range(PASSES):
                 for n, bank in enumerate(banks):
-                    half, t = divmod(n, PACK)
+                    codes = wq_late[a][:].bitcast(U8).bitcast(FP4X4)
+                    cells_pass(bank, a, codes, wq_scale_rows[:, a, :P].bitcast(U8), n * P, RISING)
+                    if a == PASSES - 1:
+                        square_turned(LATE, n, bank, n in on_vector, zero[:] if n == 0 else 0.0)
+
+        def turned_quadrature(n, on_vector=False):
+            bank = next_bank()
+            for a in range(PASSES):
+                codes = wq_early[:, a, :].bitcast(U8).bitcast(FP4X4)
+                cells_pass(bank, a, codes, wq_scale_rows[:, a, P:].bitcast(U8), n * P, RISING)
+            square_turned(EARLY, n, bank, on_vector)
+
+        def upright_quadrature(start, width, f, on_vector=False):
+            bank = next_bank()
+            per_bank = BANK // width
+            for n in range(per_bank):
+                t = per_bank * f + n
+                for a in range(PASSES):
                     codes = wq_sorted[:, a, :].bitcast(U8)[:, 2 * t * P : 2 * (t + 1) * P].bitcast(FP4X4)
                     scales = wq_planes[:, a, :].bitcast(U8)[:, t * P : (t + 1) * P]
-                    plane_pass(bank[:], a, codes, scales, half * BANK, BANK)
-                    if a == PASSES - 1:
-                        square_quadrature(UPRIGHT, n, bank)
-
-        def turned_quadrature():
-            for n in range(S // P):
-                bank = next_bank()
-                for a in range(PASSES):
-                    codes = wq_turned[:, a, :].bitcast(U8).bitcast(FP4X4)
-                    cells_pass(bank, a, codes, wq_scale_rows[:, a, P:].bitcast(U8), n * P)
-                square_quadrature(TURNED, n, bank)
+                    plane_pass(bank[:, n * width : (n + 1) * width], a, codes, scales, start, width, RISING)
+            units = power_of(EARLY, start, width).rearrange("p (u t j) -> p u t j", t=PACK, j=WIDE)
+            squared = units[:, :, per_bank * f : per_bank * (f + 1), :]
+            square(squared, bank, "p (u t j) -> p u t j", {"t": per_bank, "j": WIDE}, on_vector)
 
         wi_codes = {}
         wi_scales = {}
+        wi_grouped = {}
+
+        def round_wi(g, a):
+            wi_grouped[g, a] = stream("grouped", [P, piece], BF16)
+            nc.vector.tensor_copy(
+                wi_grouped[g, a][:].rearrange("p (t s i j) -> p t s j i", t=PACK, i=RUN, j=PACK),
+                wi_raw[g, a].rearrange("p j (s t i) -> p t s j i", t=PACK, i=RUN),
+            )
+
+        def quantize_wi(g, a):
+            wi_codes[g, a] = keep.tile([P, K_PASS], U32, name=f"wi_codes{g}_{a}", align_bytes=256)
+            wi_scales[g, a] = keep.tile([P, K_PASS], U8, name=f"wi_scales{g}_{a}", align_bytes=256)
+            nc.vector.quantize_mx(out=wi_codes[g, a][:].bitcast(FP8X4), scales=wi_scales[g, a][:], in_=wi_grouped[g, a][:])
 
         def prepare_wi(g):
             for a in range(PASSES):
-                grouped = stream("grouped", [P, piece], BF16)
-                nc.vector.tensor_copy(
-                    grouped[:].rearrange("p (t s i j) -> p t s j i", t=PACK, i=RUN, j=PACK),
-                    wi_raw[g, a].rearrange("p j (s t i) -> p t s j i", t=PACK, i=RUN),
-                )
-                wi_codes[g, a] = keep.tile([P, K_PASS], U32, name=f"wi_codes{g}_{a}", align_bytes=256)
-                wi_scales[g, a] = keep.tile([P, K_PASS], U8, name=f"wi_scales{g}_{a}", align_bytes=256)
-                nc.vector.quantize_mx(out=wi_codes[g, a][:].bitcast(FP8X4), scales=wi_scales[g, a][:], in_=grouped[:])
+                round_wi(g, a)
+                quantize_wi(g, a)
 
         squares = {}
 
         def in_phase(g, start, width):
             squares[g, start] = stream("squares", [P, PACK * width], F32)
+            per_bank = BANK // width
             for f in range(width // P):
                 bank = next_bank()
-                if g == UPRIGHT:
-                    for n, t in enumerate(range(2 * f, 2 * f + 2)):
-                        for a in range(PASSES):
+                squared = squares[g, start][:, f * BANK : (f + 1) * BANK]
+                if upright(g, start):
+                    for n in range(per_bank):
+                        t = per_bank * f + n
+                        for a in FALLING:
                             codes = wi_codes[g, a][:, t * P : (t + 1) * P].bitcast(FP8X4)
                             scales = wi_scales[g, a][:, t * P : (t + 1) * P]
-                            plane_pass(bank[:, n * width : (n + 1) * width], a, codes, scales, start, width)
+                            plane_pass(bank[:, n * width : (n + 1) * width], a, codes, scales, start, width, FALLING)
                 else:
-                    for a in range(PASSES):
-                        cells_pass(bank, a, wi_codes[g, a][:].bitcast(FP8X4), wi_scales[g, a][:], start + f * P)
-                nc.scalar.activation(squares[g, start][:, f * BANK : (f + 1) * BANK], bank[:], ACT.Square, bias=0.0)
+                    for a in FALLING:
+                        cells_pass(bank, a, wi_codes[g, a][:].bitcast(FP8X4), wi_scales[g, a][:], start + f * P, FALLING)
+                nc.scalar.activation(squared, bank[:], ACT.Square, bias=0.0)
+
+        sums = {}
+
+        def add_squares(start):
+            at = starts["grouped"] + room["grouped"] * ((PASSES + start // WIDE) % RING)
+            sums[start] = ring.tile([P, PACK * WIDE], F32, name=f"sum{start}", offset=at, align_bytes=256)
+            nc.vector.tensor_tensor(sums[start][:], squares[EARLY, start][:], power_of(EARLY, start, WIDE), ALU.add)
 
         def log_power(g, start, width):
-            total = power_of(g, start, width)
-            if g == UPRIGHT:
-                nc.vector.tensor_tensor(total, squares[g, start][:], total, ALU.add)
+            if upright(g, start):
+                total = planes_of(start, width)
                 nc.scalar.activation(total, total, ACT.Ln, bias=1.0)
                 return
+            total = power_of(g, start, width)
             banks = [next_bank() for f in range(width // P)]
             for f, bank in enumerate(banks):
                 for t in range(PACK):
                     cols = slice(f * BANK + t * P, f * BANK + (t + 1) * P)
-                    for n, term in enumerate((total, squares[g, start])):
+                    for n, term in enumerate((squares[g, start], total)):
                         nc.tensor.matmul(
                             bank[:, t * P : (t + 1) * P],
                             term[:, cols],
@@ -294,20 +326,19 @@ def tile_list_radar_log_power_kernel(tc, tab_words, tab_scales, offs, wi, wq_wor
 
         def apply_gain(g, start, width):
             h = stream("h", [P, PACK * width], BF16)
-            if g == UPRIGHT:
-                first = start % WIDE // RUN
-                unit = power_of(g, start - start % WIDE, WIDE).rearrange("p (t c i) -> p c t i", t=PACK, i=RUN)
+            factor = gains[:, g, :]
+            if upright(g, start):
                 nc.vector.tensor_tensor(
                     h[:].rearrange("p (c i t) -> p c t i", i=RUN, t=PACK),
-                    unit[:, first : first + width // RUN],
-                    gains[:, g, :].unsqueeze(1).unsqueeze(3).to_broadcast([P, width // RUN, PACK, RUN]),
+                    planes_of(start, width).rearrange("p t (c i) -> p c t i", i=RUN),
+                    factor.unsqueeze(1).unsqueeze(3).to_broadcast([P, width // RUN, PACK, RUN]),
                     ALU.mult,
                 )
             else:
                 nc.vector.tensor_tensor(
                     h[:].rearrange("p (j t) -> p j t", t=PACK),
                     power_of(g, start, width).rearrange("p (j t) -> p j t", t=PACK),
-                    gains[:, g, :].unsqueeze(1).to_broadcast([P, width, PACK]),
+                    factor.unsqueeze(1).to_broadcast([P, width, PACK]),
                     ALU.mult,
                 )
             h_rounded[g, start] = h
@@ -319,29 +350,31 @@ def tile_list_radar_log_power_kernel(tc, tab_words, tab_scales, offs, wi, wq_wor
                 in_=h_rounded[g, start][:],
             )
 
-        w2_grouped = keep.tile([P, GROUPS * PACK * N], BF16, name="w2_grouped", align_bytes=256)
+        w2_grouped = {}
         w2_codes = keep.tile([P, GROUPS * N], U32, name="w2_codes", align_bytes=256)
         w2_scales = keep.tile([P, GROUPS * N], U8, name="w2_scales", align_bytes=256)
 
-        def prepare_w2():
-            for g in range(GROUPS):
-                nc.vector.tensor_copy(
-                    w2_grouped[:, g * PACK * N : (g + 1) * PACK * N].rearrange("p (c i j) -> p c j i", i=RUN, j=PACK),
-                    w2_raw[g].rearrange("p (j c i) -> p c j i", j=PACK, i=RUN),
-                )
-            for first, last in ((0, BANK), (BANK, GROUPS * N)):
-                nc.vector.quantize_mx(
-                    out=w2_codes[:, first:last].bitcast(FP8X4),
-                    scales=w2_scales[:, first:last],
-                    in_=w2_grouped[:, PACK * first : PACK * last],
-                )
+        def round_w2(g):
+            at = starts["squares"] + room["squares"] * g
+            w2_grouped[g] = ring.tile([P, PACK * N], BF16, name=f"w2_grouped{g}", offset=at, align_bytes=256)
+            nc.vector.tensor_copy(
+                w2_grouped[g][:].rearrange("p (c i j) -> p c j i", i=RUN, j=PACK),
+                w2_raw[g].rearrange("p (j c i) -> p c j i", j=PACK, i=RUN),
+            )
+
+        def quantize_w2(g):
+            nc.vector.quantize_mx(
+                out=w2_codes[:, g * N : (g + 1) * N].bitcast(FP8X4),
+                scales=w2_scales[:, g * N : (g + 1) * N],
+                in_=w2_grouped[g][:],
+            )
 
         out_rows = out.rearrange("(c p) j -> p c j", p=P)
 
-        def features(start, width):
+        def features(start, width, copies, earlier=EARLY):
             per_bank = 1 if start + width == S else BANK // width
             banks = [(first, min(first + per_bank, N_TILES), next_bank()) for first in range(0, N_TILES, per_bank)]
-            for g in range(GROUPS):
+            for n, g in enumerate((earlier, 1 - earlier)):
                 for first, last, bank in banks:
                     for c in range(first, last):
                         col = g * N + c * P
@@ -351,49 +384,81 @@ def tile_list_radar_log_power_kernel(tc, tab_words, tab_scales, offs, wi, wq_wor
                             lhsT_scale=w2_scales[:, col : col + P],
                             rhs=h_codes[g][:, start : start + width].bitcast(FP8X4),
                             rhs_scale=h_scales[g][:, start : start + width],
-                            start=(g == 0 and c == first),
-                            stop=(g == GROUPS - 1 and c == last - 1),
+                            start=(n == 0 and c == first),
+                            stop=(n == GROUPS - 1 and c == last - 1),
                         )
             rows = out_rows[:, :, start : start + width]
             if start + width == S:
-                for (first, last, bank), copy in zip(banks, (nc.scalar.copy, nc.vector.tensor_copy, nc.scalar.copy)):
+                for (first, last, bank), copy in zip(banks, copies):
                     result = stream("piece", [P, width], F32)
                     copy(result[:], bank[:, :width])
                     nc.sync.dma_start(rows[:, first, :], result[:])
                 return
-            by_bank = start + width == S - WIDE
             result = stream("result", [P, N_TILES, width], F32)
-            for first, last, bank in banks:
-                nc.scalar.copy(result[:, first:last, :].rearrange("p c j -> p (c j)"), bank[:, : (last - first) * width])
-                if by_bank:
-                    nc.sync.dma_start(rows[:, first:last, :], result[:, first:last, :])
-            if not by_bank:
-                nc.sync.dma_start(rows, result[:])
+            for (first, last, bank), copy in zip(banks, copies):
+                copy(result[:, first:last, :].rearrange("p c j -> p (c j)"), bank[:, : (last - first) * width])
+            nc.sync.dma_start(rows, result[:])
 
-        upright_quadrature()
-        prepare_wi(UPRIGHT)
-        closing = list(UNITS[:-3]) + [(g, start, P) for start in (S - 2 * P, S - P) for g in range(GROUPS)]
-        waiting = None
-        for step in range(len(closing) + GAIN_LAG + 1):
-            if step == 1:
-                turned_quadrature()
-            if step < len(UNITS):
-                in_phase(*UNITS[step])
-            if step == 0:
-                prepare_wi(TURNED)
-            if 0 <= step - SUM_LAG < len(UNITS):
-                log_power(*UNITS[step - SUM_LAG])
-            if step == W2_STEP:
-                prepare_w2()
-            if 0 <= step - GAIN_LAG < len(closing):
-                apply_gain(*closing[step - GAIN_LAG])
-            if 0 <= step - GAIN_LAG - 1 < len(closing):
-                g, start, width = closing[step - GAIN_LAG - 1]
-                quantize_h(g, start, width)
-                if waiting is not None:
-                    features(*waiting)
-                    waiting = None
-                if g == TURNED and start == WIDE:
-                    waiting = (start, width)
-                elif g == TURNED:
-                    features(start, width)
+        by_scalar, by_vector = nc.scalar.copy, nc.vector.tensor_copy
+
+        W = WIDE
+        late_quadrature((3,))
+        for f in range(4):
+            upright_quadrature(0, BANK, f)
+        prepare_wi(EARLY)
+        for f in range(2):
+            upright_quadrature(BANK, W, f)
+        turned_quadrature(6)
+        turned_quadrature(7)
+        in_phase(EARLY, 0, W)
+        round_wi(LATE, 0)
+        quantize_wi(LATE, 0)
+        in_phase(EARLY, 3 * W, W)
+        round_wi(LATE, 1)
+        add_squares(0)
+        quantize_wi(LATE, 1)
+        in_phase(EARLY, W, W)
+        in_phase(EARLY, 2 * W, W)
+        log_power(EARLY, 3 * W, W)
+        round_w2(0)
+        add_squares(W)
+        log_power(EARLY, 0, W)
+        in_phase(LATE, 0, W)
+        round_w2(1)
+        in_phase(LATE, W, W)
+        apply_gain(EARLY, 0, W)
+        quantize_w2(0)
+        quantize_w2(1)
+        log_power(LATE, 0, W)
+        quantize_h(EARLY, 0, W)
+        add_squares(2 * W)
+        log_power(EARLY, W, W)
+        in_phase(LATE, 2 * W, W)
+        apply_gain(LATE, 0, W)
+        log_power(LATE, W, W)
+        apply_gain(EARLY, W, W)
+        quantize_h(LATE, 0, W)
+        quantize_h(EARLY, W, W)
+        log_power(EARLY, 2 * W, W)
+        apply_gain(LATE, W, W)
+        in_phase(LATE, 3 * W, W)
+        apply_gain(EARLY, 2 * W, W)
+        quantize_h(LATE, W, W)
+        log_power(LATE, 2 * W, W)
+        features(0, W, (by_scalar, by_scalar))
+        quantize_h(EARLY, 2 * W, W)
+        log_power(LATE, 3 * W, W)
+        features(W, W, (by_scalar, by_scalar))
+        apply_gain(LATE, 2 * W, W)
+        apply_gain(EARLY, 3 * W, P)
+        quantize_h(LATE, 2 * W, W)
+        features(2 * W, W, (by_scalar, by_scalar))
+        apply_gain(LATE, 3 * W, P)
+        quantize_h(EARLY, 3 * W, P)
+        apply_gain(EARLY, 3 * W + P, P)
+        quantize_h(LATE, 3 * W, P)
+        apply_gain(LATE, 3 * W + P, P)
+        quantize_h(EARLY, 3 * W + P, P)
+        features(3 * W, P, (by_scalar,))
+        quantize_h(LATE, 3 * W + P, P)
+        features(3 * W + P, P, (by_scalar, by_vector, by_scalar))

@@ -29,7 +29,7 @@ N_TILES = N // P
 RUN = 4
 WIDE = 256
 LATE, EARLY = 0, 1
-UPRIGHT_CELLS = 768
+UPRIGHT_CELLS = 1024
 RISING, FALLING = (0, 1), (1, 0)
 RING = 4
 LAST_GATHERS = (256, 256, 512)
@@ -44,23 +44,32 @@ def tile_list_radar_log_power_kernel(tc, tab_words, tab_scales, offs, wi, wq_wor
         psum = ctx.enter_context(tc.psum_pool(name="psum", bufs=1))
 
         made = {"bank": 0}
-        room = {"grouped": 4096, "squares": 4096, "h": 2048, "result": 3072, "piece": 512, "twin": 2048}
-        depth = {"grouped": RING, "squares": RING + GROUPS, "h": RING, "result": RING, "piece": N_TILES, "twin": 2}
+        turn = list(range(BANKS))
+        room = {"grouped": 4096, "spare": 2048, "late": 4096, "squares": 4096, "h": 2048, "result": 3072, "piece": 512, "twin": 2048}
+        depth = {"grouped": RING, "spare": 1, "late": S // WIDE, "squares": RING + GROUPS, "h": RING, "result": RING, "piece": N_TILES, "twin": 2}
         starts = {}
         for kind in room:
             starts[kind] = sum(room[other] * depth[other] for other in starts)
             made[kind] = 0
 
-        def next_bank():
+        def next_bank(for_good=False):
             n = made["bank"]
             made["bank"] = n + 1
-            return psum.tile([P, BANK], F32, name=f"bank{n}", offset=4 * BANK * (n % BANKS))
+            place = turn.pop(0)
+            if not for_good:
+                turn.append(place)
+            return psum.tile([P, BANK], F32, name=f"bank{n}", offset=4 * BANK * place)
+
+        def placed(name, shape, dtype, kind, slot, shift=0):
+            return ring.tile(shape, dtype, name=name, offset=starts[kind] + room[kind] * slot + shift, align_bytes=256)
+
+        def over_weights(name, shape, dtype, shift):
+            return staging.tile(shape, dtype, name=name, offset=raw_at + shift, align_bytes=256)
 
         def stream(kind, shape, dtype):
             n = made[kind]
             made[kind] = n + 1
-            at = starts[kind] + room[kind] * (n % depth[kind])
-            return ring.tile(shape, dtype, name=f"{kind}{n}", offset=at, align_bytes=256)
+            return placed(f"{kind}{n}", shape, dtype, kind, n % depth[kind])
 
         offsets = keep.tile([P, S // 16], U16, name="offsets")
         nc.sync.dma_start(offsets[:], offs)
@@ -107,6 +116,8 @@ def tile_list_radar_log_power_kernel(tc, tab_words, tab_scales, offs, wi, wq_wor
         v_planes = keep.tile([P, PASSES * S // 4], I32, name="v_planes", align_bytes=256)
         nc.vector.memset(v_planes[:], 0)
 
+        gains = keep.tile([P, P], F32, name="gains", align_bytes=256)
+        nc.vector.memset(gains[:], 0.0)
         picked_scales = keep.tile([P, S // 4], I32, name="picked_scales", align_bytes=256)
         nc.vector.tensor_copy(picked_scales[:].bitcast(U8), scale_window[:].bitcast(U8).indirect(offsets[:]))
         for quad in range(4):
@@ -155,8 +166,10 @@ def tile_list_radar_log_power_kernel(tc, tab_words, tab_scales, offs, wi, wq_wor
         )
         gain_turned = keep.tile([P, P], F32, name="gain_turned", align_bytes=256)
         nc.vector.transpose(gain_turned[:], gain_sorted[:])
-        gains = keep.tile([P, GROUPS, PACK], F32, name="gains")
-        nc.vector.tensor_copy(gains[:], gain_turned[:].rearrange("p (t g x) -> p g t x", t=PACK, g=GROUPS)[:, :, :, 0])
+        nc.vector.tensor_copy(
+            gains[:, : GROUPS * PACK].rearrange("p (g t) -> p g t", g=GROUPS),
+            gain_turned[:].rearrange("p (t g x) -> p g t x", t=PACK, g=GROUPS)[:, :, :, 0],
+        )
         gather_words(1, table1, LAST_GATHERS)
         wq_sorted = keep.tile([P, PASSES, row], I32, name="wq_sorted", align_bytes=256)
         nc.vector.tensor_copy(
@@ -164,14 +177,13 @@ def tile_list_radar_log_power_kernel(tc, tab_words, tab_scales, offs, wi, wq_wor
             wq_early[:].rearrange("p a (s t w) -> p a t s w", t=PACK, w=2),
         )
 
-        power = {}
-        for g in range(GROUPS):
-            for half in range(HALVES):
-                power[g, half] = keep.tile([P, PACK * BANK], F32, name=f"power{g}_{half}")
+        early_power = [keep.tile([P, PACK * BANK], F32, name=f"early_power{half}") for half in range(HALVES)]
+        late_power = [placed(f"late_power{u}", [P, PACK * WIDE], F32, "late", u) for u in range(S // WIDE)]
 
         def power_of(g, start, width):
-            at = PACK * (start % BANK)
-            return power[g, start // BANK][:, at : at + PACK * width]
+            tile, cells = (early_power[start // BANK], BANK) if g == EARLY else (late_power[start // WIDE], WIDE)
+            at = PACK * (start % cells)
+            return tile[:, at : at + PACK * width]
 
         def planes_of(start, width):
             first = start % WIDE
@@ -268,8 +280,8 @@ def tile_list_radar_log_power_kernel(tc, tab_words, tab_scales, offs, wi, wq_wor
 
         squares = {}
 
-        def in_phase(g, start, width):
-            squares[g, start] = stream("squares", [P, PACK * width], F32)
+        def in_phase(g, start, width, slot):
+            squares[g, start] = placed(f"squares{g}_{start}", [P, PACK * width], F32, "squares", slot)
             per_bank = BANK // width
             for f in range(width // P):
                 bank = next_bank()
@@ -288,10 +300,9 @@ def tile_list_radar_log_power_kernel(tc, tab_words, tab_scales, offs, wi, wq_wor
 
         sums = {}
 
-        def add_squares(start):
-            at = starts["grouped"] + room["grouped"] * ((PASSES + start // WIDE) % RING)
-            sums[start] = ring.tile([P, PACK * WIDE], F32, name=f"sum{start}", offset=at, align_bytes=256)
-            nc.vector.tensor_tensor(sums[start][:], squares[EARLY, start][:], power_of(EARLY, start, WIDE), ALU.add)
+        def add_squares(start, adder, where, *place):
+            sums[start] = where(f"sum{start}", [P, PACK * WIDE], F32, *place)
+            adder.tensor_tensor(sums[start][:], squares[EARLY, start][:], power_of(EARLY, start, WIDE), ALU.add)
 
         def log_power(g, start, width):
             if upright(g, start):
@@ -320,13 +331,27 @@ def tile_list_radar_log_power_kernel(tc, tab_words, tab_scales, offs, wi, wq_wor
                     bias=1.0,
                 )
 
-        h_codes = [keep.tile([P, S], U32, name=f"h_codes{g}", align_bytes=256) for g in range(GROUPS)]
+        h_codes = {}
         h_scales = [keep.tile([P, S], U8, name=f"h_scales{g}", align_bytes=256) for g in range(GROUPS)]
         h_rounded = {}
 
-        def apply_gain(g, start, width):
-            h = stream("h", [P, PACK * width], BF16)
-            factor = gains[:, g, :]
+        held = {}
+
+        gain_lines = keep.tile([P, P], F32, name="gain_lines", align_bytes=256)
+
+        def turn_gains():
+            bank = next_bank()
+            nc.tensor.transpose(bank[:, :P], gains[:], identity[:])
+            nc.scalar.copy(gain_lines[:], bank[:, :P])
+
+        def place_gains():
+            held["gains"] = next_bank(for_good=True)
+            nc.tensor.transpose(held["gains"][:, :P], gain_lines[:], identity[:])
+
+        def apply_gain(g, start, width, place=None):
+            shape = [P, PACK * width]
+            h = over_weights(f"h{g}_{start}", shape, BF16, place) if place else stream("h", shape, BF16)
+            factor = held["gains"][:, g * PACK : (g + 1) * PACK]
             if upright(g, start):
                 nc.vector.tensor_tensor(
                     h[:].rearrange("p (c i t) -> p c t i", i=RUN, t=PACK),
@@ -343,20 +368,23 @@ def tile_list_radar_log_power_kernel(tc, tab_words, tab_scales, offs, wi, wq_wor
                 )
             h_rounded[g, start] = h
 
-        def quantize_h(g, start, width):
+        def quantize_h(g, start, width, place=None):
+            name = f"h_codes{g}_{start}"
+            codes = placed(name, [P, width], U32, *place) if place else keep.tile([P, width], U32, name=name, align_bytes=256)
+            for first in range(0, width, P):
+                h_codes[g, start + first] = codes[:, first:]
             nc.vector.quantize_mx(
-                out=h_codes[g][:, start : start + width].bitcast(FP8X4),
+                out=codes[:].bitcast(FP8X4),
                 scales=h_scales[g][:, start : start + width],
                 in_=h_rounded[g, start][:],
             )
 
         w2_grouped = {}
-        w2_codes = keep.tile([P, GROUPS * N], U32, name="w2_codes", align_bytes=256)
+        w2_codes = over_weights("w2_codes", [P, GROUPS * N], U32, 8192)
         w2_scales = keep.tile([P, GROUPS * N], U8, name="w2_scales", align_bytes=256)
 
         def round_w2(g):
-            at = starts["squares"] + room["squares"] * g
-            w2_grouped[g] = ring.tile([P, PACK * N], BF16, name=f"w2_grouped{g}", offset=at, align_bytes=256)
+            w2_grouped[g] = placed(f"w2_grouped{g}", [P, PACK * N], BF16, "squares", g)
             nc.vector.tensor_copy(
                 w2_grouped[g][:].rearrange("p (c i j) -> p c j i", i=RUN, j=PACK),
                 w2_raw[g].rearrange("p (j c i) -> p c j i", j=PACK, i=RUN),
@@ -382,7 +410,7 @@ def tile_list_radar_log_power_kernel(tc, tab_words, tab_scales, offs, wi, wq_wor
                             out=bank[:, (c - first) * width : (c - first + 1) * width],
                             lhsT=w2_codes[:, col : col + P].bitcast(FP8X4),
                             lhsT_scale=w2_scales[:, col : col + P],
-                            rhs=h_codes[g][:, start : start + width].bitcast(FP8X4),
+                            rhs=h_codes[g, start][:, :width].bitcast(FP8X4),
                             rhs_scale=h_scales[g][:, start : start + width],
                             start=(n == 0 and c == first),
                             stop=(n == GROUPS - 1 and c == last - 1),
@@ -406,59 +434,55 @@ def tile_list_radar_log_power_kernel(tc, tab_words, tab_scales, offs, wi, wq_wor
         for f in range(4):
             upright_quadrature(0, BANK, f)
         prepare_wi(EARLY)
-        for f in range(2):
-            upright_quadrature(BANK, W, f)
-        turned_quadrature(6)
-        turned_quadrature(7)
-        in_phase(EARLY, 0, W)
-        round_wi(LATE, 0)
-        quantize_wi(LATE, 0)
-        in_phase(EARLY, 3 * W, W)
-        round_wi(LATE, 1)
-        add_squares(0)
-        quantize_wi(LATE, 1)
-        in_phase(EARLY, W, W)
-        in_phase(EARLY, 2 * W, W)
-        log_power(EARLY, 3 * W, W)
+        for f in range(4):
+            upright_quadrature(BANK, BANK, f)
+        in_phase(EARLY, 0, W, 0)
+        prepare_wi(LATE)
+        in_phase(EARLY, W, W, 1)
+        in_phase(EARLY, 2 * W, W, 2)
+        add_squares(0, nc.vector, placed, "grouped", 3, -2048)
+        in_phase(EARLY, 3 * W, W, 3)
+        add_squares(W, nc.vector, placed, "grouped", 3, 2048)
+        turn_gains()
         round_w2(0)
-        add_squares(W)
+        in_phase(LATE, 0, W, 4)
         log_power(EARLY, 0, W)
-        in_phase(LATE, 0, W)
         round_w2(1)
-        in_phase(LATE, W, W)
-        apply_gain(EARLY, 0, W)
+        in_phase(LATE, W, W, 5)
         quantize_w2(0)
         quantize_w2(1)
+        add_squares(2 * W, nc.gpsimd, placed, "squares", 0)
+        place_gains()
         log_power(LATE, 0, W)
-        quantize_h(EARLY, 0, W)
-        add_squares(2 * W)
         log_power(EARLY, W, W)
-        in_phase(LATE, 2 * W, W)
+        apply_gain(EARLY, 0, W, 3072)
         apply_gain(LATE, 0, W)
-        log_power(LATE, W, W)
-        apply_gain(EARLY, W, W)
+        in_phase(LATE, 2 * W, W, 1)
+        quantize_h(EARLY, 0, W, ("late", 0))
         quantize_h(LATE, 0, W)
-        quantize_h(EARLY, W, W)
+        add_squares(3 * W, nc.gpsimd, over_weights, 0)
         log_power(EARLY, 2 * W, W)
-        apply_gain(LATE, W, W)
-        in_phase(LATE, 3 * W, W)
+        log_power(LATE, W, W)
+        apply_gain(EARLY, W, W, 4096)
         apply_gain(EARLY, 2 * W, W)
+        in_phase(LATE, 3 * W, W, 4)
+        apply_gain(LATE, W, W)
+        quantize_h(EARLY, W, W, ("squares", 0))
+        quantize_h(EARLY, 2 * W, W)
         quantize_h(LATE, W, W)
+        log_power(EARLY, 3 * W, W)
         log_power(LATE, 2 * W, W)
         features(0, W, (by_scalar, by_scalar))
-        quantize_h(EARLY, 2 * W, W)
-        log_power(LATE, 3 * W, W)
-        features(W, W, (by_scalar, by_scalar))
+        apply_gain(EARLY, 3 * W, W)
         apply_gain(LATE, 2 * W, W)
-        apply_gain(EARLY, 3 * W, P)
+        log_power(LATE, 3 * W, W)
         quantize_h(LATE, 2 * W, W)
-        features(2 * W, W, (by_scalar, by_scalar))
+        quantize_h(EARLY, 3 * W, W)
+        features(W, W, (by_scalar, by_scalar))
         apply_gain(LATE, 3 * W, P)
-        quantize_h(EARLY, 3 * W, P)
-        apply_gain(EARLY, 3 * W + P, P)
-        quantize_h(LATE, 3 * W, P)
+        features(2 * W, W, (by_scalar, by_scalar))
         apply_gain(LATE, 3 * W + P, P)
-        quantize_h(EARLY, 3 * W + P, P)
-        features(3 * W, P, (by_scalar,))
+        quantize_h(LATE, 3 * W, P)
         quantize_h(LATE, 3 * W + P, P)
+        features(3 * W, P, (by_scalar,))
         features(3 * W + P, P, (by_scalar, by_vector, by_scalar))

@@ -29,10 +29,10 @@ N_TILES = N // P
 RUN = 4
 WIDE = 256
 LATE, EARLY = 0, 1
-UPRIGHT_CELLS = 1024
 RISING, FALLING = (0, 1), (1, 0)
+VECTOR_BANK = 3
 RING = 4
-LAST_GATHERS = (256, 256, 512)
+LAST_GATHER = 256
 
 
 def tile_list_radar_log_power_kernel(tc, tab_words, tab_scales, offs, wi, wq_words, wq_scales, gain, w2, out):
@@ -45,17 +45,17 @@ def tile_list_radar_log_power_kernel(tc, tab_words, tab_scales, offs, wi, wq_wor
 
         made = {"bank": 0}
         turn = list(range(BANKS))
-        room = {"grouped": 4096, "spare": 2048, "late": 4096, "squares": 4096, "h": 2048, "result": 3072, "piece": 512, "twin": 2048}
-        depth = {"grouped": RING, "spare": 1, "late": S // WIDE, "squares": RING + GROUPS, "h": RING, "result": RING, "piece": N_TILES, "twin": 2}
+        room = {"grouped": 4096, "spare": 2048, "late": 4096, "logs": 4096, "squares": 4096, "h": 2048, "result": 3072, "piece": 512, "twin": 2048}
+        depth = {"grouped": RING, "spare": 1, "late": S // WIDE, "logs": 2, "squares": RING + GROUPS, "h": RING, "result": RING + 1, "piece": N_TILES, "twin": 2}
         starts = {}
         for kind in room:
             starts[kind] = sum(room[other] * depth[other] for other in starts)
             made[kind] = 0
 
-        def next_bank(for_good=False):
+        def next_bank(for_good=False, back=BANKS):
             n = made["bank"]
             made["bank"] = n + 1
-            place = turn.pop(0)
+            place = turn.pop(max(0, len(turn) - back))
             if not for_good:
                 turn.append(place)
             return psum.tile([P, BANK], F32, name=f"bank{n}", offset=4 * BANK * place)
@@ -64,7 +64,7 @@ def tile_list_radar_log_power_kernel(tc, tab_words, tab_scales, offs, wi, wq_wor
             return ring.tile(shape, dtype, name=name, offset=starts[kind] + room[kind] * slot + shift, align_bytes=256)
 
         def over_weights(name, shape, dtype, shift):
-            return staging.tile(shape, dtype, name=name, offset=raw_at + shift, align_bytes=256)
+            return staging.tile(shape, dtype, name=name, offset=shift, align_bytes=256)
 
         def stream(kind, shape, dtype):
             n = made[kind]
@@ -75,7 +75,7 @@ def tile_list_radar_log_power_kernel(tc, tab_words, tab_scales, offs, wi, wq_wor
         nc.sync.dma_start(offsets[:], offs)
 
         piece = PACK * K_PASS
-        w2_at = GROUPS * PASSES * piece
+        w2_at = (GROUPS * PASSES - 1) * piece
         raw_columns = w2_at + GROUPS * PACK * N
         table0_at = 0
         raw_at = table0_at + 4 * T - 256
@@ -110,14 +110,13 @@ def tile_list_radar_log_power_kernel(tc, tab_words, tab_scales, offs, wi, wq_wor
         make_identity(nc, identity[:])
         zero = keep.tile([P, 1], F32, name="zero")
         nc.scalar.activation(zero[:], one[:], ACT.Ln)
-        gain_rows = keep.tile([P, P], F32, name="gain_rows", align_bytes=256)
-        nc.vector.memset(gain_rows[:], 0.0)
-        nc.sync.dma_start(gain_rows[0:P:16, :], gain.rearrange("(g b c) -> b g c", g=GROUPS, c=P))
         v_planes = keep.tile([P, PASSES * S // 4], I32, name="v_planes", align_bytes=256)
         nc.vector.memset(v_planes[:], 0)
 
-        gains = keep.tile([P, P], F32, name="gains", align_bytes=256)
-        nc.vector.memset(gains[:], 0.0)
+        ones = [placed("one_again", [P, 1], F32, "logs", 0)]
+        nc.vector.memset(ones[0][:], 1.0)
+        zero_again = placed("zero_again", [P, 1], F32, "logs", 1)
+        nc.vector.memset(zero_again[:], 0.0)
         picked_scales = keep.tile([P, S // 4], I32, name="picked_scales", align_bytes=256)
         nc.vector.tensor_copy(picked_scales[:].bitcast(U8), scale_window[:].bitcast(U8).indirect(offsets[:]))
         for quad in range(4):
@@ -129,13 +128,23 @@ def tile_list_radar_log_power_kernel(tc, tab_words, tab_scales, offs, wi, wq_wor
         nc.sync.dma_start(wq_early[:], wq_rows[:, :, row:])
 
         raw = staging.tile([P, raw_columns], F32, name="raw", offset=raw_at, align_bytes=256)
+        last_at = table0_at + 4 * row * (1 + PASSES)
+        last_piece = staging.tile([P, piece], F32, name="last_piece", offset=last_at, align_bytes=256)
         wi_raw = {}
         for n, g in enumerate((EARLY, LATE)):
             for a in range(PASSES):
                 at = (n * PASSES + a) * piece
-                wi_raw[g, a] = raw[:, at : at + piece].rearrange("p (j c) -> p j c", j=PACK)
+                values = raw[:, at : at + piece] if at < w2_at else last_piece[:]
+                wi_raw[g, a] = values.rearrange("p (j c) -> p j c", j=PACK)
                 rows = wi[a * K_PASS : (a + 1) * K_PASS, g * K_PASS : (g + 1) * K_PASS]
                 nc.sync.dma_start(wi_raw[g, a], rows.rearrange("(p j) c -> p j c", j=PACK))
+        gain_lines = staging.tile([P, P], F32, name="gain_lines", offset=last_at + 4 * piece, align_bytes=256)
+        nc.vector.memset(gain_lines[:], 0.0)
+        for g in range(GROUPS):
+            nc.sync.dma_start(
+                gain_lines[PACK * g : PACK * (g + 1), :].rearrange("t (s i) -> t s i", i=RUN),
+                gain[g * K_PASS : (g + 1) * K_PASS].rearrange("(s t i) -> t s i", t=PACK, i=RUN),
+            )
         w2_raw = [raw[:, w2_at + g * PACK * N : w2_at + (g + 1) * PACK * N] for g in range(GROUPS)]
         for g in range(GROUPS):
             rows = w2[g * K_PASS : (g + 1) * K_PASS, :].rearrange("(s t i) n -> t s i n", t=PACK, i=RUN)
@@ -144,38 +153,31 @@ def tile_list_radar_log_power_kernel(tc, tab_words, tab_scales, offs, wi, wq_wor
 
         v_codes = [keep.tile([P, S], U32, name=f"v_codes{a}", align_bytes=256) for a in range(PASSES)]
 
-        def gather_words(a, table, counts):
-            first = 0
-            for count in counts:
+        def gather_words(a, table, runs):
+            for first, count in runs:
                 nc.vector.tensor_copy(
                     v_codes[a][:, first : first + count],
                     table[:].bitcast(U32).indirect(offsets[:, first // 16 : (first + count) // 16]),
                 )
-                first = first + count
 
-        wq_planes = keep.tile([P, PASSES, K_PASS // 4], I32, name="wq_planes", align_bytes=256)
+        wq_planes = keep.tile([P, PASSES, GROUPS, K_PASS // 4], I32, name="wq_planes", align_bytes=256)
         nc.vector.tensor_copy(
-            wq_planes[:].rearrange("p a (t s) -> p a t s", t=PACK),
-            wq_scale_rows[:, :, P:].rearrange("p a (s t) -> p a t s", t=PACK),
+            wq_planes[:].rearrange("p a g (t s) -> p (a g) t s", t=PACK),
+            wq_scale_rows[:].rearrange("p a (g s t) -> p (a g) t s", g=GROUPS, t=PACK),
         )
-        gather_words(0, table0, (BANK, BANK))
-        gain_sorted = keep.tile([P, P], F32, name="gain_sorted", align_bytes=256)
-        nc.vector.tensor_copy(
-            gain_sorted[:].rearrange("p (t s i) -> p t s i", t=PACK, i=RUN),
-            gain_rows[:].rearrange("p (s t i) -> p t s i", t=PACK, i=RUN),
-        )
-        gain_turned = keep.tile([P, P], F32, name="gain_turned", align_bytes=256)
-        nc.vector.transpose(gain_turned[:], gain_sorted[:])
-        nc.vector.tensor_copy(
-            gains[:, : GROUPS * PACK].rearrange("p (g t) -> p g t", g=GROUPS),
-            gain_turned[:].rearrange("p (t g x) -> p g t x", t=PACK, g=GROUPS)[:, :, :, 0],
-        )
-        gather_words(1, table1, LAST_GATHERS)
-        wq_sorted = keep.tile([P, PASSES, row], I32, name="wq_sorted", align_bytes=256)
-        nc.vector.tensor_copy(
-            wq_sorted[:].rearrange("p a (t s w) -> p a t s w", t=PACK, w=2),
-            wq_early[:].rearrange("p a (s t w) -> p a t s w", t=PACK, w=2),
-        )
+        wq_sorted = {}
+
+        def sort_words(g, a, words):
+            wq_sorted[g, a] = keep.tile([P, row], I32, name=f"wq_sorted{g}_{a}", align_bytes=256)
+            nc.vector.tensor_copy(
+                wq_sorted[g, a][:].rearrange("p (t s w) -> p t s w", t=PACK, w=2),
+                words.rearrange("p (s t w) -> p t s w", t=PACK, w=2),
+            )
+
+        gather_words(0, table0, ((0, BANK), (BANK, BANK)))
+        gather_words(1, table1, [(first, LAST_GATHER) for first in range(0, S, LAST_GATHER)])
+        for a in range(PASSES):
+            sort_words(EARLY, a, wq_early[:, a, :])
 
         early_power = [keep.tile([P, PACK * BANK], F32, name=f"early_power{half}") for half in range(HALVES)]
         late_power = [placed(f"late_power{u}", [P, PACK * WIDE], F32, "late", u) for u in range(S // WIDE)]
@@ -185,20 +187,20 @@ def tile_list_radar_log_power_kernel(tc, tab_words, tab_scales, offs, wi, wq_wor
             at = PACK * (start % cells)
             return tile[:, at : at + PACK * width]
 
-        def planes_of(start, width):
+        def planes_of(tiles, g, start, width):
             first = start % WIDE
-            unit = sums[start - first][:].rearrange("p (t j) -> p t j", t=PACK)
+            unit = tiles[g, start - first][:].rearrange("p (t j) -> p t j", t=PACK)
             return unit[:, :, first : first + width]
 
-        def plane_pass(out_view, a, codes, scales, start, width, order):
+        def plane_pass(out_view, a, codes, scales, start, width, flags):
             nc.tensor.matmul_mx(
                 out=out_view,
                 lhsT=codes,
                 lhsT_scale=scales,
                 rhs=v_codes[a][:, start : start + width].bitcast(FP8X4),
                 rhs_scale=v_scales[:, a * S + start : a * S + start + width],
-                start=(a == order[0]),
-                stop=(a == order[-1]),
+                start=flags[0],
+                stop=flags[1],
             )
 
         def cells_pass(bank, a, codes, scales, start, order):
@@ -214,48 +216,57 @@ def tile_list_radar_log_power_kernel(tc, tab_words, tab_scales, offs, wi, wq_wor
 
         def square(squared, bank, pattern, sizes, on_vector=False, bias=0.0):
             values = bank[:].rearrange(pattern, **sizes)
-            if on_vector:
-                twin = stream("twin", [P, BANK], F32)
-                nc.vector.tensor_copy(twin[:], bank[:])
-                nc.vector.tensor_tensor(squared, values, twin[:].rearrange(pattern, **sizes), ALU.mult)
-            else:
+            if not on_vector:
                 nc.scalar.activation(squared, values, ACT.Square, bias=bias)
+                return
+            twin = stream("twin", [P, BANK], F32)
+            fillers.append(lambda: nc.vector.tensor_copy(twin[:], bank[:]))
+            copied = twin[:].rearrange(pattern, **sizes)
+            fillers.append(lambda: nc.vector.tensor_tensor(squared, copied, copied, ALU.mult))
+
+        fillers = []
+        quadrature = {}
 
         def upright(g, start):
-            return g == EARLY and start < UPRIGHT_CELLS
+            return g == EARLY
 
         def square_turned(g, n, bank, on_vector, bias=0.0):
-            squared = power_of(g, n * P, P).rearrange("p (t s i) -> p t s i", t=PACK, i=RUN)
+            if on_vector:
+                quadrature[n] = placed("vector_squares", [P, BANK], F32, "grouped", 1)[:]
+            else:
+                quadrature[n] = power_of(g, n * P, P)
+            squared = quadrature[n].rearrange("p (t s i) -> p t s i", t=PACK, i=RUN)
             square(squared, bank, "p (s t i) -> p t s i", {"t": PACK, "i": RUN}, on_vector, bias)
 
-        def late_quadrature(on_vector):
+        def quadrature_pass(g, a, bank, start, width, f):
+            per_bank = BANK // width
+            for n in range(per_bank):
+                t = per_bank * f + n
+                codes = wq_sorted[g, a][:].bitcast(U8)[:, 2 * t * P : 2 * (t + 1) * P].bitcast(FP4X4)
+                scales = wq_planes[:, a, g, :].bitcast(U8)[:, t * P : (t + 1) * P]
+                flags = (a == 0 and n == 0, a == PASSES - 1 and n == per_bank - 1)
+                plane_pass(bank[:, n * width : (n + 1) * width], a, codes, scales, start, width, flags)
+
+        def square_upright(g, bank, start, width, f, on_vector=False):
+            per_bank = BANK // width
+            units = power_of(g, start, width).rearrange("p (u t j) -> p u t j", t=PACK, j=WIDE)
+            squared = units[:, :, per_bank * f : per_bank * (f + 1), :]
+            square(squared, bank, "p (u t j) -> p u t j", {"t": per_bank, "j": WIDE}, on_vector)
+
+        def late_quadrature():
             banks = [next_bank() for n in range(S // P)]
             for a in range(PASSES):
                 for n, bank in enumerate(banks):
                     codes = wq_late[a][:].bitcast(U8).bitcast(FP4X4)
                     cells_pass(bank, a, codes, wq_scale_rows[:, a, :P].bitcast(U8), n * P, RISING)
                     if a == PASSES - 1:
-                        square_turned(LATE, n, bank, n in on_vector, zero[:] if n == 0 else 0.0)
+                        square_turned(LATE, n, bank, n == VECTOR_BANK, zero[:] if n == 0 else 0.0)
 
-        def turned_quadrature(n, on_vector=False):
+        def early_quadrature(start, f, on_vector=False):
             bank = next_bank()
             for a in range(PASSES):
-                codes = wq_early[:, a, :].bitcast(U8).bitcast(FP4X4)
-                cells_pass(bank, a, codes, wq_scale_rows[:, a, P:].bitcast(U8), n * P, RISING)
-            square_turned(EARLY, n, bank, on_vector)
-
-        def upright_quadrature(start, width, f, on_vector=False):
-            bank = next_bank()
-            per_bank = BANK // width
-            for n in range(per_bank):
-                t = per_bank * f + n
-                for a in range(PASSES):
-                    codes = wq_sorted[:, a, :].bitcast(U8)[:, 2 * t * P : 2 * (t + 1) * P].bitcast(FP4X4)
-                    scales = wq_planes[:, a, :].bitcast(U8)[:, t * P : (t + 1) * P]
-                    plane_pass(bank[:, n * width : (n + 1) * width], a, codes, scales, start, width, RISING)
-            units = power_of(EARLY, start, width).rearrange("p (u t j) -> p u t j", t=PACK, j=WIDE)
-            squared = units[:, :, per_bank * f : per_bank * (f + 1), :]
-            square(squared, bank, "p (u t j) -> p u t j", {"t": per_bank, "j": WIDE}, on_vector)
+                quadrature_pass(EARLY, a, bank, start, BANK, f)
+            square_upright(EARLY, bank, start, BANK, f, on_vector)
 
         wi_codes = {}
         wi_scales = {}
@@ -280,7 +291,7 @@ def tile_list_radar_log_power_kernel(tc, tab_words, tab_scales, offs, wi, wq_wor
 
         squares = {}
 
-        def in_phase(g, start, width, slot):
+        def in_phase(g, start, width, slot, bias=0.0):
             squares[g, start] = placed(f"squares{g}_{start}", [P, PACK * width], F32, "squares", slot)
             per_bank = BANK // width
             for f in range(width // P):
@@ -292,29 +303,34 @@ def tile_list_radar_log_power_kernel(tc, tab_words, tab_scales, offs, wi, wq_wor
                         for a in FALLING:
                             codes = wi_codes[g, a][:, t * P : (t + 1) * P].bitcast(FP8X4)
                             scales = wi_scales[g, a][:, t * P : (t + 1) * P]
-                            plane_pass(bank[:, n * width : (n + 1) * width], a, codes, scales, start, width, FALLING)
+                            plane_pass(bank[:, n * width : (n + 1) * width], a, codes, scales, start, width, (a == FALLING[0], a == FALLING[-1]))
                 else:
                     for a in FALLING:
                         cells_pass(bank, a, wi_codes[g, a][:].bitcast(FP8X4), wi_scales[g, a][:], start + f * P, FALLING)
-                nc.scalar.activation(squared, bank[:], ACT.Square, bias=0.0)
+                nc.scalar.activation(squared, bank[:], ACT.Square, bias=bias if f == 0 else 0.0)
 
         sums = {}
+        logs = {}
 
-        def add_squares(start, adder, where, *place):
-            sums[start] = where(f"sum{start}", [P, PACK * WIDE], F32, *place)
-            adder.tensor_tensor(sums[start][:], squares[EARLY, start][:], power_of(EARLY, start, WIDE), ALU.add)
+        def add_squares(g, start, adder, where, *place):
+            sums[g, start] = where(f"sum{g}_{start}", [P, PACK * WIDE], F32, *place)
+            adder.tensor_tensor(sums[g, start][:], squares[g, start][:], power_of(g, start, WIDE), ALU.add)
 
-        def log_power(g, start, width):
+        def log_power(g, start, width, where=None, *place, bias=1.0):
             if upright(g, start):
-                total = planes_of(start, width)
-                nc.scalar.activation(total, total, ACT.Ln, bias=1.0)
+                unit = (g, start - start % WIDE)
+                if where:
+                    logs[unit] = where(f"log{g}_{start}", [P, PACK * WIDE], F32, *place)
+                logs.setdefault(unit, sums[unit])
+                nc.scalar.activation(planes_of(logs, g, start, width), planes_of(sums, g, start, width), ACT.Ln, bias=1.0)
                 return
             total = power_of(g, start, width)
             banks = [next_bank() for f in range(width // P)]
             for f, bank in enumerate(banks):
                 for t in range(PACK):
-                    cols = slice(f * BANK + t * P, f * BANK + (t + 1) * P)
-                    for n, term in enumerate((squares[g, start], total)):
+                    cols = slice(t * P, (t + 1) * P)
+                    terms = (squares[g, start][:, f * BANK : (f + 1) * BANK], quadrature[start // P + f])
+                    for n, term in enumerate(terms):
                         nc.tensor.matmul(
                             bank[:, t * P : (t + 1) * P],
                             term[:, cols],
@@ -328,7 +344,7 @@ def tile_list_radar_log_power_kernel(tc, tab_words, tab_scales, offs, wi, wq_wor
                     total[:, f * BANK : (f + 1) * BANK].rearrange("p (j t) -> p j t", t=PACK),
                     bank[:].rearrange("p (t j) -> p j t", t=PACK),
                     ACT.Ln,
-                    bias=1.0,
+                    bias=bias if f == 0 else 1.0,
                 )
 
         h_codes = {}
@@ -337,25 +353,18 @@ def tile_list_radar_log_power_kernel(tc, tab_words, tab_scales, offs, wi, wq_wor
 
         held = {}
 
-        gain_lines = keep.tile([P, P], F32, name="gain_lines", align_bytes=256)
-
-        def turn_gains():
-            bank = next_bank()
-            nc.tensor.transpose(bank[:, :P], gains[:], identity[:])
-            nc.scalar.copy(gain_lines[:], bank[:, :P])
-
         def place_gains():
             held["gains"] = next_bank(for_good=True)
             nc.tensor.transpose(held["gains"][:, :P], gain_lines[:], identity[:])
 
         def apply_gain(g, start, width, place=None):
             shape = [P, PACK * width]
-            h = over_weights(f"h{g}_{start}", shape, BF16, place) if place else stream("h", shape, BF16)
+            h = over_weights(f"h{g}_{start}", shape, BF16, place) if place is not None else stream("h", shape, BF16)
             factor = held["gains"][:, g * PACK : (g + 1) * PACK]
             if upright(g, start):
                 nc.vector.tensor_tensor(
                     h[:].rearrange("p (c i t) -> p c t i", i=RUN, t=PACK),
-                    planes_of(start, width).rearrange("p t (c i) -> p c t i", i=RUN),
+                    planes_of(logs, g, start, width).rearrange("p t (c i) -> p c t i", i=RUN),
                     factor.unsqueeze(1).unsqueeze(3).to_broadcast([P, width // RUN, PACK, RUN]),
                     ALU.mult,
                 )
@@ -370,7 +379,12 @@ def tile_list_radar_log_power_kernel(tc, tab_words, tab_scales, offs, wi, wq_wor
 
         def quantize_h(g, start, width, place=None):
             name = f"h_codes{g}_{start}"
-            codes = placed(name, [P, width], U32, *place) if place else keep.tile([P, width], U32, name=name, align_bytes=256)
+            if place is None:
+                codes = keep.tile([P, width], U32, name=name, align_bytes=256)
+            elif isinstance(place, int):
+                codes = over_weights(name, [P, width], U32, place)
+            else:
+                codes = placed(name, [P, width], U32, *place)
             for first in range(0, width, P):
                 h_codes[g, start + first] = codes[:, first:]
             nc.vector.quantize_mx(
@@ -380,7 +394,7 @@ def tile_list_radar_log_power_kernel(tc, tab_words, tab_scales, offs, wi, wq_wor
             )
 
         w2_grouped = {}
-        w2_codes = over_weights("w2_codes", [P, GROUPS * N], U32, 8192)
+        w2_codes = keep.tile([P, GROUPS * N], U32, name="w2_codes", align_bytes=256)
         w2_scales = keep.tile([P, GROUPS * N], U8, name="w2_scales", align_bytes=256)
 
         def round_w2(g):
@@ -399,9 +413,11 @@ def tile_list_radar_log_power_kernel(tc, tab_words, tab_scales, offs, wi, wq_wor
 
         out_rows = out.rearrange("(c p) j -> p c j", p=P)
 
-        def features(start, width, copies, earlier=EARLY):
+        summed = {}
+
+        def features(start, width, earlier=EARLY, back=BANKS):
             per_bank = 1 if start + width == S else BANK // width
-            banks = [(first, min(first + per_bank, N_TILES), next_bank()) for first in range(0, N_TILES, per_bank)]
+            banks = [(first, min(first + per_bank, N_TILES), next_bank(back=back)) for first in range(0, N_TILES, per_bank)]
             for n, g in enumerate((earlier, 1 - earlier)):
                 for first, last, bank in banks:
                     for c in range(first, last):
@@ -415,6 +431,16 @@ def tile_list_radar_log_power_kernel(tc, tab_words, tab_scales, offs, wi, wq_wor
                             start=(n == 0 and c == first),
                             stop=(n == GROUPS - 1 and c == last - 1),
                         )
+            summed[start] = banks
+
+        def store_bank(start, width, n, copy):
+            first, last, bank = summed[start][n]
+            result = stream("result", [P, last - first, width], F32)
+            copy(result[:].rearrange("p c j -> p (c j)"), bank[:, : (last - first) * width])
+            nc.sync.dma_start(out_rows[:, first:last, start : start + width], result[:])
+
+        def store(start, width, copies):
+            banks = summed[start]
             rows = out_rows[:, :, start : start + width]
             if start + width == S:
                 for (first, last, bank), copy in zip(banks, copies):
@@ -430,59 +456,69 @@ def tile_list_radar_log_power_kernel(tc, tab_words, tab_scales, offs, wi, wq_wor
         by_scalar, by_vector = nc.scalar.copy, nc.vector.tensor_copy
 
         W = WIDE
-        late_quadrature((3,))
+        late_quadrature()
+        fillers.pop(0)()
         for f in range(4):
-            upright_quadrature(0, BANK, f)
+            early_quadrature(0, f)
         prepare_wi(EARLY)
         for f in range(4):
-            upright_quadrature(BANK, BANK, f)
+            early_quadrature(BANK, f)
         in_phase(EARLY, 0, W, 0)
-        prepare_wi(LATE)
+        round_wi(LATE, 0)
+        fillers.pop(0)()
+        quantize_wi(LATE, 0)
+        round_wi(LATE, 1)
+        quantize_wi(LATE, 1)
         in_phase(EARLY, W, W, 1)
         in_phase(EARLY, 2 * W, W, 2)
-        add_squares(0, nc.vector, placed, "grouped", 3, -2048)
+        add_squares(EARLY, 0, nc.vector, placed, "grouped", 3, -2048)
         in_phase(EARLY, 3 * W, W, 3)
-        add_squares(W, nc.vector, placed, "grouped", 3, 2048)
-        turn_gains()
+        add_squares(EARLY, W, nc.vector, placed, "grouped", 3, 2048)
         round_w2(0)
         in_phase(LATE, 0, W, 4)
         log_power(EARLY, 0, W)
         round_w2(1)
+        log_power(EARLY, W, W)
         in_phase(LATE, W, W, 5)
         quantize_w2(0)
         quantize_w2(1)
-        add_squares(2 * W, nc.gpsimd, placed, "squares", 0)
+        add_squares(EARLY, 2 * W, nc.gpsimd, placed, "squares", 1)
         place_gains()
         log_power(LATE, 0, W)
-        log_power(EARLY, W, W)
-        apply_gain(EARLY, 0, W, 3072)
+        apply_gain(EARLY, 0, W, raw_at + 8192)
+        apply_gain(EARLY, W, W, raw_at + 3072)
         apply_gain(LATE, 0, W)
-        in_phase(LATE, 2 * W, W, 1)
+        in_phase(LATE, 2 * W, W, 0)
         quantize_h(EARLY, 0, W, ("late", 0))
+        quantize_h(EARLY, W, W, ("late", 0, 1024))
         quantize_h(LATE, 0, W)
-        add_squares(3 * W, nc.gpsimd, over_weights, 0)
-        log_power(EARLY, 2 * W, W)
-        log_power(LATE, W, W)
-        apply_gain(EARLY, W, W, 4096)
-        apply_gain(EARLY, 2 * W, W)
-        in_phase(LATE, 3 * W, W, 4)
-        apply_gain(LATE, W, W)
-        quantize_h(EARLY, W, W, ("squares", 0))
-        quantize_h(EARLY, 2 * W, W)
-        quantize_h(LATE, W, W)
-        log_power(EARLY, 3 * W, W)
+        add_squares(EARLY, 3 * W, nc.gpsimd, over_weights, raw_at)
+        log_power(LATE, W, W, bias=ones[0][:])
+        log_power(EARLY, 2 * W, W, placed, "logs", 0)
         log_power(LATE, 2 * W, W)
-        features(0, W, (by_scalar, by_scalar))
-        apply_gain(EARLY, 3 * W, W)
+        in_phase(LATE, 3 * W, W, 4, zero_again[:])
+        apply_gain(LATE, W, W, raw_at + 4096)
+        apply_gain(EARLY, 2 * W, W)
         apply_gain(LATE, 2 * W, W)
-        log_power(LATE, 3 * W, W)
+        features(0, W)
+        quantize_h(LATE, W, W, ("late", 2))
+        quantize_h(EARLY, 2 * W, W, ("late", 2, 1024))
         quantize_h(LATE, 2 * W, W)
-        quantize_h(EARLY, 3 * W, W)
-        features(W, W, (by_scalar, by_scalar))
+        store_bank(0, W, 0, by_scalar)
+        log_power(EARLY, 3 * W, W, placed, "logs", 1)
+        store_bank(0, W, 1, by_scalar)
+        log_power(LATE, 3 * W, W)
+        apply_gain(EARLY, 3 * W, W, raw_at + 4096)
+        features(W, W)
+        store(W, W, (by_scalar, by_scalar))
         apply_gain(LATE, 3 * W, P)
-        features(2 * W, W, (by_scalar, by_scalar))
+        features(2 * W, W)
+        store(2 * W, W, (by_scalar, by_scalar))
+        quantize_h(EARLY, 3 * W, W)
         apply_gain(LATE, 3 * W + P, P)
         quantize_h(LATE, 3 * W, P)
         quantize_h(LATE, 3 * W + P, P)
-        features(3 * W, P, (by_scalar,))
-        features(3 * W + P, P, (by_scalar, by_vector, by_scalar))
+        features(3 * W, P)
+        store(3 * W, P, (by_vector,))
+        features(3 * W + P, P)
+        store(3 * W + P, P, (by_scalar, by_scalar, by_vector))

@@ -113,10 +113,9 @@ def tile_list_radar_log_power_kernel(tc, tab_words, tab_scales, offs, wi, wq_wor
         v_planes = keep.tile([P, PASSES * S // 4], I32, name="v_planes", align_bytes=256)
         nc.vector.memset(v_planes[:], 0)
 
-        ones = [placed("one_again", [P, 1], F32, "logs", 0)]
-        nc.vector.memset(ones[0][:], 1.0)
-        zero_again = placed("zero_again", [P, 1], F32, "logs", 1)
-        nc.vector.memset(zero_again[:], 0.0)
+        zeros = [placed(f"zero{n}", [P, 1], F32, "logs", n) for n in range(2)]
+        for tile in zeros:
+            nc.vector.memset(tile[:], 0.0)
         picked_scales = keep.tile([P, S // 4], I32, name="picked_scales", align_bytes=256)
         nc.vector.tensor_copy(picked_scales[:].bitcast(U8), scale_window[:].bitcast(U8).indirect(offsets[:]))
         for quad in range(4):
@@ -291,12 +290,22 @@ def tile_list_radar_log_power_kernel(tc, tab_words, tab_scales, offs, wi, wq_wor
 
         squares = {}
 
-        def in_phase(g, start, width, slot, bias=0.0):
+        products = {}
+
+        def square_in_phase(g, start, width, slot, bias=0.0):
             squares[g, start] = placed(f"squares{g}_{start}", [P, PACK * width], F32, "squares", slot)
-            per_bank = BANK // width
-            for f in range(width // P):
-                bank = next_bank()
+            for f, bank in enumerate(products[g, start]):
                 squared = squares[g, start][:, f * BANK : (f + 1) * BANK]
+                nc.scalar.activation(squared, bank[:], ACT.Square, bias=bias if f == 0 else 0.0)
+
+        def in_phase(g, start, width, slot, bias=0.0):
+            multiply(g, start, width)
+            square_in_phase(g, start, width, slot, bias)
+
+        def multiply(g, start, width):
+            per_bank = BANK // width
+            products[g, start] = [next_bank() for f in range(width // P)]
+            for f, bank in enumerate(products[g, start]):
                 if upright(g, start):
                     for n in range(per_bank):
                         t = per_bank * f + n
@@ -307,7 +316,6 @@ def tile_list_radar_log_power_kernel(tc, tab_words, tab_scales, offs, wi, wq_wor
                 else:
                     for a in FALLING:
                         cells_pass(bank, a, wi_codes[g, a][:].bitcast(FP8X4), wi_scales[g, a][:], start + f * P, FALLING)
-                nc.scalar.activation(squared, bank[:], ACT.Square, bias=bias if f == 0 else 0.0)
 
         sums = {}
         logs = {}
@@ -468,57 +476,56 @@ def tile_list_radar_log_power_kernel(tc, tab_words, tab_scales, offs, wi, wq_wor
         fillers.pop(0)()
         quantize_wi(LATE, 0)
         round_wi(LATE, 1)
+        add_squares(EARLY, 0, nc.vector, over_weights, last_at)
         quantize_wi(LATE, 1)
         in_phase(EARLY, W, W, 1)
         in_phase(EARLY, 2 * W, W, 2)
-        add_squares(EARLY, 0, nc.vector, placed, "grouped", 3, -2048)
         in_phase(EARLY, 3 * W, W, 3)
-        add_squares(EARLY, W, nc.vector, placed, "grouped", 3, 2048)
+        add_squares(EARLY, W, nc.vector, over_weights, last_at + 4096)
         round_w2(0)
         in_phase(LATE, 0, W, 4)
         log_power(EARLY, 0, W)
         round_w2(1)
-        log_power(EARLY, W, W)
         in_phase(LATE, W, W, 5)
         quantize_w2(0)
         quantize_w2(1)
         add_squares(EARLY, 2 * W, nc.gpsimd, placed, "squares", 1)
         place_gains()
         log_power(LATE, 0, W)
-        apply_gain(EARLY, 0, W, raw_at + 8192)
-        apply_gain(EARLY, W, W, raw_at + 3072)
+        log_power(EARLY, W, W)
+        apply_gain(EARLY, 0, W, raw_at + 3072)
         apply_gain(LATE, 0, W)
-        in_phase(LATE, 2 * W, W, 0)
+        in_phase(LATE, 2 * W, W, 0, zeros[0][:])
         quantize_h(EARLY, 0, W, ("late", 0))
-        quantize_h(EARLY, W, W, ("late", 0, 1024))
         quantize_h(LATE, 0, W)
         add_squares(EARLY, 3 * W, nc.gpsimd, over_weights, raw_at)
-        log_power(LATE, W, W, bias=ones[0][:])
         log_power(EARLY, 2 * W, W, placed, "logs", 0)
-        log_power(LATE, 2 * W, W)
-        in_phase(LATE, 3 * W, W, 4, zero_again[:])
-        apply_gain(LATE, W, W, raw_at + 4096)
+        log_power(LATE, W, W)
+        apply_gain(EARLY, W, W, raw_at + 4096)
         apply_gain(EARLY, 2 * W, W)
-        apply_gain(LATE, 2 * W, W)
-        features(0, W)
-        quantize_h(LATE, W, W, ("late", 2))
-        quantize_h(EARLY, 2 * W, W, ("late", 2, 1024))
-        quantize_h(LATE, 2 * W, W)
-        store_bank(0, W, 0, by_scalar)
+        in_phase(LATE, 3 * W, W, 4, zeros[1][:])
+        apply_gain(LATE, W, W)
+        quantize_h(EARLY, W, W, ("logs", 0))
+        quantize_h(EARLY, 2 * W, W)
+        quantize_h(LATE, W, W)
         log_power(EARLY, 3 * W, W, placed, "logs", 1)
-        store_bank(0, W, 1, by_scalar)
+        log_power(LATE, 2 * W, W)
+        features(0, W)
+        store(0, W, (by_scalar, by_scalar))
+        apply_gain(EARLY, 3 * W, W)
+        apply_gain(LATE, 2 * W, W)
         log_power(LATE, 3 * W, W)
-        apply_gain(EARLY, 3 * W, W, raw_at + 4096)
+        quantize_h(LATE, 2 * W, W)
+        quantize_h(EARLY, 3 * W, W)
         features(W, W)
         store(W, W, (by_scalar, by_scalar))
         apply_gain(LATE, 3 * W, P)
         features(2 * W, W)
         store(2 * W, W, (by_scalar, by_scalar))
-        quantize_h(EARLY, 3 * W, W)
         apply_gain(LATE, 3 * W + P, P)
         quantize_h(LATE, 3 * W, P)
         quantize_h(LATE, 3 * W + P, P)
         features(3 * W, P)
-        store(3 * W, P, (by_vector,))
+        store(3 * W, P, (by_scalar,))
         features(3 * W + P, P)
-        store(3 * W + P, P, (by_scalar, by_scalar, by_vector))
+        store(3 * W + P, P, (by_scalar, by_vector, by_scalar))

@@ -45,6 +45,7 @@ def tile_list_radar_log_power_kernel(tc, tab_words, tab_scales, offs, wi, wq_wor
 
         made = {"bank": 0}
         turn = list(range(BANKS))
+        aside = []
         room = {"grouped": 4096, "spare": 2048, "late": 4096, "logs": 4096, "squares": 4096, "h": 2048, "result": 3072, "piece": 512, "twin": 2048}
         depth = {"grouped": RING, "spare": 1, "late": S // WIDE, "logs": 2, "squares": RING + GROUPS, "h": RING, "result": RING + 1, "piece": N_TILES, "twin": 2}
         starts = {}
@@ -56,8 +57,7 @@ def tile_list_radar_log_power_kernel(tc, tab_words, tab_scales, offs, wi, wq_wor
             n = made["bank"]
             made["bank"] = n + 1
             place = turn.pop(max(0, len(turn) - back))
-            if not for_good:
-                turn.append(place)
+            (aside if for_good else turn).append(place)
             return psum.tile([P, BANK], F32, name=f"bank{n}", offset=4 * BANK * place)
 
         def placed(name, shape, dtype, kind, slot, shift=0):
@@ -213,15 +213,15 @@ def tile_list_radar_log_power_kernel(tc, tab_words, tab_scales, offs, wi, wq_wor
                 stop=(a == order[-1]),
             )
 
-        def square(squared, bank, pattern, sizes, on_vector=False, bias=0.0):
+        def square(squared, bank, pattern, sizes, on_vector=False, bias=0.0, beside_gpsimd=False):
             values = bank[:].rearrange(pattern, **sizes)
             if not on_vector:
                 nc.scalar.activation(squared, values, ACT.Square, bias=bias)
                 return
-            twin = stream("twin", [P, BANK], F32)
+            twin = over_weights("late_twin", [P, BANK], F32, raw_at + 8192) if beside_gpsimd else stream("twin", [P, BANK], F32)
             fillers.append(lambda: nc.vector.tensor_copy(twin[:], bank[:]))
             copied = twin[:].rearrange(pattern, **sizes)
-            fillers.append(lambda: nc.vector.tensor_tensor(squared, copied, copied, ALU.mult))
+            fillers.append(lambda: nc.vector.tensor_tensor(squared, values if beside_gpsimd else copied, copied, ALU.mult))
 
         fillers = []
         quadrature = {}
@@ -292,19 +292,19 @@ def tile_list_radar_log_power_kernel(tc, tab_words, tab_scales, offs, wi, wq_wor
 
         products = {}
 
-        def square_in_phase(g, start, width, slot, bias=0.0):
+        def square_in_phase(g, start, width, slot, bias=0.0, on_vector=None):
             squares[g, start] = placed(f"squares{g}_{start}", [P, PACK * width], F32, "squares", slot)
             for f, bank in enumerate(products[g, start]):
                 squared = squares[g, start][:, f * BANK : (f + 1) * BANK]
-                nc.scalar.activation(squared, bank[:], ACT.Square, bias=bias if f == 0 else 0.0)
+                square(squared, bank, "p c -> p c", {}, f == on_vector, bias if f == 0 else 0.0, True)
 
-        def in_phase(g, start, width, slot, bias=0.0):
-            multiply(g, start, width)
-            square_in_phase(g, start, width, slot, bias)
+        def in_phase(g, start, width, slot, bias=0.0, on_vector=None):
+            multiply(g, start, width, on_vector)
+            square_in_phase(g, start, width, slot, bias, on_vector)
 
-        def multiply(g, start, width):
+        def multiply(g, start, width, on_vector=None):
             per_bank = BANK // width
-            products[g, start] = [next_bank() for f in range(width // P)]
+            products[g, start] = [next_bank(f == on_vector) for f in range(width // P)]
             for f, bank in enumerate(products[g, start]):
                 if upright(g, start):
                     for n in range(per_bank):
@@ -480,7 +480,7 @@ def tile_list_radar_log_power_kernel(tc, tab_words, tab_scales, offs, wi, wq_wor
         quantize_wi(LATE, 1)
         in_phase(EARLY, W, W, 1)
         in_phase(EARLY, 2 * W, W, 2)
-        in_phase(EARLY, 3 * W, W, 3)
+        in_phase(EARLY, 3 * W, W, 3, on_vector=1)
         add_squares(EARLY, W, nc.vector, over_weights, last_at + 4096)
         round_w2(0)
         in_phase(LATE, 0, W, 4)
@@ -493,7 +493,10 @@ def tile_list_radar_log_power_kernel(tc, tab_words, tab_scales, offs, wi, wq_wor
         place_gains()
         log_power(LATE, 0, W)
         log_power(EARLY, W, W)
+        fillers.pop(0)()
         apply_gain(EARLY, 0, W, raw_at + 3072)
+        fillers.pop(0)()
+        turn.append(aside.pop(0))
         apply_gain(LATE, 0, W)
         in_phase(LATE, 2 * W, W, 0, zeros[0][:])
         quantize_h(EARLY, 0, W, ("late", 0))
@@ -521,11 +524,12 @@ def tile_list_radar_log_power_kernel(tc, tab_words, tab_scales, offs, wi, wq_wor
         store(W, W, (by_scalar, by_scalar))
         apply_gain(LATE, 3 * W, P)
         features(2 * W, W)
-        store(2 * W, W, (by_scalar, by_scalar))
+        store_bank(2 * W, W, 0, by_scalar)
+        store_bank(2 * W, W, 1, by_scalar)
         apply_gain(LATE, 3 * W + P, P)
         quantize_h(LATE, 3 * W, P)
         quantize_h(LATE, 3 * W + P, P)
         features(3 * W, P)
-        store(3 * W, P, (by_scalar,))
+        store(3 * W, P, (by_vector,))
         features(3 * W + P, P)
-        store(3 * W + P, P, (by_scalar, by_vector, by_scalar))
+        store(3 * W + P, P, (by_scalar, by_scalar, by_vector))

@@ -124,7 +124,6 @@ def tile_list_radar_log_power_kernel(tc, tab_words, tab_scales, offs, wi, wq_wor
         nc.sync.dma_start(table1[:], tab_words[1].rearrange("p t i -> p (t i)").bitcast(I32))
         v_scales = v_planes[:].bitcast(U8)
         nc.sync.dma_start(wq_late[1][:], wq_rows[:, 1, :row])
-        nc.sync.dma_start(wq_early[:], wq_rows[:, :, row:])
 
         raw = staging.tile([P, raw_columns], F32, name="raw", offset=raw_at, align_bytes=256)
         last_at = table0_at + 4 * row * (1 + PASSES)
@@ -137,6 +136,8 @@ def tile_list_radar_log_power_kernel(tc, tab_words, tab_scales, offs, wi, wq_wor
                 wi_raw[g, a] = values.rearrange("p (j c) -> p j c", j=PACK)
                 rows = wi[a * K_PASS : (a + 1) * K_PASS, g * K_PASS : (g + 1) * K_PASS]
                 nc.sync.dma_start(wi_raw[g, a], rows.rearrange("(p j) c -> p j c", j=PACK))
+                if n == 0 and a == 0:
+                    nc.sync.dma_start(wq_early[:], wq_rows[:, :, row:])
         gain_lines = staging.tile([P, P], F32, name="gain_lines", offset=last_at + 4 * piece, align_bytes=256)
         nc.vector.memset(gain_lines[:], 0.0)
         for g in range(GROUPS):
@@ -499,7 +500,7 @@ def tile_list_radar_log_power_kernel(tc, tab_words, tab_scales, offs, wi, wq_wor
         turn.append(aside.pop(0))
         apply_gain(LATE, 0, W)
         in_phase(LATE, 2 * W, W, 0, zeros[0][:])
-        quantize_h(EARLY, 0, W, ("late", 0))
+        quantize_h(EARLY, 0, W, raw_at + 8192)
         quantize_h(LATE, 0, W)
         add_squares(EARLY, 3 * W, nc.gpsimd, over_weights, raw_at)
         log_power(EARLY, 2 * W, W, placed, "logs", 0)

from contextlib import ExitStack

import concourse.mybir as mybir
from concourse.masks import make_identity

K, T, S, H, N = 1024, 4096, 1024, 1024, 384
FLOPS = 2 * (2 * K * H * S + H * N * S)

F32 = mybir.dt.float32
BF16 = mybir.dt.bfloat16
I32 = mybir.dt.int32
U32 = mybir.dt.uint32
U16 = mybir.dt.uint16
U8 = mybir.dt.uint8
FP8X4 = mybir.dt.float8_e4m3fn_x4
FP4X4 = mybir.dt.float4_e2m1fn_x4
ACT = mybir.ActivationFunctionType
ALU = mybir.AluOpType

P = 128
PACK = 4
K_PASS = P * PACK
PASSES = K // K_PASS
GROUPS = H // K_PASS
BANK = 512
BANKS = 8
HALVES = S // BANK
N_TILES = N // P
RUN = 4
WIDE = 256
LATE, EARLY = 0, 1
RISING, FALLING = (0, 1), (1, 0)
VECTOR_BANK = 3
RING = 4
LAST_GATHER = 256


def tile_list_radar_log_power_kernel(tc, tab_words, tab_scales, offs, wi, wq_words, wq_scales, gain, w2, out):
    nc = tc.nc
    with ExitStack() as ctx:
        keep = ctx.enter_context(tc.tile_pool(name="keep", bufs=1))
        staging = ctx.enter_context(tc.tile_pool(name="staging", bufs=1))
        ring = ctx.enter_context(tc.tile_pool(name="ring", bufs=1))
        psum = ctx.enter_context(tc.psum_pool(name="psum", bufs=1))

        made = {"bank": 0}
        turn = list(range(BANKS))
        aside = []
        room = {"grouped": 4096, "spare": 2048, "late": 4096, "logs": 4096, "squares": 4096, "h": 2048, "result": 3072, "piece": 512, "twin": 2048}
        depth = {"grouped": RING, "spare": 1, "late": S // WIDE, "logs": 2, "squares": RING + GROUPS, "h": RING, "result": RING + 1, "piece": N_TILES, "twin": 2}
        starts = {}
        for kind in room:
            starts[kind] = sum(room[other] * depth[other] for other in starts)
            made[kind] = 0

        def next_bank(for_good=False, back=BANKS):
            n = made["bank"]
            made["bank"] = n + 1
            place = turn.pop(max(0, len(turn) - back))
            (aside if for_good else turn).append(place)
            return psum.tile([P, BANK], F32, name=f"bank{n}", offset=4 * BANK * place)

        def placed(name, shape, dtype, kind, slot, shift=0):
            return ring.tile(shape, dtype, name=name, offset=starts[kind] + room[kind] * slot + shift, align_bytes=256)

        def over_weights(name, shape, dtype, shift):
            return staging.tile(shape, dtype, name=name, offset=shift, align_bytes=256)

        def stream(kind, shape, dtype):
            n = made[kind]
            made[kind] = n + 1
            return placed(f"{kind}{n}", shape, dtype, kind, n % depth[kind])

        offsets = keep.tile([P, S // 16], U16, name="offsets")
        nc.sync.dma_start(offsets[:], offs)

        piece = PACK * K_PASS
        w2_at = (GROUPS * PASSES - 1) * piece
        raw_columns = w2_at + GROUPS * PACK * N
        table0_at = 0
        raw_at = table0_at + 4 * T - 256
        table1_at = raw_at + 4 * raw_columns
        table1_end = table1_at + 4 * T

        row = K_PASS // 2
        wq_rows = wq_words.rearrange("a p c -> p a c").bitcast(I32)
        wq_late = [
            keep.tile([P, row], I32, name="wq_late0", align_bytes=256),
            staging.tile([P, row], I32, name="wq_late1", offset=table0_at, align_bytes=256),
        ]
        wq_early = staging.tile([P, PASSES, row], I32, name="wq_early", offset=table0_at + 4 * row, align_bytes=256)

        scale_window = staging.tile([P, T // 4], I32, name="scale_window", offset=table1_end - 256, align_bytes=256)
        nc.sync.dma_start(scale_window[96:P, :], tab_scales.rearrange("a q t -> q a t").bitcast(I32))
        nc.sync.dma_start(wq_late[0][:], wq_rows[:, 0, :row])
        wq_scale_rows = keep.tile([P, PASSES, H // 4], I32, name="wq_scale_rows", align_bytes=256)
        nc.gpsimd.memset(wq_scale_rows[:], 0)
        for quad in range(4):
            nc.sync.dma_start(
                wq_scale_rows[32 * quad : 32 * quad + 4, :, :],
                wq_scales[:, 4 * quad : 4 * quad + 4, :].rearrange("a r c -> r a c").bitcast(I32),
            )
        one = keep.tile([P, 1], F32, name="one")
        nc.vector.memset(one[:], 1.0)
        nc.vector.memset(scale_window[0:96, :], 0)
        table0 = staging.tile([P, T], I32, name="table0", offset=table0_at, align_bytes=256)
        nc.sync.dma_start(table0[:], tab_words[0].rearrange("p t i -> p (t i)").bitcast(I32))

        identity = keep.tile([P, P], F32, name="identity")
        make_identity(nc, identity[:])
        zero = keep.tile([P, 1], F32, name="zero")
        nc.scalar.activation(zero[:], one[:], ACT.Ln)
        v_planes = keep.tile([P, PASSES * S // 4], I32, name="v_planes", align_bytes=256)
        nc.vector.memset(v_planes[:], 0)

        zeros = [placed(f"zero{n}", [P, 1], F32, "logs", n) for n in range(2)]
        for tile in zeros:
            nc.vector.memset(tile[:], 0.0)
        picked_scales = keep.tile([P, S // 4], I32, name="picked_scales", align_bytes=256)
        nc.vector.tensor_copy(picked_scales[:].bitcast(U8), scale_window[:].bitcast(U8).indirect(offsets[:]))
        for quad in range(4):
            nc.sync.dma_start(v_planes[32 * quad : 32 * quad + 4, :], picked_scales[96 + 8 * quad : 104 + 8 * quad, :])
        table1 = staging.tile([P, T], I32, name="table1", offset=table1_at, align_bytes=256)
        nc.sync.dma_start(table1[:], tab_words[1].rearrange("p t i -> p (t i)").bitcast(I32))
        v_scales = v_planes[:].bitcast(U8)
        nc.sync.dma_start(wq_late[1][:], wq_rows[:, 1, :row])

        raw = staging.tile([P, raw_columns], F32, name="raw", offset=raw_at, align_bytes=256)
        last_at = table0_at + 4 * row * (1 + PASSES)
        last_piece = staging.tile([P, piece], F32, name="last_piece", offset=last_at, align_bytes=256)
        wi_raw = {}
        for n, g in enumerate((EARLY, LATE)):
            for a in range(PASSES):
                at = (n * PASSES + a) * piece
                values = raw[:, at : at + piece] if at < w2_at else last_piece[:]
                wi_raw[g, a] = values.rearrange("p (j c) -> p j c", j=PACK)
                rows = wi[a * K_PASS : (a + 1) * K_PASS, g * K_PASS : (g + 1) * K_PASS]
                nc.sync.dma_start(wi_raw[g, a], rows.rearrange("(p j) c -> p j c", j=PACK))
                if n == 0 and a == 0:
                    nc.sync.dma_start(wq_early[:], wq_rows[:, :, row:])
        gain_lines = staging.tile([P, P], F32, name="gain_lines", offset=last_at + 4 * piece, align_bytes=256)
        nc.vector.memset(gain_lines[:], 0.0)
        for g in range(GROUPS):
            nc.sync.dma_start(
                gain_lines[PACK * g : PACK * (g + 1), :].rearrange("t (s i) -> t s i", i=RUN),
                gain[g * K_PASS : (g + 1) * K_PASS].rearrange("(s t i) -> t s i", t=PACK, i=RUN),
            )
        w2_raw = [raw[:, w2_at + g * PACK * N : w2_at + (g + 1) * PACK * N] for g in range(GROUPS)]
        for g in range(GROUPS):
            rows = w2[g * K_PASS : (g + 1) * K_PASS, :].rearrange("(s t i) n -> t s i n", t=PACK, i=RUN)
            for t in range(PACK):
                nc.sync.dma_start(w2_raw[g][:, t * N : (t + 1) * N], rows[t])

        v_codes = [keep.tile([P, S], U32, name=f"v_codes{a}", align_bytes=256) for a in range(PASSES)]

        def gather_words(a, table, runs):
            for first, count in runs:
                nc.vector.tensor_copy(
                    v_codes[a][:, first : first + count],
                    table[:].bitcast(U32).indirect(offsets[:, first // 16 : (first + count) // 16]),
                )

        wq_planes = keep.tile([P, PASSES, GROUPS, K_PASS // 4], I32, name="wq_planes", align_bytes=256)
        nc.vector.tensor_copy(
            wq_planes[:].rearrange("p a g (t s) -> p (a g) t s", t=PACK),
            wq_scale_rows[:].rearrange("p a (g s t) -> p (a g) t s", g=GROUPS, t=PACK),
        )
        wq_sorted = {}

        def sort_words(g, a, words):
            wq_sorted[g, a] = keep.tile([P, row], I32, name=f"wq_sorted{g}_{a}", align_bytes=256)
            nc.vector.tensor_copy(
                wq_sorted[g, a][:].rearrange("p (t s w) -> p t s w", t=PACK, w=2),
                words.rearrange("p (s t w) -> p t s w", t=PACK, w=2),
            )

        gather_words(0, table0, ((0, BANK), (BANK, BANK)))
        gather_words(1, table1, [(first, LAST_GATHER) for first in range(0, S, LAST_GATHER)])
        for a in range(PASSES):
            sort_words(EARLY, a, wq_early[:, a, :])

        early_power = [keep.tile([P, PACK * BANK], F32, name=f"early_power{half}") for half in range(HALVES)]
        late_power = [placed(f"late_power{u}", [P, PACK * WIDE], F32, "late", u) for u in range(S // WIDE)]

        def power_of(g, start, width):
            tile, cells = (early_power[start // BANK], BANK) if g == EARLY else (late_power[start // WIDE], WIDE)
            at = PACK * (start % cells)
            return tile[:, at : at + PACK * width]

        def planes_of(tiles, g, start, width):
            first = start % WIDE
            unit = tiles[g, start - first][:].rearrange("p (t j) -> p t j", t=PACK)
            return unit[:, :, first : first + width]

        def plane_pass(out_view, a, codes, scales, start, width, flags):
            nc.tensor.matmul_mx(
                out=out_view,
                lhsT=codes,
                lhsT_scale=scales,
                rhs=v_codes[a][:, start : start + width].bitcast(FP8X4),
                rhs_scale=v_scales[:, a * S + start : a * S + start + width],
                start=flags[0],
                stop=flags[1],
            )

        def cells_pass(bank, a, codes, scales, start, order):
            nc.tensor.matmul_mx(
                out=bank[:],
                lhsT=v_codes[a][:, start : start + P].bitcast(FP8X4),
                lhsT_scale=v_scales[:, a * S + start : a * S + start + P],
                rhs=codes,
                rhs_scale=scales,
                start=(a == order[0]),
                stop=(a == order[-1]),
            )

        def square(squared, bank, pattern, sizes, on_vector=False, bias=0.0, beside_gpsimd=False):
            values = bank[:].rearrange(pattern, **sizes)
            if not on_vector:
                nc.scalar.activation(squared, values, ACT.Square, bias=bias)
                return
            twin = over_weights("late_twin", [P, BANK], F32, raw_at + 8192) if beside_gpsimd else stream("twin", [P, BANK], F32)
            fillers.append(lambda: nc.vector.tensor_copy(twin[:], bank[:]))
            copied = twin[:].rearrange(pattern, **sizes)
            fillers.append(lambda: nc.vector.tensor_tensor(squared, values if beside_gpsimd else copied, copied, ALU.mult))

        fillers = []
        quadrature = {}

        def upright(g, start):
            return g == EARLY

        def square_turned(g, n, bank, on_vector, bias=0.0):
            if on_vector:
                quadrature[n] = placed("vector_squares", [P, BANK], F32, "grouped", 1)[:]
            else:
                quadrature[n] = power_of(g, n * P, P)
            squared = quadrature[n].rearrange("p (t s i) -> p t s i", t=PACK, i=RUN)
            square(squared, bank, "p (s t i) -> p t s i", {"t": PACK, "i": RUN}, on_vector, bias)

        def quadrature_pass(g, a, bank, start, width, f):
            per_bank = BANK // width
            for n in range(per_bank):
                t = per_bank * f + n
                codes = wq_sorted[g, a][:].bitcast(U8)[:, 2 * t * P : 2 * (t + 1) * P].bitcast(FP4X4)
                scales = wq_planes[:, a, g, :].bitcast(U8)[:, t * P : (t + 1) * P]
                flags = (a == 0 and n == 0, a == PASSES - 1 and n == per_bank - 1)
                plane_pass(bank[:, n * width : (n + 1) * width], a, codes, scales, start, width, flags)

        def square_upright(g, bank, start, width, f, on_vector=False):
            per_bank = BANK // width
            units = power_of(g, start, width).rearrange("p (u t j) -> p u t j", t=PACK, j=WIDE)
            squared = units[:, :, per_bank * f : per_bank * (f + 1), :]
            square(squared, bank, "p (u t j) -> p u t j", {"t": per_bank, "j": WIDE}, on_vector)

        def late_quadrature():
            banks = [next_bank() for n in range(S // P)]
            for a in range(PASSES):
                for n, bank in enumerate(banks):
                    codes = wq_late[a][:].bitcast(U8).bitcast(FP4X4)
                    cells_pass(bank, a, codes, wq_scale_rows[:, a, :P].bitcast(U8), n * P, RISING)
                    if a == PASSES - 1:
                        square_turned(LATE, n, bank, n == VECTOR_BANK, zero[:] if n == 0 else 0.0)

        def early_quadrature(start, f, on_vector=False):
            bank = next_bank()
            for a in range(PASSES):
                quadrature_pass(EARLY, a, bank, start, BANK, f)
            square_upright(EARLY, bank, start, BANK, f, on_vector)

        wi_codes = {}
        wi_scales = {}
        wi_grouped = {}

        def round_wi(g, a):
            wi_grouped[g, a] = stream("grouped", [P, piece], BF16)
            nc.vector.tensor_copy(
                wi_grouped[g, a][:].rearrange("p (t s i j) -> p t s j i", t=PACK, i=RUN, j=PACK),
                wi_raw[g, a].rearrange("p j (s t i) -> p t s j i", t=PACK, i=RUN),
            )

        def quantize_wi(g, a):
            wi_codes[g, a] = keep.tile([P, K_PASS], U32, name=f"wi_codes{g}_{a}", align_bytes=256)
            wi_scales[g, a] = keep.tile([P, K_PASS], U8, name=f"wi_scales{g}_{a}", align_bytes=256)
            nc.vector.quantize_mx(out=wi_codes[g, a][:].bitcast(FP8X4), scales=wi_scales[g, a][:], in_=wi_grouped[g, a][:])

        def prepare_wi(g):
            for a in range(PASSES):
                round_wi(g, a)
                quantize_wi(g, a)

        squares = {}

        products = {}

        def square_in_phase(g, start, width, slot, bias=0.0, on_vector=None):
            squares[g, start] = placed(f"squares{g}_{start}", [P, PACK * width], F32, "squares", slot)
            for f, bank in enumerate(products[g, start]):
                squared = squares[g, start][:, f * BANK : (f + 1) * BANK]
                square(squared, bank, "p c -> p c", {}, f == on_vector, bias if f == 0 else 0.0, True)

        def in_phase(g, start, width, slot, bias=0.0, on_vector=None):
            multiply(g, start, width, on_vector)
            square_in_phase(g, start, width, slot, bias, on_vector)

        def multiply(g, start, width, on_vector=None):
            per_bank = BANK // width
            products[g, start] = [next_bank(f == on_vector) for f in range(width // P)]
            for f, bank in enumerate(products[g, start]):
                if upright(g, start):
                    for n in range(per_bank):
                        t = per_bank * f + n
                        for a in FALLING:
                            codes = wi_codes[g, a][:, t * P : (t + 1) * P].bitcast(FP8X4)
                            scales = wi_scales[g, a][:, t * P : (t + 1) * P]
                            plane_pass(bank[:, n * width : (n + 1) * width], a, codes, scales, start, width, (a == FALLING[0], a == FALLING[-1]))
                else:
                    for a in FALLING:
                        cells_pass(bank, a, wi_codes[g, a][:].bitcast(FP8X4), wi_scales[g, a][:], start + f * P, FALLING)

        sums = {}
        logs = {}

        def add_squares(g, start, adder, where, *place):
            sums[g, start] = where(f"sum{g}_{start}", [P, PACK * WIDE], F32, *place)
            adder.tensor_tensor(sums[g, start][:], squares[g, start][:], power_of(g, start, WIDE), ALU.add)

        def log_power(g, start, width, where=None, *place, bias=1.0):
            if upright(g, start):
                unit = (g, start - start % WIDE)
                if where:
                    logs[unit] = where(f"log{g}_{start}", [P, PACK * WIDE], F32, *place)
                logs.setdefault(unit, sums[unit])
                nc.scalar.activation(planes_of(logs, g, start, width), planes_of(sums, g, start, width), ACT.Ln, bias=1.0)
                return
            total = power_of(g, start, width)
            banks = [next_bank() for f in range(width // P)]
            for f, bank in enumerate(banks):
                for t in range(PACK):
                    cols = slice(t * P, (t + 1) * P)
                    terms = (squares[g, start][:, f * BANK : (f + 1) * BANK], quadrature[start // P + f])
                    for n, term in enumerate(terms):
                        nc.tensor.matmul(
                            bank[:, t * P : (t + 1) * P],
                            term[:, cols],
                            identity[:],
                            start=(n == 0),
                            stop=(n == 1),
                            is_transpose=True,
                        )
            for f, bank in enumerate(banks):
                nc.scalar.activation(
                    total[:, f * BANK : (f + 1) * BANK].rearrange("p (j t) -> p j t", t=PACK),
                    bank[:].rearrange("p (t j) -> p j t", t=PACK),
                    ACT.Ln,
                    bias=bias if f == 0 else 1.0,
                )

        h_codes = {}
        h_scales = [keep.tile([P, S], U8, name=f"h_scales{g}", align_bytes=256) for g in range(GROUPS)]
        h_rounded = {}

        held = {}

        def place_gains():
            held["gains"] = next_bank(for_good=True)
            nc.tensor.transpose(held["gains"][:, :P], gain_lines[:], identity[:])

        def apply_gain(g, start, width, place=None):
            shape = [P, PACK * width]
            h = over_weights(f"h{g}_{start}", shape, BF16, place) if place is not None else stream("h", shape, BF16)
            factor = held["gains"][:, g * PACK : (g + 1) * PACK]
            if upright(g, start):
                nc.vector.tensor_tensor(
                    h[:].rearrange("p (c i t) -> p c t i", i=RUN, t=PACK),
                    planes_of(logs, g, start, width).rearrange("p t (c i) -> p c t i", i=RUN),
                    factor.unsqueeze(1).unsqueeze(3).to_broadcast([P, width // RUN, PACK, RUN]),
                    ALU.mult,
                )
            else:
                nc.vector.tensor_tensor(
                    h[:].rearrange("p (j t) -> p j t", t=PACK),
                    power_of(g, start, width).rearrange("p (j t) -> p j t", t=PACK),
                    factor.unsqueeze(1).to_broadcast([P, width, PACK]),
                    ALU.mult,
                )
            h_rounded[g, start] = h

        def quantize_h(g, start, width, place=None):
            name = f"h_codes{g}_{start}"
            if place is None:
                codes = keep.tile([P, width], U32, name=name, align_bytes=256)
            elif isinstance(place, int):
                codes = over_weights(name, [P, width], U32, place)
            else:
                codes = placed(name, [P, width], U32, *place)
            for first in range(0, width, P):
                h_codes[g, start + first] = codes[:, first:]
            nc.vector.quantize_mx(
                out=codes[:].bitcast(FP8X4),
                scales=h_scales[g][:, start : start + width],
                in_=h_rounded[g, start][:],
            )

        w2_grouped = {}
        w2_codes = keep.tile([P, GROUPS * N], U32, name="w2_codes", align_bytes=256)
        w2_scales = keep.tile([P, GROUPS * N], U8, name="w2_scales", align_bytes=256)

        def round_w2(g):
            w2_grouped[g] = placed(f"w2_grouped{g}", [P, PACK * N], BF16, "squares", g)
            nc.vector.tensor_copy(
                w2_grouped[g][:].rearrange("p (c i j) -> p c j i", i=RUN, j=PACK),
                w2_raw[g].rearrange("p (j c i) -> p c j i", j=PACK, i=RUN),
            )

        def quantize_w2(g):
            nc.vector.quantize_mx(
                out=w2_codes[:, g * N : (g + 1) * N].bitcast(FP8X4),
                scales=w2_scales[:, g * N : (g + 1) * N],
                in_=w2_grouped[g][:],
            )

        out_rows = out.rearrange("(c p) j -> p c j", p=P)

        summed = {}

        def features(start, width, earlier=EARLY, back=BANKS):
            per_bank = 1 if start + width == S else BANK // width
            banks = [(first, min(first + per_bank, N_TILES), next_bank(back=back)) for first in range(0, N_TILES, per_bank)]
            for n, g in enumerate((earlier, 1 - earlier)):
                for first, last, bank in banks:
                    for c in range(first, last):
                        col = g * N + c * P
                        nc.tensor.matmul_mx(
                            out=bank[:, (c - first) * width : (c - first + 1) * width],
                            lhsT=w2_codes[:, col : col + P].bitcast(FP8X4),
                            lhsT_scale=w2_scales[:, col : col + P],
                            rhs=h_codes[g, start][:, :width].bitcast(FP8X4),
                            rhs_scale=h_scales[g][:, start : start + width],
                            start=(n == 0 and c == first),
                            stop=(n == GROUPS - 1 and c == last - 1),
                        )
            summed[start] = banks

        def store_bank(start, width, n, copy):
            first, last, bank = summed[start][n]
            result = stream("result", [P, last - first, width], F32)
            copy(result[:].rearrange("p c j -> p (c j)"), bank[:, : (last - first) * width])
            nc.sync.dma_start(out_rows[:, first:last, start : start + width], result[:])

        def store(start, width, copies):
            banks = summed[start]
            rows = out_rows[:, :, start : start + width]
            if start + width == S:
                for (first, last, bank), copy in zip(banks, copies):
                    result = stream("piece", [P, width], F32)
                    copy(result[:], bank[:, :width])
                    nc.sync.dma_start(rows[:, first, :], result[:])
                return
            result = stream("result", [P, N_TILES, width], F32)
            for (first, last, bank), copy in zip(banks, copies):
                copy(result[:, first:last, :].rearrange("p c j -> p (c j)"), bank[:, : (last - first) * width])
            nc.sync.dma_start(rows, result[:])

        by_scalar, by_vector = nc.scalar.copy, nc.vector.tensor_copy

        W = WIDE
        late_quadrature()
        fillers.pop(0)()
        for f in range(4):
            early_quadrature(0, f)
        prepare_wi(EARLY)
        for f in range(4):
            early_quadrature(BANK, f)
        in_phase(EARLY, 0, W, 0)
        round_wi(LATE, 0)
        fillers.pop(0)()
        quantize_wi(LATE, 0)
        round_wi(LATE, 1)
        add_squares(EARLY, 0, nc.vector, over_weights, last_at)
        quantize_wi(LATE, 1)
        in_phase(EARLY, W, W, 1)
        in_phase(EARLY, 2 * W, W, 2)
        in_phase(EARLY, 3 * W, W, 3, on_vector=1)
        add_squares(EARLY, W, nc.vector, over_weights, last_at + 4096)
        round_w2(0)
        in_phase(LATE, 0, W, 4)
        log_power(EARLY, 0, W)
        round_w2(1)
        in_phase(LATE, W, W, 5)
        quantize_w2(0)
        quantize_w2(1)
        add_squares(EARLY, 2 * W, nc.gpsimd, placed, "squares", 1)
        place_gains()
        log_power(LATE, 0, W)
        log_power(EARLY, W, W)
        fillers.pop(0)()
        apply_gain(EARLY, 0, W, raw_at + 3072)
        fillers.pop(0)()
        turn.append(aside.pop(0))
        apply_gain(LATE, 0, W)
        in_phase(LATE, 2 * W, W, 0, zeros[0][:])
        quantize_h(EARLY, 0, W, raw_at + 8192)
        quantize_h(LATE, 0, W)
        add_squares(EARLY, 3 * W, nc.gpsimd, over_weights, raw_at)
        log_power(EARLY, 2 * W, W, placed, "logs", 0)
        log_power(LATE, W, W)
        apply_gain(EARLY, W, W, raw_at + 4096)
        apply_gain(EARLY, 2 * W, W)
        in_phase(LATE, 3 * W, W, 4, zeros[1][:])
        apply_gain(LATE, W, W)
        quantize_h(EARLY, W, W, ("logs", 0))
        quantize_h(EARLY, 2 * W, W)
        quantize_h(LATE, W, W)
        log_power(EARLY, 3 * W, W, placed, "logs", 1)
        log_power(LATE, 2 * W, W)
        features(0, W)
        store(0, W, (by_scalar, by_scalar))
        apply_gain(EARLY, 3 * W, W)
        apply_gain(LATE, 2 * W, W)
        log_power(LATE, 3 * W, W)
        quantize_h(LATE, 2 * W, W)
        quantize_h(EARLY, 3 * W, W)
        features(W, W)
        store(W, W, (by_scalar, by_scalar))
        apply_gain(LATE, 3 * W, P)
        features(2 * W, W)
        store_bank(2 * W, W, 0, by_scalar)
        store_bank(2 * W, W, 1, by_scalar)
        apply_gain(LATE, 3 * W + P, P)
        quantize_h(LATE, 3 * W, P)
        quantize_h(LATE, 3 * W + P, P)
        features(3 * W, P)
        store(3 * W, P, (by_vector,))
        features(3 * W + P, P)
        store(3 * W + P, P, (by_scalar, by_scalar, by_vector))
